import numpy as np, ml_dtypes
CORES = [9,25,41,57]
N = 4
BF = ml_dtypes.bfloat16
def gentries(a):
    return np.ascontiguousarray(a.reshape(8, 16, -1).transpose(0, 2, 1)).reshape(8, -1)
def gtable(e):
    e = np.asarray(e); return np.ascontiguousarray(e.reshape(8, -1, 16).transpose(0, 2, 1)).reshape(128, -1).astype(np.int32)
FR, PR, MS, M, NT, KR, H, S = 2, 2, 2048, 4096, 1024, 4, 512, 10
C = 64
SIZES = ((24, 0), (48, 0), (80, 0), (128, 8), (192, 16), (320, 24), (640, 24), (NT, 24))
def sign(rng, shape):
    return 2 * rng.integers(0, 2, shape) - 1
def far(rng, shape):
    return rng.integers(244, 257, shape)
def scene(rng, size, w):
    pm = np.argsort(rng.random((8, M)), axis=1); inv = np.argsort(pm, axis=1); cl = pm % C
    cen = np.rint(rng.integers(16, 241, (8, 16, C)) * size)
    z = np.take_along_axis(cen, cl[:, None, :], 2)[None] + np.rint((2 * rng.random((FR, 8, 16, M)) - 1) * w)
    n0 = rng.integers(0, M, (8, NT)); c0 = np.take_along_axis(cl, n0, 1)
    x0 = np.take_along_axis(cen, c0[:, None, :], 2) + np.rint((2 * rng.random((8, 16, NT)) - 1) * rng.choice(np.array([16.0, 32.0, 48.0]), (8, 1, NT)))
    j = ((M // C) * rng.random((FR, 8, 3, M)) ** 3).astype(np.int64)
    same = inv[np.arange(8)[None, :, None, None], cl[None, :, None, :] + C * j]
    nx = np.where(rng.random((FR, 8, 3, M)) < np.array([0.6, 0.3, 0.3])[:, None], same, rng.integers(0, M, (FR, 8, 3, M)))
    nx[:, :, 1] = np.where(rng.random((FR, 8, M)) < 0.03125, nx[:, :, 0], nx[:, :, 1])
    return {"z": z, "nx": nx, "x0": x0, "n0": n0}
def folk(rng, s):
    return rng.permutation(NT)[:s][(s * rng.random((N, KR, H)) ** 1.5).astype(np.int64)]
def life(rng, d):
    o = rng.permutation(8); d["hy"] = np.zeros((N, 8, KR, H), np.int64); d["u"] = np.zeros((N, 8, FR, KR, H), np.int64)
    for g in range(8):
        s, lo = SIZES[int(o[g])]; d["hy"][:, g] = folk(rng, s); d["u"][:, g] = rng.integers(lo, 64, (N, FR, KR, H))
    return d
def plain(rng):
    return life(rng, scene(rng, np.ones((8, 1, C)), rng.choice(np.array([16.0, 32.0, 48.0, 64.0, 80.0]), (FR, 8, 1, M))))
def deal(rng, s):
    f = rng.permutation(N * H).reshape(N, 1, H) * KR + np.arange(KR)[:, None]
    return rng.permutation(NT)[:s][f % s], f // s
def quad(rng, d, g, near):
    b = rng.permutation(M // 4)[:NT]; d["n0"][g] = 4 * b
    x = rng.integers(32, 129, (16, NT)); d["x0"][g] = x
    for m in range(3): d["nx"][:, g, m] = 4 * (np.arange(M) // 4) + m + 1
    zz = d["z"][:, g]; zz[:] = far(rng, zz.shape)
    safe = np.argsort(rng.random((16, NT)), axis=0) < (16 if near == 3 else rng.integers(5, 17, (1, NT)))
    for m in range(1, near + 1):
        zz[:, :, 4 * b + m] = x + np.where(safe, rng.integers(-16, 17, (FR, 16, NT)), rng.integers(-72, 73, (FR, 16, NT)))
def soft(rng, d):
    q = int(rng.integers(0, N)); e = 3 * KR; k = np.arange(KR)[:, None]
    for g in range(8):
        c = rng.permutation(M)[:e]
        near = np.argsort(rng.random((16, e)), axis=0) < 5; near[:, :KR] = True
        x = np.where(near, rng.integers(96, 161, (16, e)), rng.integers(224, 257, (16, e))).astype(np.float64)
        step = np.full((16, e), 32.0); step[:, :KR] = 4.0 * (1 + rng.permutation(16) % 7)[:, None]
        d["x0"][g][:, :e] = x; d["n0"][g][:e] = c; d["nx"][:, g][:, :, c] = c
        for t in range(FR):
            v = np.where(near, x + sign(rng, (16, e)) * step, np.where(x >= 132, 8.0, 256.0))
            d["z"][t, g][:, c] = v; x = x + 0.25 * (v - x)
        o = rng.permutation(H)[H // 32:]; few = o[:H // 128]
        d["hy"][q, g][:, o] = KR + 2 * k + rng.integers(0, 2, (KR, len(o))); d["hy"][q, g][:, few] = k
        d["u"][q, g][:, :, o] = 63
def pack(d):
    z = np.clip(d["z"], 8, 256) * 0.03125; x = (np.clip(d["x0"], 8, 256) * 0.03125).reshape(1, 128, NT)
    z = np.ascontiguousarray(z.reshape(FR, 8, 16, PR, MS).transpose(0, 3, 1, 2, 4)).reshape(N, 128, MS)
    s = np.ascontiguousarray(d["nx"].reshape(FR, 8, 3, PR, MS).transpose(0, 3, 1, 2, 4)).reshape(N, 24, MS)
    return {"z": z.astype(np.float32).astype(BF), "nx": s.astype(np.int32), "x0": np.ascontiguousarray(np.repeat(x, N, axis=0)).astype(np.float32),
            "n0": np.ascontiguousarray(np.repeat(d["n0"][None], N, axis=0)).astype(np.int32),
            "hyp": np.stack([gtable(a.reshape(8, -1)) for a in d["hy"]]), "uu": np.stack([gtable(a.reshape(8, -1)) for a in d["u"]])}
def setup_inputs(rng):
    return pack(plain(rng))
def setup_inputs_spread(rng):
    d = life(rng, scene(rng, rng.choice(np.array([0.5, 0.75, 1.0, 1.25]), (8, 1, C)), 40 * np.exp2(2 * rng.random((FR, 8, 1, M)) - 1)))
    v = (64 * rng.random(d["u"].shape) ** rng.choice(np.array([0.5, 1.0, 2.0]), (1, 8, 1, 1, 1))).astype(np.int64)
    d["u"] = np.where(rng.random(v.shape) < 0.25, v, d["u"])
    soft(rng, d)
    return pack(d)
def atends(rng, a, hi, share):
    return np.where(rng.random(a.shape) < share, hi * rng.integers(0, 2, a.shape), a)
def setup_inputs_ends(rng):
    d = plain(rng); v = sign(rng, (8, 16, 1)); p = np.array([0.0, 0.0, 0.1, 0.3])
    sz = v[None] * sign(rng, (FR, 8, 1, M)) * np.where(rng.random((FR, 8, 16, M)) < rng.choice(p, (FR, 8, 1, M)), -1, 1)
    sx = v * sign(rng, (8, 1, NT)) * np.where(rng.random((8, 16, NT)) < rng.choice(p, (8, 1, NT)), -1, 1)
    sz[..., 0] = -v[None, :, :, 0]; sz[..., M - 1] = v[None, :, :, 0]; sx[..., 0] = -v[..., 0]; sx[..., NT - 1] = v[..., 0]
    d["z"] = np.where(sz > 0, 256, 8); d["x0"] = np.where(sx > 0, 256, 8)
    d["n0"] = atends(rng, d["n0"], M - 1, 0.8); d["n0"][:, 0] = 0; d["n0"][:, NT - 1] = M - 1
    d["nx"] = atends(rng, d["nx"], M - 1, 0.8); d["nx"][:, :, 0, 0] = 0; d["nx"][:, :, 2, M - 1] = M - 1
    d["nx"][:, 2, :, M - 1] = M - 1; d["nx"][:, 7, :, M - 1] = M - 1
    for g in range(8):
        d["hy"][:, g] = np.where(rng.random((N, KR, H)) < 0.78, (NT - 1) * rng.integers(0, 2, (N, KR, H)), rng.permutation(NT)[:60][rng.integers(0, 60, (N, KR, H))])
    d["u"] = atends(rng, rng.integers(0, 64, d["u"].shape), 63, 0.7)
    d["u"][:, 3] = 0; d["u"][:, 0] = 0; d["u"][N - 1, 0, :, KR - 1, H - 1] = 63; d["hy"][N - 1, 0, KR - 1, H - 1] = NT - 1
    quad(rng, d, 6, 3); hy, oc = deal(rng, NT); d["hy"][:, 6] = hy; d["u"][:, 6, 0] = np.array([0, 16, 32, 63])[oc % 4]
    return pack(d)
def setup_inputs_corners(rng):
    d = plain(rng); r = int(rng.integers(0, 8)); gs = [(r + i) % 8 for i in range(8)]
    for i in (0, 2, 4, 6): d["u"][:, gs[i]] = rng.integers(0, 64, (N, FR, KR, H))
    for i, s, one in ((1, NT, 0), (3, NT, 1), (5, NT - 1, 1)):
        g = gs[i]; quad(rng, d, g, 1); d["hy"][:, g] = deal(rng, s)[0]; d["u"][:, g] = 0
        if one: d["u"][N - 1, g, 0, KR - 1, H - 1] = 63
    g = gs[4]; quad(rng, d, g, 3); hy, oc = deal(rng, NT); d["hy"][:, g] = hy; d["u"][:, g, 0] = np.array([0, 16, 32, 63])[oc % 4]
    g = gs[6]; quad(rng, d, g, 1); hy, oc = deal(rng, NT // 2); d["hy"][:, g] = hy; d["u"][:, g, 0] = 63 * (oc % 2)
    d["z"][:, gs[7]] = far(rng, (FR, 16, M)); d["x0"][gs[7]] = np.minimum(d["x0"][gs[7]], 208)
    return pack(d)
def setup_inputs_crowd(rng):
    d = plain(rng); r = int(rng.integers(0, 8)); gs = [(r + i) % 8 for i in range(8)]
    for i in range(6): quad(rng, d, gs[i], 3)
    for i in range(7): d["u"][:, gs[i]] = rng.integers(0, 64, (N, FR, KR, H))
    a = rng.permutation(NT)
    d["hy"][:, gs[0]] = a[0]; d["u"][:, gs[0]] = 0
    d["hy"][:, gs[1]] = a[1]; d["hy"][N - 1, gs[1], KR - 1, H - 1] = a[2]; d["u"][:, gs[1], 0] = 0
    d["hy"][:, gs[2]] = NT - 1; d["u"][:, gs[2], 0] = 63
    d["hy"][:, gs[3]] = 0
    d["hy"][:, gs[4]] = (NT - 1) * rng.integers(0, 2, (N, KR, H))
    d["u"][:, gs[5], 0] = 0
    for q in range(N):
        f = rng.permutation(KR * H); d["hy"][q, gs[5]] = np.where(f < 256, a[3], np.where(f < 511, a[4], a[5])).reshape(KR, H)
    d["hy"][:, gs[6]] = a[6:9][rng.integers(0, 3, (N, KR, H))]
    return pack(d)
def setup_inputs_calm(rng):
    d = plain(rng); par = int(rng.integers(0, 2)); off = int(rng.integers(0, 4))
    for i in range(4):
        g = (2 * i + 1 + par) % 8; h = (g + 7) % 8; quad(rng, d, g, 1); d["hy"][:, g] = deal(rng, 64)[0]
        for t in range(FR):
            c = ((i + t + off) % 4) * 2 ** S + int(rng.integers(0, 2)) * (2 ** S - 1)
            d["u"][:, g, t] = np.where(rng.permutation(N * KR * H) < c, 0, 63).reshape(N, KR, H)
        d["u"][:, h] = np.where(rng.random((N, FR, KR, H)) < 0.5, rng.choice(np.array([8, 16, 24, 32]), (N, FR, KR, H)), rng.integers(0, 64, (N, FR, KR, H)))
    return pack(d)
def check_ranges(d):
    bad = []
    for k, lo, hi in (("nx", 0, M - 1), ("n0", 0, M - 1), ("hyp", 0, NT - 1), ("uu", 0, 63)):
        if np.min(d[k]) < lo or np.max(d[k]) > hi: bad.append("range of " + k)
    for k in ("z", "x0"):
        v = np.asarray(d[k], np.float64) * 32
        if not np.all((v >= 8) & (v <= 256) & (v == np.rint(v))): bad.append("range of " + k)
    for k in ("x0", "n0"):
        if np.any(np.asarray(d[k]) != np.asarray(d[k])[:1]): bad.append(k + " isn't alike on all ranks")
    return bad
def reference(z, nx, x0, n0, hyp, uu):
    zz = z.astype(np.float64).reshape(FR, PR, 8, 16, MS).transpose(0, 2, 3, 1, 4).reshape(FR, 8, 16, M)
    sx = nx.astype(np.int64).reshape(FR, PR, 8, 3, MS).transpose(0, 2, 3, 1, 4).reshape(FR, 8, 3, M)
    x = x0[0].astype(np.float64).reshape(8, 16, NT); n = n0[0].astype(np.int64)
    tr = np.stack([gentries(a) for a in hyp]).astype(np.int64).reshape(N, 8, KR, H)
    u = np.stack([gentries(a) for a in uu]).astype(np.int64).reshape(N, 8, FR, KR, H)
    live = np.ones((N, 8, KR, H), bool); w0 = np.full(8, 2, np.int64); gi = np.arange(8)[None, :, None]
    ye = np.zeros((N, 8, 16, H)); yx = np.zeros((N, 8, 16, H))
    for t in range(FR):
        nm = np.take_along_axis(sx[t], n[:, None, :], 2)
        zc = np.take_along_axis(zz[t], nm.reshape(8, 1, 3 * NT), 2).reshape(8, 16, 3, NT)
        dist = np.abs(zc - x[:, :, None, :])
        wt = np.maximum(np.add.reduce((dist <= 1).astype(np.int64), axis=1) - 4, 0)
        m = np.zeros((N, 8, KR, H), np.int64); took = np.full((N, 8, KR, H), -1, np.int64)
        for k in range(KR):
            T = tr[:, :, k]
            c = np.stack([nm[gi, i, T] for i in range(3)], axis=2); w = np.stack([wt[gi, i, T] for i in range(3)], axis=2)
            for j in range(k): w = np.where(c == took[:, :, j][:, :, None, :], 0, w)
            p = np.add.accumulate(np.concatenate([np.broadcast_to(w0[None, :, None, None], (N, 8, 1, H)), w], axis=2), axis=2)
            pick = np.argmax(64 * p > u[:, :, t, k][:, :, None, :] * p[:, :, 3:], axis=2)
            m[:, :, k] = pick
            name = np.take_along_axis(c, np.maximum(pick - 1, 0)[:, :, None, :], 2)[:, :, 0]
            took[:, :, k] = np.where(live[:, :, k] & (pick > 0), name, -1)
        pair = 4 * tr + m
        ex = np.exp(-np.concatenate([np.ones((8, 16, 1, NT)), dist], axis=2)).transpose(0, 1, 3, 2).reshape(8, 16, 4 * NT)
        for q in range(N):
            v = np.take_along_axis(ex, pair[q].reshape(8, 1, KR * H), 2).reshape(8, 16, KR, H)
            ye[q] = ye[q] + np.add.reduce(np.where(live[q][:, None], v, 0.0), axis=2)
        miss = np.add.reduce((live & (m == 0)).astype(np.int64), axis=(0, 2, 3))
        w0 = 1 + (np.roll(miss, -1) >> S)
        mark = np.zeros((8, 4 * NT), np.int64)
        for g in range(8): mark[g, pair[:, g][live[:, g]]] = 1
        place = np.add.accumulate(mark, axis=1) - mark
        xn = np.zeros((8, 16, NT)); nn = np.zeros((8, NT), np.int64)
        for g in range(8):
            o = np.nonzero(mark[g])[0][:NT]; T = o >> 2; hit = (o & 3) > 0; i = np.maximum((o & 3) - 1, 0); xo = x[g][:, T]
            xn[g][:, :len(o)] = np.where(hit, xo + 0.25 * (zc[g][:, i, T] - xo), xo)
            nn[g, :len(o)] = np.where(hit, nm[g, i, T], n[g, T])
        new = place[np.arange(8)[None, :, None, None], pair]
        live = live & (new < NT); tr = np.where(live, new, 0); x = xn; n = nn
    for q in range(N):
        v = np.take_along_axis(x, tr[q].reshape(8, 1, KR * H), 2).reshape(8, 16, KR, H)
        yx[q] = np.add.reduce(np.where(live[q][:, None], v, 0.0), axis=2)
    return {"ye": ye.reshape(N, 128, H).astype(np.float32), "yx": yx.reshape(N, 128, H).astype(np.float32)}

def check_inputs(d):
    bad = list(check_ranges(d))
    if not bad:
        for name, y in reference(**d).items():
            for q in range(N):
                v = np.abs(np.asarray(y[q], np.float64)); s = np.sqrt(np.mean(v * v))
                if v.max() > 7 * s or s < 2.0 ** -1: bad.append('%s of rank %d is uneven or too small' % (name, q))
    return bad

@@ -1,0 +1,787 @@
+from concourse.bass import DstId, RemoteDMATransfer
+from concourse.mybir import AluOpType, AxisListType, ActivationFunctionType
+import math
+
+F32, BF, F16, I32, U16 = "float32", "bfloat16", "float16", "int32", "uint16"
+SCRATCH = {
+    "zs": ("dram", [4, 128, 512], BF), "zl": ("dram", [4, 128, 512], BF),
+    "nxs": ("dram", [4, 128, 96], I32), "nxl": ("dram", [4, 128, 96], I32),
+}
+for _n, _w, _d in [
+    ("zw0", 5120, BF), ("zw1", 4096, BF), ("nxw", 4096, I32), ("HU", 384, I32), ("HUh", 384, F16), ("HUs", 384, F16),
+    ("HUl", 384, F16), ("N0t", 16, I32), ("N0e", 128, F16), ("X0", 1024, F32), ("xo", 256, F16), ("xa", 256, F32), ("xb", 256, F32),
+    ("ip", 2, I32), ("ib", 8, I32), ("cf", 32, F32), ("XI", 224, BF), ("XD", 224, BF), ("XM", 160, BF), ("XE", 128, BF),
+    ("MA", 4, F32), ("MB", 8, F32), ("OH16", 16, F32), ("OH16b", 16, BF), ("OH32", 32, F32), ("GM", 8, F32),
+    ("M0", 8, F32), ("Wd", 896, BF), ("Dw", 144, BF), ("Wq", 544, BF), ("Rep", 512, BF), ("Rep4", 512, BF),
+    ("SelA", 32, BF), ("SelB", 32, BF), ("Sel5", 8, F32), ("Id", 512, BF), ("PL", 1280, BF), ("OE", 128, BF),
+    ("Yw", 132, BF), ("Yw32", 132, F32), ("Cb", 512, BF), ("tmpb", 128, BF), ("junk", 64, F32), ("ioi", 256, I32),
+    ("K0", 256, F32), ("Kb", 256, F32), ("L0", 16, U16), ("LN", 80, U16), ("R", 768, F16), ("d", 768, F16), ("ad", 768, F16),
+    ("ind", 768, BF), ("F", 1024, F32), ("G", 2048, F16), ("E", 4104, F32), ("XN", 4104, F32), ("V", 2048, F32),
+    ("pay", 1024, F32), ("pg", 256, F32), ("sw", 3072, F32), ("msk", 2048, BF), ("Qw", 256, F32), ("Ab", 8320, BF), ("Nb", 8320, BF),
+    ("LT", 128, U16), ("Llo", 128, U16), ("Lw", 128, U16), ("Lx", 128, U16), ("Ly", 128, U16), ("Lsc", 64, U16),
+    ("i1", 128, I32), ("i2", 128, I32), ("i3", 128, I32), ("i4", 128, I32), ("i5", 128, I32), ("i6", 128, I32),
+    ("baseN", 128, I32), ("keyM", 128, BF), ("key", 128, BF), ("mT", 128, F16), ("uT", 256, F32), ("f1", 128, F32), ("f2", 128, F32),
+    ("f3", 128, F32), ("Tl", 128, F16), ("Tx", 128, F16), ("wb", 128, F16), ("P", 128, F32), ("c", 384, F16), ("pr", 128, F32),
+    ("tk", 128, F32), ("Xq", 576, F32), ("ka", 64, F32), ("Mk", 128, BF), ("Cs", 132, F32), ("Cd", 128, F32), ("Dm", 256, F32),
+    ("Sz", 136, BF), ("Pq", 64, F16), ("zb", 1024, BF), ("Sq", 512, BF),
+    ("Hc", 4, F32), ("W0c", 4, F32), ("w0l", 4, F32), ("W0v", 32, F32), ("tixf", 128, F32), ("prf", 128, F32),
+    ("Ye", 512, F32), ("Yx", 512, F32), ("yel", 512, F32), ("yxl", 512, F32),
+]:
+    SCRATCH[_n] = ("sbuf", [128, _w], _d)
+for _n in ["pY", "pF0", "pF1", "pA", "pB", "pC", "pM", "pN"]:
+    SCRATCH[_n] = ("psum", [128, 512], F32)
+
+SEMAPHORES = (["cv", "ca", "cp", "cg", "lsem", "dz", "dz2", "dn", "dh", "d0", "dx", "wn0", "wn1", "wz0", "wz1", "ahu", "aw0", "sto"]
+              + ["%s%d" % (a, b) for a in ("an", "az", "ae", "ax") for b in range(4)])
+NA = (16, 13)
+MD = 21
+
+
+def rank_program(g, core, T, topo):
+    r = T.rank_of(core)
+    if r is None:
+        return
+    op = AluOpType
+    fn = ActivationFunctionType
+    Q = {"v": g.vector, "a": g.scalar, "p": g.tensor, "g": g, "s": g.sync}
+    cnt = {"v": 0, "a": 0, "p": 0, "g": 0}
+    seen = {q: {} for q in Q}
+    hist = {}
+    total = {}
+
+    def A(name, c0=0, c1=None, st=1, p0=0, p1=128):
+        t = T[name]
+        if c1 is None:
+            c1 = t.shape[1]
+        ap = t[p0:p1, c0:c1] if st == 1 else t[p0:p1, c0:c1:st]
+        return (ap, [(name, p0, p1, c0, c1, st)])
+
+    def col(name, c):
+        return A(name, c, c + 1)
+
+    def hp(n, c0, c1, p=64, st=1):
+        return A(n, c0, c1, st, 0, p)
+
+    def Ind(win, off):
+        return (win[0].indirect(off[0]), win[1] + off[1], win[1], off[1])
+
+    def wait(q, sem, val):
+        if seen[q].get(sem, 0) < val:
+            Q[q].wait_ge(T.sem[sem], val)
+            seen[q][sem] = val
+
+    def deps(q, reads, writes, skip=None):
+        need = {}
+        for regs, w in ((reads, False), (writes, True)):
+            for (n, p0, p1, c0, c1, st) in regs:
+                ps = SCRATCH[n][0] == "psum"
+                for key, (sem, val) in hist.get(n, {}).items():
+                    rq, rw, a0, a1, b0, b1, bs = key
+                    if (rq == "p" and q == "p") or sem == skip:
+                        continue
+                    apart = bs == st and (c0 - b0) % st != 0
+                    if (ps and rq != q) or ((w or rw) and a0 < p1 and p0 < a1 and b0 < c1 and c0 < b1 and not apart):
+                        need[sem] = max(need.get(sem, 0), val)
+        for sem, val in need.items():
+            wait(q, sem, val)
+
+    def note(q, reads, writes, sem, val):
+        for regs, w in ((reads, False), (writes, True)):
+            for (n, p0, p1, c0, c1, st) in regs:
+                hist.setdefault(n, {})[(q, w, p0, p1, c0, c1, st)] = (sem, val)
+
+    def issue(q, call, outs, ins, inc=True):
+        reads, writes = [], []
+        for x in ins:
+            if isinstance(x, tuple):
+                reads += x[1]
+        for x in outs:
+            if len(x) == 4:
+                writes += x[2]
+                reads += x[3]
+            else:
+                writes += x[1]
+        deps(q, reads, writes)
+        ins_ = call()
+        note(q, reads, writes, "c" + q, cnt[q] + 1)
+        if inc:
+            ins_.then_inc(T.sem["c" + q], 1)
+            cnt[q] += 1
+
+    def raw(x):
+        return x[0] if isinstance(x, tuple) else x
+
+    def ts(out, in0, s1, o0, s2=None, o1=None):
+        if o1 is None:
+            issue("v", lambda: g.vector.tensor_scalar(out[0], in0[0], raw(s1), None, o0), [out], [in0, s1])
+        else:
+            issue("v", lambda: g.vector.tensor_scalar(out[0], in0[0], raw(s1), raw(s2), o0, o1), [out], [in0, s1, s2])
+
+    def tt(out, a, b, o):
+        issue("v", lambda: g.vector.tensor_tensor(out[0], a[0], b[0], o), [out], [a, b])
+
+    def cp(out, a):
+        issue("v", lambda: g.vector.tensor_copy(out[0], a[0]), [out], [a])
+
+    def ms(out, val):
+        issue("v", lambda: g.vector.memset(out[0], val), [out], [])
+
+    def red(out, a):
+        issue("v", lambda: g.vector.tensor_reduce(out[0], a[0], AxisListType.X, op.add), [out], [a])
+
+    def act(out, a, f, bias=None, scale=None):
+        kw = {}
+        if bias is not None:
+            kw["bias"] = raw(bias)
+        if scale is not None:
+            kw["scale"] = raw(scale)
+        issue("a", lambda: g.scalar.activation(out[0], a[0], f, **kw), [out], [a, bias, scale])
+
+    def mm(out, l, rhs, start, stop, inc=None):
+        issue("p", lambda: g.tensor.matmul(out[0], l[0], rhs[0], start, stop), [out], [l, rhs], stop if inc is None else inc)
+
+    def iota(out, pat, base, cm):
+        if SCRATCH[out[1][0][0]][2] == I32:
+            issue("g", lambda: g.iota(out[0], pat, base, cm), [out], [])
+        else:
+            issue("g", lambda: g.iota(out[0], pat, base, cm, allow_small_or_imprecise_dtypes=True), [out], [])
+
+    def asel(out, a, pat, o, base, cm, fl=0.0):
+        issue("g", lambda: g.affine_select(out[0], a[0], pat, o, fl, base, cm), [out], [a])
+
+    def dma(q, out, in_, sem, n, wr=(), rd=()):
+        deps(q, list(rd), list(wr), sem)
+        Q[q].dma_start(out, in_).then_inc(T.sem[sem], 16)
+        total[sem] = 16 * n
+        note("d" + sem, list(rd), list(wr), sem, 16 * n)
+
+    def landed(regs, sem, val):
+        total[sem] = val
+        note("x" + sem, [], regs, sem, val)
+
+    def whole(n, c0=0, c1=None):
+        return [(n, 0, 128, c0, T[n].shape[-1] if c1 is None else c1, 1)]
+
+    def slot(n, s):
+        return [(n, 128 * s, 128 * s + 128, 0, 1, 1)]
+
+    def send(items, rd):
+        deps("g", rd, [])
+        tr = []
+        for (q, src, dst, sem, e0, ne) in items:
+            eng = topo.engines(core, T.cores[q])
+            m = 0
+            for e in eng[e0:e0 + ne]:
+                m |= 1 << e
+            rid, pid, se = topo.addr(T.cores[q])
+            tr.append((rid, pid, m, src, dst, sem))
+            total["lsem"] = total.get("lsem", 0) + ne
+        if len(tr) == 1:
+            rid, pid, m, src, dst, sem = tr[0]
+            g.remote_dma(dst, src, T.sem[sem], T.sem.lsem, pid, rid, m)
+        else:
+            g.remote_dma_fused([RemoteDMATransfer(dst_ids=[DstId(rid=rid, pnc=pid)], dma_engine_mask=m, remote_sem=T.sem[sem],
+                                                  src=src, dst=dst) for (rid, pid, m, src, dst, sem) in tr], local_sem=T.sem.lsem)
+
+    NE = len(topo.engines(core, T.cores[(r + 1) % 4]))
+    oth = [(r + 1) % 4, (r + 2) % 4, (r + 3) % 4]
+    frm = [(r - 1) % 4, (r - 2) % 4, (r - 3) % 4]
+    split3 = [(0, NE // 2), (NE // 2, NE // 4), (3 * NE // 4, NE // 4)]
+    eng3 = [NE // 2, NE // 4, NE // 4]
+    engz = [NE // 2, NE // 2, NE]
+
+    def send3(src, dst, w, sem):
+        send([(oth[j], T[src][:, w * oth[j]:w * oth[j] + w], T[dst][:, w * r:w * r + w], sem, split3[j][0], split3[j][1])
+              for j in range(3)], whole(src))
+
+    fill = []
+
+    def gap(n=1):
+        for _ in range(n):
+            if fill:
+                fill.pop(0)()
+
+    def run(L):
+        for f in L:
+            f()
+
+    dma("s", T.nxs[:], T.nx[:], "dn", 1, slot("nxs", 0))
+    for j in range(3):
+        dma("sa"[j % 2], T.zs[oth[j]], T.z[32 * oth[j]:32 * oth[j] + 32, :], "dz" if j < 2 else "dz2", 2 if j < 2 else 1, slot("zs", j // 2))
+    dma("a", T.HU[:, 0:128], T.hyp[:], "dh", 2, whole("HU"))
+    dma("a", T.HU[:, 128:384], T.uu[:], "dh", 2, whole("HU"))
+    dma("a", T.N0t[:], T.n0[2 * r:2 * r + 2, :], "d0", 1, whole("N0t"))
+    for a in range(4):
+        dma("sa"[a % 2], T.X0[32 * a:32 * a + 32, :], T.x0[32 * r:32 * r + 32, :], "dx", 4, whole("X0"))
+
+    def zhop(s, qs):
+        t, b = s >> 1, s & 1
+        w = "zw%d" % t
+        for a in range(4):
+            src = T.z[32 * r:32 * r + 32, :] if s == r else T.zl[s]
+            dma(qs[a % len(qs)], T[w][32 * a:32 * a + 32, 2048 * b:2048 * b + 2048], src, "wz%d" % t, 8 if t else 4,
+                whole(w, 0, 4096) if t else whole(w, 2048 * b, 2048 * b + 2048), [] if s == r else slot("zl", s))
+
+    zhop(r, "s")
+    for j, s in enumerate(frm):
+        landed(slot("nxl", s), "an%d" % s, eng3[j])
+        landed(slot("zl", s) if s >= 2 else whole("zb", 512 * s, 512 * s + 512), "az%d" % s, engz[j])
+        landed(whole("yel", 128 * s, 128 * s + 128), "ae%d" % s, eng3[j])
+        landed(whole("yxl", 128 * s, 128 * s + 128), "ax%d" % s, engz[j])
+        landed(whole("HUl", 96 * s, 96 * s + 96), "ahu", NE)
+    landed(whole("w0l"), "aw0", 1)
+
+    ms(A("nxw", 0, 768), 0)
+    iota(col("ip", 0), [[0, 1]], 0, 1)
+    iota(A("XD"), [[1, 224]], 0, -1)
+    iota(A("ioi"), [[1, 256]], 0, 256)
+    iota(A("nxw", 3584, 4096), [[0, 512]], 0, 0)
+    P0 = col("ip", 0)
+    ts(col("ib", 0), P0, 5, op.arith_shift_right)
+    ts(col("ib", 1), P0, 15, op.bitwise_and)
+    ts(col("ib", 2), P0, 16, op.bitwise_and)
+    ts(col("ib", 3), P0, 31, op.bitwise_and)
+    ts(col("ib", 4), P0, 4, op.arith_shift_right)
+    ts(col("ib", 5), P0, 3, op.arith_shift_right, 6, op.bitwise_and)
+    ts(col("ib", 6), P0, 6, op.arith_shift_right)
+    ts(col("ib", 7), P0, 112, op.bitwise_and)
+    cp(col("cf", 28), P0)
+    cp(A("cf", 0, 8), A("ib"))
+    ts(A("XI"), A("XD"), col("cf", 28), op.add)
+    ca, ci, ce16, c32, cg = col("cf", 0), col("cf", 1), col("cf", 2), col("cf", 3), col("cf", 4)
+    tt(col("cf", 8), col("cf", 5), col("cf", 6), op.add)
+    ts(A("MA"), A("XI", 0, 4), ca, op.is_equal)
+    ts(A("OH16"), A("XI", 0, 16), ci, op.is_equal)
+    ts(A("MB"), A("XI", 0, 8), col("cf", 8), op.is_equal)
+    for q in oth + [r]:
+        ts(A("Wd", 224 * q, 224 * q + 224), A("XD"), float(96 - 32 * q), op.is_equal, col("MA", q), op.mult)
+    cp(A("HUh"), A("HU"))
+    ms(A("nxw", 768, 3584), 0)
+    for q in oth + [r]:
+        for kind in range(3):
+            for k in range(4):
+                mm(A("pM", 96 * q + kind, 96 * q + 96, 3), A("Wd", 224 * q + 96 - 32 * k, 224 * q + 224 - 32 * k),
+                   A("HUh", 128 * kind + 32 * k, 128 * kind + 32 * k + 32), k == 0, k == 3, k == 3 and kind == 2)
+    cp(A("HUs"), A("pM", 0, 384))
+    ts(A("OH16b"), A("XI", 0, 16), ci, op.is_equal)
+    for b in range(8):
+        ts(A("N0e", 16 * b, 16 * b + 16), A("N0t"), -2047.0, op.add, col("MB", b), op.mult)
+    mm(A("pN", 0, 16), A("N0e"), A("OH16b"), True, True)
+    Zb, One, Neg, Qrt = [A("Cb", 128 * j, 128 * j + 128) for j in range(4)]
+    ts(A("OH32"), A("XI", 0, 32), c32, op.is_equal)
+    ts(col("cf", 9), col("cf", 7), 15.0, op.add)
+    ts(col("cf", 10), ce16, 8.0, op.add)
+    ms(Zb, 0.0)
+    tt(A("M0", 0, 3), A("OH32", 0, 13, 6), A("OH32", 18, 31, 6), op.add)
+    cp(col("M0", 3), col("OH16", 4))
+    ts(A("Dw"), A("XI", 0, 144), col("cf", 9), op.is_equal)
+    ts(A("M0", 4, 8), A("M0", 0, 4), -2047.0, op.mult)
+    ts(A("L0"), A("pN", 0, 16), 2047.0, op.add)
+    ts(A("ioi"), A("ioi"), 4095, op.bitwise_and)
+    cp(A("HUl", 96 * r, 96 * r + 96), A("HUs", 96 * r, 96 * r + 96))
+    ms(Neg, -2048.0)
+    ms(Qrt, 0.25)
+
+    def send_z():
+        dst = T.zl[r] if r >= 2 else T.zb[:, 512 * r:512 * r + 512]
+        send([(oth[j], T.zs[oth[j]], dst, "az%d" % r, j * NE // 2, NE // 2) for j in range(2)], slot("zs", 0))
+        send([(oth[2], T.zs[oth[2]], dst, "az%d" % r, 0, NE)], slot("zs", 1))
+
+    send([(oth[j], T.nxs[oth[j]], T.nxl[r], "an%d" % r, split3[j][0], split3[j][1]) for j in range(3)], slot("nxs", 0))
+    if r < 2:
+        send_z()
+    iota(A("XM"), [[0, 5], [1, 32]], 0, 0)
+    iota(One, [[0, 128]], 1, 0)
+    if r < 2:
+        send3("HUs", "HUl", 96, "ahu")
+    for cq in range(4):
+        asel(A("Sq", 128 * cq, 128 * cq + 128), One, [[0, 4], [-4, 32]], op.is_equal, -cq, 1)
+    if r >= 2:
+        send3("HUs", "HUl", 96, "ahu")
+        deps("g", whole("zb"), [])
+        send_z()
+    iota(A("K0"), [[1, 256]], 0, 0)
+    iota(A("junk"), [[16, 64]], 2048, 0)
+    iota(hp("Dm", 128, 256, 65), [[-2, 2], [0, 64]], 1, 0)
+    asel(hp("Dm", 0, 64, 65), hp("Dm", 128, 192, 65), [[-1, 64]], op.is_equal, 0, 1)
+    asel(hp("Dm", 64, 128, 65), hp("Dm", 192, 256, 65), [[-1, 64]], op.is_equal, -1, 1)
+    asel(hp("Dm", 64, 128, 65), hp("Dm", 64, 128, 65), [[1, 64]], op.is_ge, -MD, 0)
+    o64, n64, t64 = hp("Cb", 128, 256), hp("Cb", 256, 384), hp("tmpb", 0, 128)
+
+    def pl(e, j):
+        return hp("PL", 640 * e + 128 * j, 640 * e + 128 * j + 128)
+    for e in range(2):
+        se = [-128 * (1 - 2 * e), 2]
+        asel(pl(e, 2), o64, [[-16, 4], se, [-1, 16]], op.is_equal, -128 * e, 1)
+        asel(pl(e, 4), n64, [[-16, 4], se, [-1, 16]], op.is_equal, -128 * e, 1)
+        asel(t64, o64, [[-16, 4], se, [-1, 16]], op.is_gt, -128 * e, 1)
+        asel(pl(e, 0), t64, [[16, 4], [0, 32]], op.is_gt, 16, -1)
+        asel(t64, o64, [[16, 4], se, [1, 16]], op.is_gt, -128 * e, -1)
+        asel(pl(e, 1), t64, [[-16, 4], [0, 32]], op.is_ge, 0, 1)
+        asel(pl(e, 3), o64, [[16, 4], se, [0, 16]], op.is_gt, -128 * e, -1)
+    for q in range(4):
+        asel(A("Rep", 128 * q, 128 * q + 128), One, [[0, 4], [-1, 32]], op.is_equal, -32 * q, 1)
+    iota(A("sw", 0, 2048), [[0, 2048]], 0, 0)
+    asel(A("E", 0, 1024), A("X0"), [[0, 1024]], op.is_equal, 1, 0, math.exp(-1.0))
+    iota(A("XE"), [[0, 4], [16, 2], [0, 16]], 0, 0)
+    for q in range(4):
+        asel(A("Rep4", 128 * q, 128 * q + 128), Qrt, [[0, 4], [-1, 32]], op.is_equal, -32 * q, 1)
+
+    act(A("zw0", 4096, 5120), A("X0"), fn.Copy)
+    for a in range(4):
+        act(A("xo", 0, 256, 1, 32 * a, 32 * a + 32), A("X0", 256 * a, 256 * a + 256, 1, 32 * a, 32 * a + 32), fn.Copy)
+
+    def nxhop(t, qs, n):
+        for s in [x for x in [r] + frm if x >> 1 == t]:
+            for a in range(4):
+                src = T.nx[6 * r:6 * r + 6, :] if s == r else T.nxl[s]
+                dma(qs[a % len(qs)], T.nxw[32 * a + t:32 * a + 32:6, 2048 * (s & 1):2048 * (s & 1) + 2048], src, "wn%d" % t, n,
+                    whole("nxw"), [] if s == r else slot("nxl", s))
+    nxhop(0, "sa", 8)
+
+    def zspread(j, cqs):
+        L = []
+        for s in [x for x in frm if x < 2][j:j + 1]:
+            for cq in cqs:
+                b = [["pY", "pA", "pB", "pC"], ["pM", "pY", "pA", "pB"]][j][cq]
+                mm(A(b), A("Sq", 128 * cq, 128 * cq + 128), A("zb", 512 * s, 512 * s + 512), True, True)
+                o = A("zw0", 2048 * s + 512 * cq, 2048 * s + 512 * cq + 512)
+                if (j == 0 and (r >= 2 or cq < 2)) or (j == 1 and cq == 3):
+                    act(o, A(b), fn.Copy)
+                else:
+                    L.append(lambda o=o, b=b: cp(o, A(b)))
+        return L
+
+    ts(A("Id", 0, 128), A("XD", 0, 128), 0.0, op.is_equal)
+    for q in range(4):
+        ts(A("Wq", 136 * q, 136 * q + 136), A("XM", 0, 136), col("cf", 10), op.is_equal, col("MA", q), op.mult)
+    ts(col("cf", 11), ci, 3.0, op.is_lt, 2051.0, op.mult)
+    ts(col("cf", 13), ci, 3.0, op.is_lt, -2047.0, op.mult)
+    ts(A("GM"), A("XI", 0, 8), cg, op.is_equal)
+    ts(col("cf", 15), col("OH16", 6), 2048.0, op.mult)
+    tt(A("cf", 16, 18), A("OH16", 1, 3), A("OH16", 0, 2), op.subtract)
+    cp(A("cf", 21, 24), A("OH16", 3, 6))
+    ts(col("cf", 12), col("cf", 11), -4.0, op.add)
+    tt(col("cf", 14), col("cf", 13), col("OH16", 6), op.add)
+    ts(A("cf", 18, 21), A("OH16", 0, 3), col("cf", 15), op.add)
+    cEv, cGa = col("cf", 12), col("cf", 14)
+    sel = [lambda s=s, e=e: ts(A("SelA" if s < 4 else "SelB", 2 * (s % 4) + e, 32, 8), A("GM", e, 8, 2), col("cf", 16 + s), op.mult)
+           for s in range(8) for e in range(2)]
+    run(sel)
+
+    def row_keys(src):
+        return [lambda: cp(A("i1"), src),
+                lambda: ts(A("baseN"), A("i1"), 2, op.arith_shift_right, 60, op.bitwise_and),
+                lambda: ts(A("i2"), A("i1"), 4, op.arith_shift_right, 112, op.bitwise_and),
+                lambda: ts(A("i3"), A("i1"), 15, op.bitwise_and),
+                lambda: tt(A("keyM"), A("i2"), A("i3"), op.add)]
+
+    def hot_m(n):
+        return [lambda v=v: ts(A("Ab", 128 * v, 128 * v + 128), A("keyM"), float(v), op.is_equal) for v in range(n)]
+    steps = [lambda v=v: act(A("Ab", 128 * v, 128 * v + 128), A("keyM"), fn.Sign, 0.5 - v) for v in range(MD, 64)]
+
+    def gates(t, early, mid):
+        zw = A("zw%d" % t, 0, 4096)
+
+        def tab(f, src, m, last):
+            for q in range(4):
+                mm(A("pF%d" % (q >> 1), 256 * (q & 1), 256 * (q & 1) + 256), A("Wq", 136 * q + 8 - f, 136 * q + 136 - f),
+                   A(src, 256 * m, 256 * m + 256), False, last and (q & 1) == 1)
+        for m in range(3):
+            tab(m, "R", m, False)
+        early()
+        for m in range(3):
+            s = (256 * m, 256 * m + 256)
+            tt(A("d", *s), Ind(zw, A("LN", 16 * m, 16 * m + 16)), A("xo"), op.subtract)
+            act(A("ad", *s), A("d", *s), fn.Abs)
+            if m > 0:
+                ts(A("ind", s[0] - 256, s[0]), A("ad", s[0] - 256, s[0]), 1.0, op.is_le)
+                tab(2 + m, "ind", m - 1, False)
+        gap(3)
+        ts(A("ind", 512, 768), A("ad", 512, 768), 1.0, op.is_le)
+        tab(5, "ind", 2, True)
+        mid()
+
+    def clear_tab():
+        for b in range(2):
+            mm(A("pF%d" % b), Zb, A("Wq", 0, 512), True, False, False)
+
+    def fields(pause=None):
+        act(A("F", 0, 512), A("pF0"), fn.Relu, cEv)
+        ts(A("F", 512, 1024), A("pF1"), cEv, op.add, 0.0, op.max)
+        if pause:
+            pause()
+        act(A("G", 0, 1024), Ind(A("F"), A("LT", 0, 64)), fn.Identity, cGa)
+        ts(A("G", 1024, 2048), Ind(A("F"), A("LT", 64, 128)), cGa, op.add)
+        for n, s in (("pB", "SelB"), ("pA", "SelA")):
+            for i in range(16):
+                mm(A(n, i, 512, 16), A("G", i, 2048, 16), A(s), True, True, i == 15)
+
+    def tables(t, banks, later=None):
+        j = 0
+        for m in range(3):
+            for h in range(2):
+                b = banks[j % len(banks)]
+                j += 1
+                for u in range(2):
+                    q = 2 * h + u
+                    mm(A(b, 256 * u, 256 * u + 256), A("Rep", 128 * q, 128 * q + 128), A("ad", 256 * m, 256 * m + 256), True, True, u == 1)
+                o = 1024 * (m + 1) + 512 * h
+                if later is None:
+                    act(A("E", o, o + 512), A(b), fn.Exp, None, -1.0)
+                else:
+                    later.append(lambda o=o, b=b: act(A("E", o, o + 512), A(b), fn.Exp, None, -1.0))
+
+    def new_x(js, banks):
+        for j, b in zip(js, banks):
+            m, h = j >> 1, j & 1
+            for u in range(2):
+                q = 2 * h + u
+                mm(A(b, 256 * u, 256 * u + 256), A("Rep", 128 * q, 128 * q + 128), A("xo"), True, m == 0, m == 0 and u == 1)
+                if m:
+                    mm(A(b, 256 * u, 256 * u + 256), A("Rep4", 128 * q, 128 * q + 128), A("d", 256 * m - 256, 256 * m), False, True, u == 1)
+            act(A("XN", 512 * j, 512 * j + 512), A(b), fn.Copy)
+
+    def draws(t):
+        def N(k, f):
+            return A("pA", 128 * k + 64 + 32 * f, 128 * k + 96 + 32 * f) if f < 2 else A("pB", 128 * k, 128 * k + 32)
+
+        def excl(j, k):
+            x = 96 * {(0, 1): 0, (0, 2): 1, (0, 3): 2, (1, 2): 3, (1, 3): 4, (2, 3): 5}[(j, k)]
+            Vk = A("pB", 128 * k + 32, 128 * k + 128)
+            L = [lambda f=f: tt(A("Xq", x + 32 * f, x + 32 * f + 32), N(k, f), A("tk", 32 * j, 32 * j + 32), op.not_equal) for f in (2, 0, 1)]
+            L.append(lambda: tt(Vk, Vk, A("Xq", x, x + 96), op.mult))
+            return L
+        own = []
+
+        def g1():
+            if own:
+                own.pop(0)()
+            else:
+                gap()
+        for k in range(4):
+            def V(m):
+                return A("pB", 128 * k + 32 * m, 128 * k + 32 * m + 32)
+
+            def Pm(m):
+                return A("P", 32 * m, 32 * m + 32)
+
+            def C(s, n=1):
+                return A("c", 96 * k + 32 * s, 96 * k + 32 * (s + n))
+            if t == 0:
+                ts(Pm(1), V(1), 2.0, op.add)
+            else:
+                tt(Pm(1), V(1), A("W0v"), op.add)
+            g1()
+            tt(Pm(2), V(2), Pm(1), op.add)
+            g1()
+            tt(Pm(3), V(3), Pm(2), op.add)
+            g1()
+            tt(Pm(0), Pm(3), A("uT", 128 * t + 32 * k, 128 * t + 32 * k + 32), op.mult)
+            g1()
+            if t == 0:
+                ts(C(2), Pm(0), 2.0, op.is_ge)
+            else:
+                tt(C(2), Pm(0), A("W0v"), op.is_ge)
+            tt(C(0), Pm(0), Pm(1), op.is_ge)
+            tt(C(1), Pm(0), Pm(2), op.is_ge)
+            kk = [lambda k=k, C=C: tt(A("ka", 0, 32), C(2), A("baseN", 32 * k, 32 * k + 32), op.add),
+                  lambda C=C: tt(A("ka", 32, 64), C(0), C(1), op.add),
+                  lambda k=k: tt(A("key", 32 * k, 32 * k + 32), A("ka", 0, 32), A("ka", 32, 64), op.add)]
+            if k == 3:
+                kk[0]()
+                kk[1]()
+                gap()
+                kk[2]()
+                break
+            kk[0]()
+            tt(A("pr", 0, 96), A("pA", 128 * k, 128 * k + 96), C(0, 3), op.mult)
+            kk[1]()
+            tt(A("pr", 96, 128), A("pr", 0, 32), A("pr", 32, 64), op.add)
+            kk[2]()
+            tt(A("tk", 32 * k, 32 * k + 32), A("pr", 96, 128), A("pr", 64, 96), op.add)
+            g1()
+            while own:
+                own.pop(0)()
+            L = excl(k, k + 1)
+            run(L[:3])
+            for k2 in range(k + 2, 4):
+                own.extend(excl(k, k2))
+            g1()
+            L[3]()
+            g1()
+
+    def lists_after(t, Tx, T4):
+        tt(A("mT"), A("key"), A("baseN"), op.subtract)
+        mm(A("pN", 0, 128), A("mT"), A("Id", 128, 256), True, False)
+        mm(A("pN", 0, 128), A("Id", 0, 128), Tx, False, True, False)
+        if t == 0:
+            mm(A("pN", 128, 256), A("mT"), A("Id", 256, 384), True, False)
+            mm(A("pN", 128, 256), A("Id", 0, 128), A("wb"), False, True)
+        else:
+            mm(A("pN", 128, 256), A("mT"), A("Id", 0, 128), True, False)
+            mm(A("pN", 128, 256), A("Id", 384, 512), T4, False, True)
+
+    def hot_n(t, between):
+        nd = 64 - NA[t]
+        for v in range(nd, 64):
+            act(A("Nb", 128 * v, 128 * v + 128), A("key"), fn.Sign, 0.5 - v)
+        for v in range(nd):
+            ts(A("Nb", 128 * v, 128 * v + 128), A("key"), float(v), op.is_equal)
+            if v == 10:
+                between()
+
+    def counts(t):
+        nn = 65 if NA[t] else 64
+        nm = 65 - t
+        for e in range(2):
+            cols = [32 * k + 16 * e + i for k in range(4) for i in range(16)]
+            for j, c in enumerate(cols):
+                mm(hp("pC", 65 * e, 65 * e + nn, nm), A("Ab", c, 128 * nm, 128), A("Nb", c, 128 * nn, 128), j == 0, j == 63, j == 63 and e == 1)
+
+    def places(t):
+        nd = 64 - NA[t]
+        if t == 0:
+            if NA[0]:
+                cp(hp("Cs", 0, 130, 65), hp("pC", 0, 130, 65))
+            for e in range(2):
+                cp(hp("Cd", 64 * e, 64 * e + nd, 65), hp("pC", 65 * e, 65 * e + nd, 65))
+            if NA[0]:
+                for e in range(2):
+                    tt(hp("Cd", 64 * e + nd, 64 * e + 64, 65), hp("pC", 65 * e + nd, 65 * e + 64, 65),
+                       hp("Cs", 65 * e + nd + 1, 65 * e + 65, 65), op.subtract)
+            mm(hp("pM", 256, 384), hp("Dm", 128, 192, 65), hp("Cd", 0, 128, 65), True, True)
+            ts(hp("Mk", 0, 128), hp("pM", 256, 384), 0.0, op.is_gt)
+        else:
+            cp(hp("Cs", 0, 130), hp("pC", 0, 130))
+            for e in range(2):
+                ts(hp("Mk", 64 * e, 64 * e + nd), hp("pC", 65 * e, 65 * e + nd), 0.0, op.is_gt)
+            for e in range(2):
+                tt(hp("Mk", 64 * e + nd, 64 * e + 64), hp("pC", 65 * e + nd, 65 * e + 64), hp("Cs", 65 * e + nd + 1, 65 * e + 65), op.is_gt)
+        for e in range(2):
+            o, d0, d1 = hp("Sz", 68 * e + 4, 68 * e + 68), hp("Mk", 64 * e, 64 * e + 64), hp("Cb", 0, 64)
+            issue("v", lambda: g.vector.tensor_tensor_scan(o[0], d0[0], d1[0], 0.0, op.add, op.add), [o], [d0, d1])
+        for e in range(2):
+            mm(A("pM", 64, 65), pl(e, 3), hp("Sz", 68 * e + 67, 68 * e + 68), e == 0, e == 1, False)
+        for m in range(4):
+            L = []
+            for e in range(2):
+                L.append((pl(e, 0), hp("Sz", 68 * e + 3, 68 * e + 64, 64, 4)))
+                L.append((pl(e, 1), hp("Sz", 68 * e + 7, 68 * e + 68, 64, 4)))
+                L.append((pl(e, 2), hp("Sz", 68 * e + 3 + m, 68 * e + 64 + m, 64, 4)))
+                if t == 0:
+                    L.append((pl(e, 4), hp("Mk", 64 * e + m, 64 * e + 64, 64, 4)))
+            for j, (a_, b_) in enumerate(L):
+                mm(A("pM", 16 * m, 16 * m + 16), a_, b_, j == 0, j == len(L) - 1, j == len(L) - 1 and m == 3)
+
+    def terms_gather(q):
+        act(A("V", 512 * q, 512 * q + 512), Ind(A("E"), A("Lx", 32 * q, 32 * q + 32)), fn.Copy)
+
+    def terms_sum(q, last=False):
+        for u in range(4):
+            mm(A("pY", 128 * q, 128 * q + 128), A("Yw32", 3 - u, 131 - u), A("V", 512 * q + 128 * u, 512 * q + 128 * u + 128),
+               False, last and u == 3, u == 3)
+
+    nxw = A("nxw")
+    Tl0 = A("HUl", 0, 384, 3)
+    clear_tab()
+    zev = zspread(0, range(4)) + zspread(1, (0, 1))
+    for m in range(3):
+        ts(A("R", 256 * m, 256 * m + 256), Ind(nxw, A("L0")), -2047.0, op.add, col("M0", m), op.mult)
+    for i in range(16):
+        mm(A("pN", 0, 48), A("Dw", 15 - i, 143 - i), A("R", i, 768, 16), i == 0, i == 15)
+    dma("s", T.nxw[4:128:16, :], T.ioi[:], "wn1", 9, whole("nxw"), whole("ioi"))
+    nxhop(1, "s", 9)
+    for s in (2, 3):
+        if s != r:
+            zhop(s, "s")
+    zev += zspread(1, (2, 3))
+    run(zev[:1])
+    ts(A("LN", 0, 48), A("pN", 0, 48), 2047.0, op.add)
+    run(zev[1:])
+
+    def early0():
+        for kind in range(3):
+            mm(A("pC", 128 * kind, 128 * kind + 128), A("HUl", kind, 384, 3), A("Id", 0, 128), True, True, kind == 2)
+
+    def mid0():
+        cp(A("LT"), Tl0)
+        run(row_keys(A("pC", 0, 128)))
+    gates(0, early0, mid0)
+    fields()
+    run(steps)
+    ts(A("uT"), A("pC", 128, 384), 1.0 / 64, op.mult)
+    cp(A("i4"), Tl0)
+    for j, v in ((1, 1024.0), (2, 16.0), (3, 4.0)):
+        fill.append(lambda j=j, v=v: ts(A("Id", 128 * j, 128 * j + 128), A("XD", 0, 128), 0.0, op.is_equal, v, op.mult))
+    ts(A("i5"), A("i4"), 15, op.bitwise_and)
+    ts(A("i6"), A("i4"), 2, op.arith_shift_right, 192, op.bitwise_and)
+    fill.extend([lambda: ts(A("i4"), A("i4"), 4, op.arith_shift_right, 15, op.bitwise_and), lambda: ms(A("E", 4096, 4104), 0.0),
+                 lambda: tt(A("wb"), A("i4"), A("i6"), op.add),
+                 lambda: ms(A("Nb", 8192, 8320), -1.0), lambda: ms(A("Ab", 8192, 8320), -1.0)])
+    fill.extend(hot_m(MD))
+    draws(0)
+    gap(100)
+    lists_after(0, Tl0, None)
+    for k in range(4):
+        mm(A("pN", 256, 288), One, A("c", 96 * k + 64, 96 * k + 96), k == 0, k == 3)
+    ex0 = []
+    tables(0, ["pM", "pY", "pF0", "pF1", "pA", "pB"], ex0)
+    hot_n(0, lambda: cp(A("Lx"), A("pN", 0, 128)))
+    cp(A("Llo"), A("i5"))
+    counts(0)
+    run(ex0)
+    for q in range(4):
+        terms_gather(q)
+    act(A("msk"), Ind(A("OH16"), A("Llo")), fn.Copy)
+    for e in range(2):
+        red(col("Hc", e), A("pN", 256 + 16 * e, 272 + 16 * e))
+    cp(A("Lw"), A("pN", 128, 256))
+    ts(A("ib", 0, 2), A("Hc", 0, 2), -1.0, op.mult, 8192.0, op.add)
+    ts(A("ib", 2, 4), A("ib", 0, 2), 10, op.arith_shift_right)
+    ts(col("cf", 24), ca, 256.0, op.mult, 4096.0, op.add)
+    tt(col("cf", 25), col("OH16", 4), col("OH16", 5), op.add)
+    ts(col("cf", 26), col("OH16", 4), -1.0, op.mult, 1.0, op.add)
+    ts(A("W0c", 0, 2), A("ib", 2, 4), 1.0, op.add)
+    send([((r - 1) % 4, T.W0c[:, 0:2], T.w0l[:, 0:2], "aw0", 0, 1)], whole("W0c", 0, 2))
+    ts(A("Kb"), A("K0"), col("cf", 24), op.add, col("OH16", 5), op.mult)
+    ts(A("pg"), Ind(nxw, A("L0")), col("cf", 26), op.mult)
+    ts(A("K0"), A("K0"), col("cf", 24), op.add, col("cf", 25), op.mult)
+    for m in range(3):
+        tt(A("pay", 256 * m + 256, 256 * m + 512), Ind(nxw, A("LN", 16 * m, 16 * m + 16)), A("Kb"), op.add)
+    tt(A("pay", 0, 256), A("pg"), A("K0"), op.add)
+    ms(A("Sz"), 0.0)
+    tt(hp("Dm", 128, 192, 65), hp("Dm", 0, 64, 65), hp("Dm", 64, 128, 65), op.add)
+    ts(A("junk"), A("junk"), ci, op.add)
+    tt(A("Sel5", 0, 3), A("OH32", 1, 14, 6), A("OH32", 19, 32, 6), op.add)
+    cp(col("Sel5", 3), col("OH16", 5))
+    cp(col("Sel5", 4), col("OH16", 4))
+    places(0)
+    ms(A("XN", 4096, 4104), 0.0)
+    ts(col("cf", 27), c32, 4.0, op.mult, 3.0, op.add)
+    ts(A("OE"), A("XE"), ce16, op.is_equal)
+    ts(A("Yw32"), A("XI", 0, 132), col("cf", 27), op.is_equal)
+    ts(A("Yw"), A("XI", 0, 132), col("cf", 27), op.is_equal)
+    I = A("i1", 0, 64)
+    ts(I, A("pM", 0, 64), col("pM", 64), op.add, 2048.0, op.add)
+    ts(A("i2", 0, 64), I, 4, op.arith_shift_right)
+    ts(A("i3", 0, 64), I, 8, op.arith_shift_right)
+    ts(A("f1", 0, 64), I, 1024.0, op.is_ge, 8192.0, op.mult)
+    ts(A("f2", 0, 64), A("i2", 0, 64), 112.0, op.mult, ce16, op.add)
+    ts(A("f3", 0, 64), A("i3", 0, 64), -2016.0, op.mult)
+    tt(A("f1", 64, 128), A("f1", 0, 64), I, op.add)
+    tt(A("f2", 64, 128), A("f2", 0, 64), A("f3", 0, 64), op.add)
+    ts(A("Pq"), I, 1024.0, op.min)
+    tt(A("f3", 64, 128), A("f1", 64, 128), A("f2", 64, 128), op.add)
+    for q in range(4):
+        mm(A("pC", 64 * q, 64 * q + 64), A("Rep", 128 * q, 128 * q + 128), A("Pq"), True, True, q == 3)
+    act(A("Qw"), A("pC", 0, 256), fn.Copy)
+    ts(A("W0v", 0, 16), A("Cb", 0, 16), col("W0c", 1), op.add)
+    tt(A("f1", 0, 64), A("f3", 64, 128), A("junk"), op.min)
+    cp(A("Lsc"), A("f1", 0, 64))
+    cp(Ind(A("sw"), A("Lsc")), A("pay"))
+    mm(A("pY"), Zb, A("Wq", 0, 512), True, False, False)
+    clear_tab()
+    terms_sum(0)
+    terms_sum(1)
+    for c in range(16):
+        mm(A("pM", c, 80, 16), A("sw", 128 * c, 128 * c + 128), A("Sel5", 0, 5), True, True, c == 15)
+
+    def place_rows(j):
+        tt(A("G", 512 * j, 512 * j + 512), Ind(A("Qw"), A("Lw", 32 * j, 32 * j + 32)), A("msk", 512 * j, 512 * j + 512), op.mult)
+    for j in range(3):
+        place_rows(j)
+    cp(A("LN"), A("pM", 0, 80))
+
+    def new_rows(h):
+        for i in range(16):
+            mm(A("pN", 64 * h, 64 * h + 64), A("Dw", 15 - i, 143 - i), A("G", 1024 * h + i, 1024 * h + 1024, 16), i == 0, i == 15)
+    new_rows(0)
+    zx = A("zw0")
+    act(A("xa"), Ind(zx, A("LN", 64, 80)), fn.Copy, None, 0.25)
+    ts(A("xb"), Ind(zx, A("LN", 48, 64)), 0.75, op.mult)
+    for m in range(3):
+        act(A("R", 256 * m, 256 * m + 256), Ind(nxw, A("LN", 16 * m, 16 * m + 16)), fn.Identity, col("M0", 7), col("M0", 3))
+    tt(A("xo"), A("xa"), A("xb"), op.add)
+    place_rows(3)
+
+    def mid1():
+        cp(A("Tl"), A("pN", 0, 128))
+        ts(A("LT"), A("pN", 0, 128), 1023.0, op.min)
+        mm(A("pC", 0, 128), A("Tl"), A("Id", 0, 128), True, True)
+        terms_sum(2)
+        terms_sum(3)
+        ts(A("W0v", 16, 32), A("Cb", 0, 16), col("w0l", 0), op.add)
+        ts(A("f2"), A("Tl"), 1024.0, op.is_ge, 3072.0, op.mult)
+        tt(A("Tx"), A("f2"), A("Tl"), op.add)
+    gates(1, lambda: new_rows(1), mid1)
+    fields()
+    ts(A("f1"), A("pC", 0, 128), 1024.0, op.is_ge, -2.0, op.mult)
+    km = row_keys(A("pC", 0, 128))
+    km[0]()
+    tt(A("uT", 128, 256), A("uT", 128, 256), A("f1"), op.add)
+    tables(1, ["pM", "pN", "pF1", "pF0"])
+    new_x(range(5), ["pC", "pF1", "pF0", "pM", "pC"])
+    fill.extend(km[1:] + hot_m(64))
+    draws(1)
+    lists_after(1, A("Tx"), A("Tl"))
+    gap(3)
+    cp(A("Lx"), A("pN", 0, 128))
+    for q in range(4):
+        terms_gather(q)
+    gap(100)
+    hot_n(1, lambda: None)
+    new_x(range(5, 8), ["pA", "pB", "pF1"])
+    for q in range(4):
+        terms_sum(q, q == 3)
+    counts(1)
+    act(A("Ye"), A("pY"), fn.Copy)
+    send3("Ye", "yel", 128, "ae%d" % r)
+    cp(A("tixf"), A("pN", 0, 128))
+    cp(A("prf"), A("pN", 128, 256))
+    places(1)
+    ts(A("Pq"), A("pM", 0, 64), col("pM", 64), op.add, 1024.0, op.is_lt)
+    mm(A("pC", 0, 64), A("OE"), A("Pq"), True, True)
+    red(col("Hc", 2), A("pC", 0, 64))
+    ts(A("f1"), A("prf"), col("Hc", 2), op.is_ge, 8192.0, op.mult)
+    tt(A("f2"), A("f1"), A("tixf"), op.add)
+    ts(A("Ly"), A("f2"), 4096.0, op.min)
+    bank = dict(zip(oth + [r], ["pA", "pB", "pN", "pM"]))
+
+    def last_gather(q, e):
+        o, s = A("G", 512 * q, 512 * q + 512), Ind(A("XN"), A("Ly", 32 * q, 32 * q + 32))
+        if e == "a":
+            act(o, s, fn.Identity, -4.0)
+        else:
+            ts(o, s, -4.0, op.add)
+        for u in range(4):
+            mm(A(bank[q], 0, 128), A("Yw", 3 - u, 131 - u), A("G", 512 * q + 128 * u, 512 * q + 128 * u + 128), u == 0, u == 3)
+
+    def last_out(q, e):
+        o = A("Yx", 128 * q, 128 * q + 128)
+        if e == "a":
+            act(o, A(bank[q], 0, 128), fn.Identity, 16.0)
+        else:
+            ts(o, A(bank[q], 0, 128), 16.0, op.add)
+    last_gather(oth[0], "v")
+    last_gather(oth[1], "a")
+    last_gather(oth[2], "v")
+    last_out(oth[0], "a")
+    last_out(oth[1], "a")
+    send([(oth[j], T.Yx[:, 128 * oth[j]:128 * oth[j] + 128], T.yxl[:, 128 * r:128 * r + 128], "ax%d" % r, j * NE // 2, NE // 2)
+          for j in range(2)], whole("Yx", 128 * oth[0], 128 * oth[0] + 128) + whole("Yx", 128 * oth[1], 128 * oth[1] + 128))
+    last_gather(r, "a")
+    last_out(oth[2], "v")
+    send([(oth[2], T.Yx[:, 128 * oth[2]:128 * oth[2] + 128], T.yxl[:, 128 * r:128 * r + 128], "ax%d" % r, 0, NE)],
+         whole("Yx", 128 * oth[2], 128 * oth[2] + 128))
+    last_out(r, "v")
+    for out, own, land in (("ye", "Ye", "yel"), ("yx", "Yx", "yxl")):
+        for j, s in enumerate(frm[:2] + [r, frm[2]]):
+            n = own if s == r else land
+            dma("s" if out == "ye" else "sa"[j % 2], T[out][32 * s:32 * s + 32, :], T[n][:, 128 * s:128 * s + 128], "sto", 8, [],
+                whole(n, 128 * s, 128 * s + 128))
+    for q in cnt:
+        total["c" + q] = cnt[q]
+    for sem, val in total.items():
+        if val:
+            wait("g", sem, val)

@@ -17,13 +17,13 @@ for _n, _w, _d in [
     ("Yw", 132, BF), ("Yw32", 132, F32), ("Cb", 512, BF), ("tmpb", 128, BF), ("junk", 64, F32), ("ioi", 256, I32),
     ("K0", 256, F32), ("Kb", 256, F32), ("L0", 16, U16), ("LN", 80, U16), ("R", 768, F16), ("d", 768, F16), ("ad", 768, F16),
     ("ind", 768, BF), ("F", 1024, F32), ("G", 2048, F16), ("E", 4104, F32), ("XN", 4104, F32), ("V", 2048, F32),
-    ("pay", 1024, F32), ("pg", 256, F32), ("sw", 3072, F32), ("msk", 2048, BF), ("Qw", 256, F32), ("Ab", 8320, BF), ("Nb", 8320, BF),
+    ("pay", 1024, F32), ("pg", 256, F32), ("sw", 3072, F32), ("msk", 2048, BF), ("Qw", 256, F32), ("Ab", 8192, BF), ("Nb", 9216, BF),
     ("LT", 128, U16), ("Llo", 128, U16), ("Lw", 128, U16), ("Lx", 128, U16), ("Ly", 128, U16), ("Lsc", 64, U16),
     ("i1", 128, I32), ("i2", 128, I32), ("i3", 128, I32), ("i4", 128, I32), ("i5", 128, I32), ("i6", 128, I32),
-    ("baseN", 128, I32), ("keyM", 128, BF), ("key", 128, BF), ("mT", 128, F16), ("uT", 256, F32), ("f1", 128, F32), ("f2", 128, F32),
+    ("baseN", 128, F32), ("bI", 128, I32), ("keyM", 128, BF), ("key", 128, BF), ("mT", 128, F16), ("uT", 256, F32), ("f1", 128, F32), ("f2", 128, F32),
     ("f3", 128, F32), ("Tl", 128, F16), ("Tx", 128, F16), ("wb", 128, F16), ("P", 128, F32), ("c", 384, F16), ("pr", 128, F32),
     ("tk", 128, F32), ("Xq", 576, F32), ("ka", 64, F32), ("Mk", 128, BF), ("Cs", 132, F32), ("Cd", 128, F32), ("Dm", 256, F32),
-    ("Sz", 136, BF), ("Pq", 64, F16), ("zb", 1024, BF), ("Sq", 512, BF),
+    ("Sz", 136, BF), ("Pq", 64, F16), ("zb", 1024, BF), ("Vs", 128, F32), ("Sq", 512, BF),
     ("Hc", 4, F32), ("W0c", 4, F32), ("w0l", 4, F32), ("W0v", 32, F32), ("tixf", 128, F32), ("prf", 128, F32),
     ("Ye", 512, F32), ("Yx", 512, F32), ("yel", 512, F32), ("yxl", 512, F32),
 ]:
@@ -34,6 +34,10 @@ for _n in ["pY", "pF0", "pF1", "pA", "pB", "pC", "pM", "pN"]:
 SEMAPHORES = (["cv", "ca", "cp", "cg", "lsem", "dz", "dz2", "dn", "dh", "d0", "dx", "wn0", "wn1", "wz0", "wz1", "ahu", "aw0", "sto"]
               + ["%s%d" % (a, b) for a in ("an", "az", "ae", "ax") for b in range(4)])
 NA = (16, 13)
+LA = (0, 62)
+ND = (48, 94)
+EA = (50, 22)
+NF = (3, 3)
 MD = 21
 
 
@@ -302,10 +306,8 @@ def rank_program(g, core, T, topo):
         send_z()
     iota(A("K0"), [[1, 256]], 0, 0)
     iota(A("junk"), [[16, 64]], 2048, 0)
-    iota(hp("Dm", 128, 256, 65), [[-2, 2], [0, 64]], 1, 0)
-    asel(hp("Dm", 0, 64, 65), hp("Dm", 128, 192, 65), [[-1, 64]], op.is_equal, 0, 1)
-    asel(hp("Dm", 64, 128, 65), hp("Dm", 192, 256, 65), [[-1, 64]], op.is_equal, -1, 1)
-    asel(hp("Dm", 64, 128, 65), hp("Dm", 64, 128, 65), [[1, 64]], op.is_ge, -MD, 0)
+    for q in range(4):
+        asel(A("Rep", 128 * q, 128 * q + 128), One, [[0, 4], [-1, 32]], op.is_equal, -32 * q, 1)
     o64, n64, t64 = hp("Cb", 128, 256), hp("Cb", 256, 384), hp("tmpb", 0, 128)
 
     def pl(e, j):
@@ -319,8 +321,6 @@ def rank_program(g, core, T, topo):
         asel(t64, o64, [[16, 4], se, [1, 16]], op.is_gt, -128 * e, -1)
         asel(pl(e, 1), t64, [[-16, 4], [0, 32]], op.is_ge, 0, 1)
         asel(pl(e, 3), o64, [[16, 4], se, [0, 16]], op.is_gt, -128 * e, -1)
-    for q in range(4):
-        asel(A("Rep", 128 * q, 128 * q + 128), One, [[0, 4], [-1, 32]], op.is_equal, -32 * q, 1)
     iota(A("sw", 0, 2048), [[0, 2048]], 0, 0)
     asel(A("E", 0, 1024), A("X0"), [[0, 1024]], op.is_equal, 1, 0, math.exp(-1.0))
     iota(A("XE"), [[0, 4], [16, 2], [0, 16]], 0, 0)
@@ -368,10 +368,16 @@ def rank_program(g, core, T, topo):
     sel = [lambda s=s, e=e: ts(A("SelA" if s < 4 else "SelB", 2 * (s % 4) + e, 32, 8), A("GM", e, 8, 2), col("cf", 16 + s), op.mult)
            for s in range(8) for e in range(2)]
     run(sel)
+    ts(col("cf", 24), ca, 256.0, op.mult, 4096.0, op.add)
+    tt(col("cf", 25), col("OH16", 4), col("OH16", 5), op.add)
+    ts(col("cf", 26), col("OH16", 4), -1.0, op.mult, 1.0, op.add)
+    ts(col("cf", 27), c32, 4.0, op.mult, 3.0, op.add)
+    ms(A("Sz"), 0.0)
 
     def row_keys(src):
         return [lambda: cp(A("i1"), src),
-                lambda: ts(A("baseN"), A("i1"), 2, op.arith_shift_right, 60, op.bitwise_and),
+                lambda: ts(A("bI"), A("i1"), 2, op.arith_shift_right, 60, op.bitwise_and),
+                lambda: ts(A("baseN"), A("bI"), 0.5, op.add),
                 lambda: ts(A("i2"), A("i1"), 4, op.arith_shift_right, 112, op.bitwise_and),
                 lambda: ts(A("i3"), A("i1"), 15, op.bitwise_and),
                 lambda: tt(A("keyM"), A("i2"), A("i3"), op.add)]
@@ -457,11 +463,12 @@ def rank_program(g, core, T, topo):
         def g1():
             if own:
                 own.pop(0)()
+                gap(NF[t] - 1)
             else:
-                gap()
+                gap(NF[t])
         for k in range(4):
             def V(m):
-                return A("pB", 128 * k + 32 * m, 128 * k + 32 * m + 32)
+                return A("pB", 32 * m, 32 * m + 32) if k == 0 else A("Vs", 32 * m - 32, 32 * m)
 
             def Pm(m):
                 return A("P", 32 * m, 32 * m + 32)
@@ -472,11 +479,16 @@ def rank_program(g, core, T, topo):
                 ts(Pm(1), V(1), 2.0, op.add)
             else:
                 tt(Pm(1), V(1), A("W0v"), op.add)
+            if k:
+                tt(A("Vs", 96, 128), V(2), V(3), op.add)
             g1()
+            if k:
+                tt(Pm(3), A("Vs", 96, 128), Pm(1), op.add)
             tt(Pm(2), V(2), Pm(1), op.add)
             g1()
-            tt(Pm(3), V(3), Pm(2), op.add)
-            g1()
+            if k == 0:
+                tt(Pm(3), V(3), Pm(2), op.add)
+                g1()
             tt(Pm(0), Pm(3), A("uT", 128 * t + 32 * k, 128 * t + 32 * k + 32), op.mult)
             g1()
             if t == 0:
@@ -497,18 +509,21 @@ def rank_program(g, core, T, topo):
             kk[0]()
             tt(A("pr", 0, 96), A("pA", 128 * k, 128 * k + 96), C(0, 3), op.mult)
             kk[1]()
-            tt(A("pr", 96, 128), A("pr", 0, 32), A("pr", 32, 64), op.add)
-            kk[2]()
-            tt(A("tk", 32 * k, 32 * k + 32), A("pr", 96, 128), A("pr", 64, 96), op.add)
             g1()
+            tt(A("pr", 96, 128), A("pr", 0, 32), A("pr", 32, 64), op.add)
+            for f in range(3):
+                tt(A("Xq", 480 + 32 * f, 512 + 32 * f), N(k + 1, f), A("pr", 64, 96), op.subtract)
+            kk[2]()
             while own:
                 own.pop(0)()
-            L = excl(k, k + 1)
-            run(L[:3])
+            for f in range(3):
+                tt(A("Xq", 32 * f, 32 * f + 32), A("Xq", 480 + 32 * f, 512 + 32 * f), A("pr", 96, 128), op.not_equal)
+            if k < 2:
+                tt(A("tk", 32 * k, 32 * k + 32), A("pr", 96, 128), A("pr", 64, 96), op.add)
+            gap(NF[t])
+            tt(A("Vs", 0, 96), A("pB", 128 * k + 160, 128 * k + 256), A("Xq", 0, 96), op.mult)
             for k2 in range(k + 2, 4):
                 own.extend(excl(k, k2))
-            g1()
-            L[3]()
             g1()
 
     def lists_after(t, Tx, T4):
@@ -521,6 +536,31 @@ def rank_program(g, core, T, topo):
         else:
             mm(A("pN", 128, 256), A("mT"), A("Id", 0, 128), True, False)
             mm(A("pN", 128, 256), A("Id", 384, 512), T4, False, True)
+
+    def count_cols(t, between):
+        nd, early = ND[t], EA[t]
+        ca_, cv_ = list(range(128 - nd)), list(range(128 - nd, 128))
+        order = ca_[:early]
+        ra = ca_[early:]
+        j = 0
+        for n, c in enumerate(cv_):
+            order.append(c)
+            while j < len(ra) and j * (len(cv_) - LA[t]) <= (n - LA[t]) * len(ra):
+                order.append(ra[j])
+                j += 1
+        order += ra[j:]
+        first = [[c for c in order if (c >> 4) & 1 == e][0] for e in range(2)]
+        last = [[c for c in order if (c >> 4) & 1 == e][-1] for e in range(2)]
+        for n, c in enumerate(order):
+            o = A("Nb", 72 * c, 72 * c + 65)
+            if c < 128 - nd:
+                act(o, A("XI", 0, 65), fn.Sign, col("key", c), -1.0)
+            else:
+                ts(o, A("XI", 0, 65), col("key", c), op.is_le, 2.0, op.mult)
+            if n in between:
+                between[n]()
+            e = (c >> 4) & 1
+            mm(hp(["pC", "pM"][e], 0, 65), A("Ab", c, 8192, 128), o, c == first[e], c == last[e])
 
     def hot_n(t, between):
         nd = 64 - NA[t]
@@ -540,24 +580,10 @@ def rank_program(g, core, T, topo):
                 mm(hp("pC", 65 * e, 65 * e + nn, nm), A("Ab", c, 128 * nm, 128), A("Nb", c, 128 * nn, 128), j == 0, j == 63, j == 63 and e == 1)
 
     def places(t):
-        nd = 64 - NA[t]
-        if t == 0:
-            if NA[0]:
-                cp(hp("Cs", 0, 130, 65), hp("pC", 0, 130, 65))
-            for e in range(2):
-                cp(hp("Cd", 64 * e, 64 * e + nd, 65), hp("pC", 65 * e, 65 * e + nd, 65))
-            if NA[0]:
-                for e in range(2):
-                    tt(hp("Cd", 64 * e + nd, 64 * e + 64, 65), hp("pC", 65 * e + nd, 65 * e + 64, 65),
-                       hp("Cs", 65 * e + nd + 1, 65 * e + 65, 65), op.subtract)
-            mm(hp("pM", 256, 384), hp("Dm", 128, 192, 65), hp("Cd", 0, 128, 65), True, True)
-            ts(hp("Mk", 0, 128), hp("pM", 256, 384), 0.0, op.is_gt)
-        else:
-            cp(hp("Cs", 0, 130), hp("pC", 0, 130))
-            for e in range(2):
-                ts(hp("Mk", 64 * e, 64 * e + nd), hp("pC", 65 * e, 65 * e + nd), 0.0, op.is_gt)
-            for e in range(2):
-                tt(hp("Mk", 64 * e + nd, 64 * e + 64), hp("pC", 65 * e + nd, 65 * e + 64), hp("Cs", 65 * e + nd + 1, 65 * e + 65), op.is_gt)
+        for e in range(2):
+            cp(hp("Cs", 64 * e, 64 * e + 64), hp(["pC", "pM"][e], 1, 65))
+        for e in range(2):
+            tt(hp("Mk", 64 * e, 64 * e + 64), hp(["pC", "pM"][e], 0, 64), hp("Cs", 64 * e, 64 * e + 64), op.is_gt)
         for e in range(2):
             o, d0, d1 = hp("Sz", 68 * e + 4, 68 * e + 68), hp("Mk", 64 * e, 64 * e + 64), hp("Cb", 0, 64)
             issue("v", lambda: g.vector.tensor_tensor_scan(o[0], d0[0], d1[0], 0.0, op.add, op.add), [o], [d0, d1])
@@ -609,7 +635,7 @@ def rank_program(g, core, T, topo):
         run(row_keys(A("pC", 0, 128)))
     gates(0, early0, mid0)
     fields()
-    run(steps)
+    tables(0, ["pF0", "pF1", "pY"])
     ts(A("uT"), A("pC", 128, 384), 1.0 / 64, op.mult)
     cp(A("i4"), Tl0)
     for j, v in ((1, 1024.0), (2, 16.0), (3, 4.0)):
@@ -617,53 +643,34 @@ def rank_program(g, core, T, topo):
     ts(A("i5"), A("i4"), 15, op.bitwise_and)
     ts(A("i6"), A("i4"), 2, op.arith_shift_right, 192, op.bitwise_and)
     fill.extend([lambda: ts(A("i4"), A("i4"), 4, op.arith_shift_right, 15, op.bitwise_and), lambda: ms(A("E", 4096, 4104), 0.0),
-                 lambda: tt(A("wb"), A("i4"), A("i6"), op.add),
-                 lambda: ms(A("Nb", 8192, 8320), -1.0), lambda: ms(A("Ab", 8192, 8320), -1.0)])
-    fill.extend(hot_m(MD))
+                 lambda: tt(A("wb"), A("i4"), A("i6"), op.add)])
+    fill.extend(hot_m(64))
+    fill.extend([lambda: cp(A("Llo"), A("i5")),
+                 lambda: ts(A("Kb"), A("K0"), col("cf", 24), op.add, col("OH16", 5), op.mult),
+                 lambda: ts(A("K0"), A("K0"), col("cf", 24), op.add, col("cf", 25), op.mult),
+                 lambda: ts(A("junk"), A("junk"), ci, op.add),
+                 lambda: tt(A("Sel5", 0, 3), A("OH32", 1, 14, 6), A("OH32", 19, 32, 6), op.add),
+                 lambda: cp(col("Sel5", 3), col("OH16", 5)), lambda: cp(col("Sel5", 4), col("OH16", 4)),
+                 lambda: ts(A("Yw32"), A("XI", 0, 132), col("cf", 27), op.is_equal),
+                 lambda: ts(A("Yw"), A("XI", 0, 132), col("cf", 27), op.is_equal)])
     draws(0)
     gap(100)
+    count_cols(0, {})
     lists_after(0, Tl0, None)
     for k in range(4):
-        mm(A("pN", 256, 288), One, A("c", 96 * k + 64, 96 * k + 96), k == 0, k == 3)
-    ex0 = []
-    tables(0, ["pM", "pY", "pF0", "pF1", "pA", "pB"], ex0)
-    hot_n(0, lambda: cp(A("Lx"), A("pN", 0, 128)))
-    cp(A("Llo"), A("i5"))
-    counts(0)
-    run(ex0)
-    for q in range(4):
-        terms_gather(q)
+        mm(A("pA", 0, 32), One, A("c", 96 * k + 64, 96 * k + 96), k == 0, k == 3)
+    act(A("pg"), Ind(nxw, A("L0")), fn.Copy, None, col("cf", 26))
     act(A("msk"), Ind(A("OH16"), A("Llo")), fn.Copy)
-    for e in range(2):
-        red(col("Hc", e), A("pN", 256 + 16 * e, 272 + 16 * e))
-    cp(A("Lw"), A("pN", 128, 256))
-    ts(A("ib", 0, 2), A("Hc", 0, 2), -1.0, op.mult, 8192.0, op.add)
-    ts(A("ib", 2, 4), A("ib", 0, 2), 10, op.arith_shift_right)
-    ts(col("cf", 24), ca, 256.0, op.mult, 4096.0, op.add)
-    tt(col("cf", 25), col("OH16", 4), col("OH16", 5), op.add)
-    ts(col("cf", 26), col("OH16", 4), -1.0, op.mult, 1.0, op.add)
-    ts(A("W0c", 0, 2), A("ib", 2, 4), 1.0, op.add)
-    send([((r - 1) % 4, T.W0c[:, 0:2], T.w0l[:, 0:2], "aw0", 0, 1)], whole("W0c", 0, 2))
-    ts(A("Kb"), A("K0"), col("cf", 24), op.add, col("OH16", 5), op.mult)
-    ts(A("pg"), Ind(nxw, A("L0")), col("cf", 26), op.mult)
-    ts(A("K0"), A("K0"), col("cf", 24), op.add, col("cf", 25), op.mult)
-    for m in range(3):
-        tt(A("pay", 256 * m + 256, 256 * m + 512), Ind(nxw, A("LN", 16 * m, 16 * m + 16)), A("Kb"), op.add)
-    tt(A("pay", 0, 256), A("pg"), A("K0"), op.add)
-    ms(A("Sz"), 0.0)
-    tt(hp("Dm", 128, 192, 65), hp("Dm", 0, 64, 65), hp("Dm", 64, 128, 65), op.add)
-    ts(A("junk"), A("junk"), ci, op.add)
-    tt(A("Sel5", 0, 3), A("OH32", 1, 14, 6), A("OH32", 19, 32, 6), op.add)
-    cp(col("Sel5", 3), col("OH16", 5))
-    cp(col("Sel5", 4), col("OH16", 4))
     places(0)
-    ms(A("XN", 4096, 4104), 0.0)
-    ts(col("cf", 27), c32, 4.0, op.mult, 3.0, op.add)
-    ts(A("OE"), A("XE"), ce16, op.is_equal)
-    ts(A("Yw32"), A("XI", 0, 132), col("cf", 27), op.is_equal)
-    ts(A("Yw"), A("XI", 0, 132), col("cf", 27), op.is_equal)
+
+    def payload(m):
+        tt(A("pay", 256 * m + 256, 256 * m + 512), Ind(nxw, A("LN", 16 * m, 16 * m + 16)), A("Kb"), op.add)
+    cp(A("Lx"), A("pN", 0, 128))
+    payload(0)
+    payload(1)
     I = A("i1", 0, 64)
     ts(I, A("pM", 0, 64), col("pM", 64), op.add, 2048.0, op.add)
+    cp(A("Lw"), A("pN", 128, 256))
     ts(A("i2", 0, 64), I, 4, op.arith_shift_right)
     ts(A("i3", 0, 64), I, 8, op.arith_shift_right)
     ts(A("f1", 0, 64), I, 1024.0, op.is_ge, 8192.0, op.mult)
@@ -676,14 +683,27 @@ def rank_program(g, core, T, topo):
     for q in range(4):
         mm(A("pC", 64 * q, 64 * q + 64), A("Rep", 128 * q, 128 * q + 128), A("Pq"), True, True, q == 3)
     act(A("Qw"), A("pC", 0, 256), fn.Copy)
-    ts(A("W0v", 0, 16), A("Cb", 0, 16), col("W0c", 1), op.add)
+    for q in range(4):
+        terms_gather(q)
+    payload(2)
     tt(A("f1", 0, 64), A("f3", 64, 128), A("junk"), op.min)
+    tt(A("pay", 0, 256), A("pg"), A("K0"), op.add)
     cp(A("Lsc"), A("f1", 0, 64))
     cp(Ind(A("sw"), A("Lsc")), A("pay"))
     mm(A("pY"), Zb, A("Wq", 0, 512), True, False, False)
     clear_tab()
     terms_sum(0)
-    terms_sum(1)
+
+    def miss_weight():
+        for e in range(2):
+            red(col("Hc", e), A("pA", 16 * e, 16 + 16 * e))
+        ts(A("ib", 0, 2), A("Hc", 0, 2), -1.0, op.mult, 8192.0, op.add)
+        ts(A("OE"), A("XE"), ce16, op.is_equal)
+        ts(A("ib", 2, 4), A("ib", 0, 2), 10, op.arith_shift_right)
+        ms(A("XN", 4096, 4104), 0.0)
+        ts(A("W0c", 0, 2), A("ib", 2, 4), 1.0, op.add)
+        send([((r - 1) % 4, T.W0c[:, 0:2], T.w0l[:, 0:2], "aw0", 0, 1)], whole("W0c", 0, 2))
+    fill.append(miss_weight)
     for c in range(16):
         mm(A("pM", c, 80, 16), A("sw", 128 * c, 128 * c + 128), A("Sel5", 0, 5), True, True, c == 15)
 
@@ -709,9 +729,9 @@ def rank_program(g, core, T, topo):
         cp(A("Tl"), A("pN", 0, 128))
         ts(A("LT"), A("pN", 0, 128), 1023.0, op.min)
         mm(A("pC", 0, 128), A("Tl"), A("Id", 0, 128), True, True)
+        terms_sum(1)
         terms_sum(2)
-        terms_sum(3)
-        ts(A("W0v", 16, 32), A("Cb", 0, 16), col("w0l", 0), op.add)
+        ts(A("W0v", 0, 16), A("Cb", 0, 16), col("W0c", 1), op.add)
         ts(A("f2"), A("Tl"), 1024.0, op.is_ge, 3072.0, op.mult)
         tt(A("Tx"), A("f2"), A("Tl"), op.add)
     gates(1, lambda: new_rows(1), mid1)
@@ -720,26 +740,26 @@ def rank_program(g, core, T, topo):
     km = row_keys(A("pC", 0, 128))
     km[0]()
     tt(A("uT", 128, 256), A("uT", 128, 256), A("f1"), op.add)
+    ts(A("W0v", 16, 32), A("Cb", 0, 16), col("w0l", 0), op.add)
+    terms_sum(3)
     tables(1, ["pM", "pN", "pF1", "pF0"])
-    new_x(range(5), ["pC", "pF1", "pF0", "pM", "pC"])
+    new_x(range(8), ["pC", "pF1", "pF0", "pM", "pC", "pN", "pF1", "pF0"])
     fill.extend(km[1:] + hot_m(64))
     draws(1)
     lists_after(1, A("Tx"), A("Tl"))
-    gap(3)
-    cp(A("Lx"), A("pN", 0, 128))
-    for q in range(4):
-        terms_gather(q)
     gap(100)
-    hot_n(1, lambda: None)
-    new_x(range(5, 8), ["pA", "pB", "pF1"])
-    for q in range(4):
-        terms_sum(q, q == 3)
-    counts(1)
+    def terms_list():
+        cp(A("Lx"), A("pN", 0, 128))
+        for q in range(4):
+            terms_gather(q)
+    count_cols(1, {EA[1] + 10: terms_list, EA[1] + 36: lambda: terms_sum(0), EA[1] + 56: lambda: terms_sum(1),
+                   EA[1] + 76: lambda: terms_sum(2)})
+    places(1)
+    terms_sum(3, True)
     act(A("Ye"), A("pY"), fn.Copy)
     send3("Ye", "yel", 128, "ae%d" % r)
     cp(A("tixf"), A("pN", 0, 128))
     cp(A("prf"), A("pN", 128, 256))
-    places(1)
     ts(A("Pq"), A("pM", 0, 64), col("pM", 64), op.add, 1024.0, op.is_lt)
     mm(A("pC", 0, 64), A("OE"), A("Pq"), True, True)
     red(col("Hc", 2), A("pC", 0, 64))

@@ -1,44 +1,53 @@
 from concourse.bass import DstId, RemoteDMATransfer
 from concourse.mybir import AluOpType, AxisListType, ActivationFunctionType
-import math
 
 F32, BF, F16, I32, U16 = "float32", "bfloat16", "float16", "int32", "uint16"
 SCRATCH = {
     "zs": ("dram", [4, 128, 512], BF), "zl": ("dram", [4, 128, 512], BF),
-    "nxs": ("dram", [4, 128, 96], I32), "nxl": ("dram", [4, 128, 96], I32),
+    "nxs": ("dram", [4, 128, 96], I32), "nxl": ("dram", [4, 128, 96], I32), "nxd": ("dram", [384, 128], I32),
+    "Xd": ("dram", [32, 3, 4, 256], F32),
 }
 for _n, _w, _d in [
-    ("zw0", 5120, BF), ("zw1", 4096, BF), ("nxw", 4096, I32), ("HU", 384, I32), ("HUh", 384, F16), ("HUs", 384, F16),
-    ("HUl", 384, F16), ("N0t", 16, I32), ("N0e", 128, F16), ("X0", 1024, F32), ("xo", 256, F16), ("xa", 256, F32), ("xb", 256, F32),
-    ("ip", 2, I32), ("ib", 8, I32), ("cf", 32, F32), ("XI", 224, BF), ("XD", 224, BF), ("XM", 160, BF), ("XE", 128, BF),
-    ("MA", 4, F32), ("MB", 8, F32), ("OH16", 16, F32), ("OH16b", 16, BF), ("OH32", 32, F32), ("GM", 8, F32),
-    ("M0", 8, F32), ("Wd", 896, BF), ("Dw", 144, BF), ("Wq", 544, BF), ("Rep", 512, BF), ("Rep4", 512, BF),
-    ("SelA", 32, BF), ("SelB", 32, BF), ("Sel5", 8, F32), ("Id", 512, BF), ("PL", 1280, BF), ("OE", 128, BF),
-    ("Yw", 132, BF), ("Yw32", 132, F32), ("Cb", 512, BF), ("tmpb", 128, BF), ("junk", 64, F32), ("ioi", 256, I32),
-    ("K0", 256, F32), ("Kb", 256, F32), ("L0", 16, U16), ("LN", 80, U16), ("R", 768, F16), ("d", 768, F16), ("ad", 768, F16),
-    ("ind", 768, BF), ("F", 1024, F32), ("G", 2048, F16), ("E", 4104, F32), ("XN", 4104, F32), ("V", 2048, F32),
-    ("pay", 1024, F32), ("pg", 256, F32), ("sw", 3072, F32), ("msk", 2048, BF), ("Qw", 256, F32), ("Ab", 8192, BF), ("Nb", 9216, BF),
-    ("LT", 128, U16), ("Llo", 128, U16), ("Lw", 128, U16), ("Lx", 128, U16), ("Ly", 128, U16), ("Lsc", 64, U16),
-    ("i1", 128, I32), ("i2", 128, I32), ("i3", 128, I32), ("i4", 128, I32), ("i5", 128, I32), ("i6", 128, I32),
-    ("baseN", 128, F32), ("bI", 128, I32), ("keyM", 128, BF), ("key", 128, BF), ("mT", 128, F16), ("uT", 256, F32), ("f1", 128, F32), ("f2", 128, F32),
-    ("f3", 128, F32), ("Tl", 128, F16), ("Tx", 128, F16), ("wb", 128, F16), ("P", 128, F32), ("c", 384, F16), ("pr", 128, F32),
-    ("tk", 128, F32), ("Xq", 576, F32), ("ka", 64, F32), ("Mk", 128, BF), ("Cs", 132, F32), ("Cd", 128, F32), ("Dm", 256, F32),
-    ("Sz", 136, BF), ("Pq", 64, F16), ("zb", 1024, BF), ("Vs", 128, F32), ("Sq", 512, BF),
-    ("Hc", 4, F32), ("W0c", 4, F32), ("w0l", 4, F32), ("W0v", 32, F32), ("tixf", 128, F32), ("prf", 128, F32),
-    ("Ye", 512, F32), ("Yx", 512, F32), ("yel", 512, F32), ("yxl", 512, F32),
+    ("zw0", 5120, BF), ("zw1", 4096, BF), ("nxw", 4096, I32), ("HU", 384, I32), ("Hh", 384, F16), ("Hs", 384, F16),
+    ("Hl", 384, F16), ("XS", 128, BF), ("XR", 128, BF),
+    ("N0t", 16, I32), ("X0", 256, F32), ("xs", 256, BF), ("xo", 256, F16), ("xo1", 256, F16), ("xa", 256, F32), ("xb", 256, F32),
+    ("ib", 10, I32), ("cf", 48, F32), ("XI", 176, BF), ("XD", 128, BF), ("XM", 144, BF),
+    ("MA", 4, F32), ("MQ", 4, F32), ("OH", 16, F32), ("GM", 8, F32), ("Wd", 704, BF), ("Dw", 144, BF), ("Wq", 576, BF),
+    ("Rep", 528, BF), ("Rep4", 512, BF), ("Sq", 512, BF), ("SelW", 32, BF), ("SelH", 32, BF), ("SelN", 32, BF), ("SelT", 8, BF),
+    ("Sel6", 8, F32), ("Id", 896, BF), ("Qw", 256, F32), ("msk", 2048, BF), ("Pm", 256, BF), ("Tri", 256, BF), ("OE", 128, BF), ("Yw", 132, BF), ("Yw32", 132, F32),
+    ("Cb", 512, BF), ("ch", 4, F16), ("nxb", 256, I32), ("nxh", 256, F16), ("XQ", 128, BF),
+    ("SN", 2048, BF), ("p16", 20, F32), ("K1", 256, F32), ("K", 1024, F32), ("J", 64, F32), ("LS", 16, U16),
+    ("LA", 64, U16), ("LN", 96, U16), ("R", 256, F16), ("Rm", 768, F16), ("d", 768, F16), ("ad0", 768, F16),
+    ("ind", 768, BF), ("F", 1032, F32), ("G", 2048, F16), ("E", 4104, F32), ("XN", 4104, F32), ("V", 2048, F32),
+    ("pg", 1024, F32), ("sw", 8192, F32), ("Ab", 8192, BF), ("Nb", 9216, BF),
+    ("LT", 128, U16), ("Lp", 128, U16), ("Lx", 128, U16), ("Ly", 128, U16), ("Lsc", 64, U16),
+    ("hi", 128, BF), ("aa", 128, BF), ("base", 128, BF), ("key", 128, BF), ("uT", 256, F32), ("f1", 128, F32),
+    ("Tl", 128, F16), ("Tx", 128, F16), ("S4", 128, F16), ("eb", 128, F16), ("ec", 128, F16), ("Vs", 128, F16),
+    ("P", 128, F16), ("t", 32, F32), ("cb", 512, BF), ("mb", 512, BF), ("tk", 384, F32),
+    ("Cs", 64, F32), ("Mk", 64, BF), ("nM", 64, F32), ("S", 64, BF),
+    ("Pq", 64, F16), ("Lv", 64, BF), ("zb", 1024, BF), ("Hc", 4, F32), ("W0b", 2, BF), ("W0c", 4, F32), ("w0l", 4, F32),
+    ("tixf", 128, F32), ("prf", 128, F32), ("Ye", 512, F32), ("Yx", 512, F32), ("yel", 512, F32), ("yxl", 512, F32),
 ]:
     SCRATCH[_n] = ("sbuf", [128, _w], _d)
-for _n in ["pY", "pF0", "pF1", "pA", "pB", "pC", "pM", "pN"]:
+for _n in ["pY", "pF0", "pF1", "pC"]:
     SCRATCH[_n] = ("psum", [128, 512], F32)
+for _n in ["pW", "pH", "pN", "pM"]:
+    SCRATCH[_n] = ("psum", [128, 4, 128], F32)
 
-SEMAPHORES = (["cv", "ca", "cp", "cg", "lsem", "dz", "dz2", "dn", "dh", "d0", "dx", "wn0", "wn1", "wz0", "wz1", "ahu", "aw0", "sto"]
+SEMAPHORES = (["cv", "ca", "cp", "cg", "lsem", "dz", "dz2", "dn", "dh", "d0", "dx", "du", "wn0", "wn1", "wn1a", "wn1b", "wz1a", "wz1b", "Xda", "Xdb", "Xd1", "wz0", "wz1", "ah", "aw0", "sto"]
               + ["%s%d" % (a, b) for a in ("an", "az", "ae", "ax") for b in range(4)])
-NA = (16, 13)
-LA = (0, 62)
-ND = (48, 94)
-EA = (50, 22)
-NF = (3, 3)
-MD = 21
+ROUND2 = 3.0 * 2 ** 23
+H0 = 160.0
+KT = 2 + 241 * H0
+NF = 4
+FAR = (0, 4, 4, 4)
+EARLY = 80
+ACOL = ((20, 20, 20, 14), (20, 20, 20, 0))
+FA = (64, 64)
+NV1 = 12
+HOT0, HOT1 = 8, 12
+XDMA = True
+NX1 = 5
 
 
 def rank_program(g, core, T, topo):
@@ -55,16 +64,22 @@ def rank_program(g, core, T, topo):
 
     def A(name, c0=0, c1=None, st=1, p0=0, p1=128):
         t = T[name]
+        if len(t.shape) == 3:
+            return (t[p0:p1], [(name, p0, p1, 0, 512, 1)])
         if c1 is None:
             c1 = t.shape[1]
         ap = t[p0:p1, c0:c1] if st == 1 else t[p0:p1, c0:c1:st]
         return (ap, [(name, p0, p1, c0, c1, st)])
 
-    def col(name, c):
-        return A(name, c, c + 1)
+    def B(name, k, c0=0, c1=128, st=1, p0=0, p1=128):
+        t = T[name]
+        if isinstance(k, tuple):
+            return (t[p0:p1, k[0]:k[1], c0:c1], [(name, p0, p1, 128 * k[0] + c0, 128 * (k[1] - 1) + c1, 1)])
+        ap = t[p0:p1, k, c0:c1] if st == 1 else t[p0:p1, k, c0:c1:st]
+        return (ap, [(name, p0, p1, 128 * k + c0, 128 * k + c1, st)])
 
-    def hp(n, c0, c1, p=64, st=1):
-        return A(n, c0, c1, st, 0, p)
+    def col(name, c, p0=0, p1=128):
+        return A(name, c, c + 1, 1, p0, p1)
 
     def Ind(win, off):
         return (win[0].indirect(off[0]), win[1] + off[1], win[1], off[1])
@@ -74,7 +89,62 @@ def rank_program(g, core, T, topo):
             Q[q].wait_ge(T.sem[sem], val)
             seen[q][sem] = val
 
+    pool = []
+    mode = {"hold": None, "each": False, "far": 0}
+
+    def meet(ra, rb):
+        for (n, p0, p1, c0, c1, st) in ra:
+            for (m, a0, a1, b0, b1, bs) in rb:
+                if n == m and a0 < p1 and p0 < a1 and b0 < c1 and c0 < b1 and not (bs == st and (c0 - b0) % st != 0):
+                    return True
+        return False
+
+    def clash(a, reads, writes):
+        return meet(a[2], reads) or meet(a[2], writes) or meet(a[1], writes)
+
+    def later(fs, front=False, tag=None):
+        for j, f in enumerate(fs):
+            mode["hold"] = []
+            f()
+            calls, mode["hold"] = mode["hold"], None
+            e = (calls, [x for c in calls for x in c[2]], [x for c in calls for x in c[3] if tag is None or x[0] != "pC"], tag)
+            pool.insert(j if front else len(pool), e)
+
+    def emit(j):
+        for c in pool.pop(j)[0]:
+            put(*c)
+
+    def force(reads, writes):
+        j = 0
+        while j < len(pool):
+            if clash(pool[j], reads, writes):
+                e = pool[j]
+                first = [i for i in range(j) if clash(pool[i], e[1], e[2])]
+                emit(first[0] if first else j)
+                j = 0
+            else:
+                j += 1
+
+    def gap(n=1, wait_ok=False):
+        while n > 0 and pool:
+            for j, e in enumerate(pool[:24]):
+                c = e[0][0]
+                need = needs("v", c[2], c[3])
+                free = all(seen["v"].get(s, 0) >= v or (s == "cv" and v <= cnt["v"] - NF) for s, v in need.items())
+                if free and not any(clash(pool[i], e[1], e[2]) for i in range(j)):
+                    break
+            else:
+                if not wait_ok:
+                    return
+                j = 0
+            emit(j)
+            n -= 1
+
     def deps(q, reads, writes, skip=None):
+        for sem, val in needs(q, reads, writes, skip).items():
+            wait(q, sem, val)
+
+    def needs(q, reads, writes, skip=None):
         need = {}
         for regs, w in ((reads, False), (writes, True)):
             for (n, p0, p1, c0, c1, st) in regs:
@@ -86,8 +156,7 @@ def rank_program(g, core, T, topo):
                     apart = bs == st and (c0 - b0) % st != 0
                     if (ps and rq != q) or ((w or rw) and a0 < p1 and p0 < a1 and b0 < c1 and c0 < b1 and not apart):
                         need[sem] = max(need.get(sem, 0), val)
-        for sem, val in need.items():
-            wait(q, sem, val)
+        return need
 
     def note(q, reads, writes, sem, val):
         for regs, w in ((reads, False), (writes, True)):
@@ -105,6 +174,19 @@ def rank_program(g, core, T, topo):
                 reads += x[3]
             else:
                 writes += x[1]
+        if mode["hold"] is not None:
+            mode["hold"].append((q, call, reads, writes, inc))
+            return
+        if q == "v" and mode["each"]:
+            pool.append(([(q, call, reads, writes, inc)], reads, writes, None))
+            return
+        force(reads, writes)
+        if q == "v":
+            need = {s: v for s, v in needs(q, reads, writes).items() if seen[q].get(s, 0) < v}
+            gap(max([NF - (cnt[q] - need["cv"]) if "cv" in need else 0] + [mode["far"] for s in need if s != "cv"]))
+        put(q, call, reads, writes, inc)
+
+    def put(q, call, reads, writes, inc):
         deps(q, reads, writes)
         ins_ = call()
         note(q, reads, writes, "c" + q, cnt[q] + 1)
@@ -133,6 +215,9 @@ def rank_program(g, core, T, topo):
     def red(out, a):
         issue("v", lambda: g.vector.tensor_reduce(out[0], a[0], AxisListType.X, op.add), [out], [a])
 
+    def scan(out, d0, d1, o0):
+        issue("v", lambda: g.vector.tensor_tensor_scan(out[0], d0[0], d1[0], 0.0, o0, op.add), [out], [d0, d1])
+
     def act(out, a, f, bias=None, scale=None):
         kw = {}
         if bias is not None:
@@ -154,6 +239,7 @@ def rank_program(g, core, T, topo):
         issue("g", lambda: g.affine_select(out[0], a[0], pat, o, fl, base, cm), [out], [a])
 
     def dma(q, out, in_, sem, n, wr=(), rd=()):
+        force(list(rd), list(wr))
         deps(q, list(rd), list(wr), sem)
         Q[q].dma_start(out, in_).then_inc(T.sem[sem], 16)
         total[sem] = 16 * n
@@ -170,6 +256,7 @@ def rank_program(g, core, T, topo):
         return [(n, 128 * s, 128 * s + 128, 0, 1, 1)]
 
     def send(items, rd):
+        force(rd, [])
         deps("g", rd, [])
         tr = []
         for (q, src, dst, sem, e0, ne) in items:
@@ -193,580 +280,609 @@ def rank_program(g, core, T, topo):
     split3 = [(0, NE // 2), (NE // 2, NE // 4), (3 * NE // 4, NE // 4)]
     eng3 = [NE // 2, NE // 4, NE // 4]
     engz = [NE // 2, NE // 2, NE]
+    EA = [(e, a) for a in range(4) for e in range(2)]
 
     def send3(src, dst, w, sem):
         send([(oth[j], T[src][:, w * oth[j]:w * oth[j] + w], T[dst][:, w * r:w * r + w], sem, split3[j][0], split3[j][1])
               for j in range(3)], whole(src))
 
-    fill = []
-
-    def gap(n=1):
-        for _ in range(n):
-            if fill:
-                fill.pop(0)()
-
     def run(L):
         for f in L:
             f()
 
-    dma("s", T.nxs[:], T.nx[:], "dn", 1, slot("nxs", 0))
-    for j in range(3):
-        dma("sa"[j % 2], T.zs[oth[j]], T.z[32 * oth[j]:32 * oth[j] + 32, :], "dz" if j < 2 else "dz2", 2 if j < 2 else 1, slot("zs", j // 2))
-    dma("a", T.HU[:, 0:128], T.hyp[:], "dh", 2, whole("HU"))
-    dma("a", T.HU[:, 128:384], T.uu[:], "dh", 2, whole("HU"))
-    dma("a", T.N0t[:], T.n0[2 * r:2 * r + 2, :], "d0", 1, whole("N0t"))
-    for a in range(4):
-        dma("sa"[a % 2], T.X0[32 * a:32 * a + 32, :], T.x0[32 * r:32 * r + 32, :], "dx", 4, whole("X0"))
+    if r < 2:
+        dma("s", T.nxd[:], T.nx[:], "dn", 1, slot("nxs", 0))
+    dma("a", T.HU[:, 0:128], T.hyp[:], "dh", 1, whole("HU", 0, 128))
+    if r < 2:
+        dma("s", T.zs[oth[0]:oth[0] + 2], T.z[32 * oth[0]:32 * oth[0] + 64, :], "dz", 1, slot("zs", 0))
+        dma("a", T.zs[oth[2]], T.z[32 * oth[2]:32 * oth[2] + 32, :], "dz2", 1, slot("zs", 1))
+    else:
+        dma("s", T.nxs[:], T.nx[:], "dn", 1, slot("nxs", 0))
+    dma("s", T.X0[:], T.x0[32 * r:32 * r + 32, :], "dx", 1, whole("X0"))
+    dma("a", T.HU[:, 128:384], T.uu[:], "du", 1, whole("HU", 128, 384))
+    dma("s", T.N0t[:], T.n0[2 * r:2 * r + 2, :], "d0", 1, whole("N0t"))
+    if r < 2:
+        dma("a", T.nxb[:, 128 * r:128 * r + 128], T.nx[6 * r:6 * r + 8, :], "wn0", 1, whole("nxb", 128 * r, 128 * r + 128))
+        dma("s", T.zb[:, 512 * r:512 * r + 512], T.z[32 * r:32 * r + 32, :], "wz0", 1, whole("zb", 512 * r, 512 * r + 512))
+    else:
+        dma("a", T.zs[:], T.z[:], "dz", 1, slot("zs", 0) + slot("zs", 1))
 
-    def zhop(s, qs):
-        t, b = s >> 1, s & 1
-        w = "zw%d" % t
-        for a in range(4):
-            src = T.z[32 * r:32 * r + 32, :] if s == r else T.zl[s]
-            dma(qs[a % len(qs)], T[w][32 * a:32 * a + 32, 2048 * b:2048 * b + 2048], src, "wz%d" % t, 8 if t else 4,
-                whole(w, 0, 4096) if t else whole(w, 2048 * b, 2048 * b + 2048), [] if s == r else slot("zl", s))
+    def double(w, p0, st, sem):
+        for j, n in enumerate((16, 32)):
+            for e in range(2):
+                p = 64 * e + p0
+                dma("s", T[w][p + n:64 * e + 2 * n:st, :], T[w][p:64 * e + n:st, :], sem + "ab"[j], 2, whole(w), whole(w))
 
-    zhop(r, "s")
+    def zhop():
+        for s in [x for x in [r] + frm if x >= 2]:
+            for e in range(2):
+                src = T.z[32 * r + 16 * e:32 * r + 16 * e + 16, :] if s == r else T.zl[s, 64 * e:64 * e + 64]
+                dma("s", T.zw1[64 * e:64 * e + 16, 2048 * (s & 1):2048 * (s & 1) + 2048], src, "wz1", 4, whole("zw1"),
+                    [] if s == r else slot("zl", s))
+        double("zw1", 0, 1, "wz1")
+
+    def nxhop():
+        for s in [x for x in [r] + frm if x >= 2]:
+            for e in range(2):
+                src = T.nx[6 * r + 3 * e:6 * r + 3 * e + 3, :] if s == r else T.nxl[s, 64 * e:64 * e + 64]
+                dma("s", T.nxw[64 * e + 1:64 * e + 13:4, 2048 * (s & 1):2048 * (s & 1) + 2048], src, "wn1", 4,
+                    whole("nxw"), [] if s == r else slot("nxl", s))
+        double("nxw", 1, 4, "wn1")
+
     for j, s in enumerate(frm):
-        landed(slot("nxl", s), "an%d" % s, eng3[j])
+        landed(slot("nxl", s) if s >= 2 else whole("nxb", 128 * s, 128 * s + 128), "an%d" % s, eng3[j])
         landed(slot("zl", s) if s >= 2 else whole("zb", 512 * s, 512 * s + 512), "az%d" % s, engz[j])
-        landed(whole("yel", 128 * s, 128 * s + 128), "ae%d" % s, eng3[j])
+        landed(whole("yel", 128 * s, 128 * s + 128), "ae%d" % s, NE)
         landed(whole("yxl", 128 * s, 128 * s + 128), "ax%d" % s, engz[j])
-        landed(whole("HUl", 96 * s, 96 * s + 96), "ahu", NE)
-    landed(whole("w0l"), "aw0", 1)
+        landed(whole("Hl", 96 * s, 96 * s + 96), "ah", NE)
+    landed(whole("w0l"), "aw0", NE)
 
-    ms(A("nxw", 0, 768), 0)
-    iota(col("ip", 0), [[0, 1]], 0, 1)
-    iota(A("XD"), [[1, 224]], 0, -1)
-    iota(A("ioi"), [[1, 256]], 0, 256)
-    iota(A("nxw", 3584, 4096), [[0, 512]], 0, 0)
-    P0 = col("ip", 0)
-    ts(col("ib", 0), P0, 5, op.arith_shift_right)
-    ts(col("ib", 1), P0, 15, op.bitwise_and)
-    ts(col("ib", 2), P0, 16, op.bitwise_and)
-    ts(col("ib", 3), P0, 31, op.bitwise_and)
-    ts(col("ib", 4), P0, 4, op.arith_shift_right)
-    ts(col("ib", 5), P0, 3, op.arith_shift_right, 6, op.bitwise_and)
-    ts(col("ib", 6), P0, 6, op.arith_shift_right)
-    ts(col("ib", 7), P0, 112, op.bitwise_and)
-    cp(col("cf", 28), P0)
-    cp(A("cf", 0, 8), A("ib"))
-    ts(A("XI"), A("XD"), col("cf", 28), op.add)
-    ca, ci, ce16, c32, cg = col("cf", 0), col("cf", 1), col("cf", 2), col("cf", 3), col("cf", 4)
-    tt(col("cf", 8), col("cf", 5), col("cf", 6), op.add)
-    ts(A("MA"), A("XI", 0, 4), ca, op.is_equal)
-    ts(A("OH16"), A("XI", 0, 16), ci, op.is_equal)
-    ts(A("MB"), A("XI", 0, 8), col("cf", 8), op.is_equal)
-    for q in oth + [r]:
-        ts(A("Wd", 224 * q, 224 * q + 224), A("XD"), float(96 - 32 * q), op.is_equal, col("MA", q), op.mult)
-    cp(A("HUh"), A("HU"))
-    ms(A("nxw", 768, 3584), 0)
-    for q in oth + [r]:
-        for kind in range(3):
-            for k in range(4):
-                mm(A("pM", 96 * q + kind, 96 * q + 96, 3), A("Wd", 224 * q + 96 - 32 * k, 224 * q + 224 - 32 * k),
-                   A("HUh", 128 * kind + 32 * k, 128 * kind + 32 * k + 32), k == 0, k == 3, k == 3 and kind == 2)
-    cp(A("HUs"), A("pM", 0, 384))
-    ts(A("OH16b"), A("XI", 0, 16), ci, op.is_equal)
-    for b in range(8):
-        ts(A("N0e", 16 * b, 16 * b + 16), A("N0t"), -2047.0, op.add, col("MB", b), op.mult)
-    mm(A("pN", 0, 16), A("N0e"), A("OH16b"), True, True)
     Zb, One, Neg, Qrt = [A("Cb", 128 * j, 128 * j + 128) for j in range(4)]
-    ts(A("OH32"), A("XI", 0, 32), c32, op.is_equal)
-    ts(col("cf", 9), col("cf", 7), 15.0, op.add)
-    ts(col("cf", 10), ce16, 8.0, op.add)
+    iota(col("ib", 8), [[0, 1]], 0, 1)
+    iota(A("XI"), [[1, 176]], 0, 0)
+    for e in range(2):
+        iota(A("XQ", 64 * e, 64 * e + 64), [[0, 4], [16, 4], [1000, 4]], 48 * e + 96 * r - min(96 * r, 256), 0)
+    iota(A("XS"), [[64, 2], [0, 4], [4, 16]], 0, 0)
+    iota(A("XD"), [[1, 128]], 0, -1)
+    iota(A("XR"), [[64, 2], [0, 4], [1, 16]], 0, 0)
+    mode["each"] = True
+    ms(One, 1.0)
     ms(Zb, 0.0)
-    tt(A("M0", 0, 3), A("OH32", 0, 13, 6), A("OH32", 18, 31, 6), op.add)
-    cp(col("M0", 3), col("OH16", 4))
-    ts(A("Dw"), A("XI", 0, 144), col("cf", 9), op.is_equal)
-    ts(A("M0", 4, 8), A("M0", 0, 4), -2047.0, op.mult)
-    ts(A("L0"), A("pN", 0, 16), 2047.0, op.add)
-    ts(A("ioi"), A("ioi"), 4095, op.bitwise_and)
-    cp(A("HUl", 96 * r, 96 * r + 96), A("HUs", 96 * r, 96 * r + 96))
-    ms(Neg, -2048.0)
-    ms(Qrt, 0.25)
+    ms(Neg, -1.0)
+    P0 = col("ib", 8)
+    ts(col("ib", 0), P0, 15, op.bitwise_and)
+    ts(col("ib", 1), P0, 5, op.arith_shift_right)
+    ts(col("ib", 2), P0, 16, op.bitwise_and)
+    ts(col("ib", 3), P0, 6, op.arith_shift_right)
+    ts(col("ib", 4), P0, 4, op.arith_shift_right, 3, op.bitwise_and)
+    ts(col("ib", 5), P0, 112, op.bitwise_and)
+    ts(col("ib", 6), P0, 63, op.bitwise_and)
+    ts(col("ib", 7), P0, 3, op.arith_shift_right, 4, op.bitwise_and)
+    cp(A("cf", 0, 8), A("ib", 0, 8))
+    ci, ce, ca = col("cf", 0), col("cf", 3), col("cf", 4)
+    cp(col("cf", 47), P0)
+    ts(col("cf", 8), col("cf", 2), 4.0, op.mult, ci, op.add)
+    ts(A("MQ"), A("XI", 0, 4), col("cf", 1), op.is_equal)
+    ts(col("cf", 9), col("cf", 8), 48.0, op.add)
+    ts(A("OH"), A("XI", 0, 16), ci, op.is_equal)
+    for q in oth + [r]:
+        ts(A("Wd", 176 * q, 176 * q + 176), A("XI"), col("cf", 9), op.is_equal, col("MQ", q), op.mult)
+    ts(A("p16", 0, 16), A("XI", 0, 16), -1.0, op.mult, col("cf", 47), op.add)
+    ms(A("Rep"), 0.0)
+    ms(A("XM", 0, 16), 99.0)
+    for j in range(16):
+        ts(A("SN", 128 * j, 128 * j + 128), A("XQ"), col("p16", j), op.is_equal)
+
+    for cq in range(4):
+        ts(A("Sq", 128 * cq, 128 * cq + 128), A("XS"), col("p16", cq), op.is_equal)
+    mode["each"] = False
+    gap(100, True)
+    for kind in range(3):
+        cp(A("Hh", kind, 384, 3), A("HU", 128 * kind, 128 * kind + 128))
+    for q in oth + [r]:
+        for k in range(4):
+            mm(A("pY", 96 * q, 96 * q + 96), A("Wd", 176 * q + 48 - 16 * k, 176 * q + 176 - 16 * k), A("Hh", 96 * k, 96 * k + 96), k == 0, k == 3)
+    cp(A("xs"), A("X0"))
+    cp(A("Hs"), A("pY", 0, 384))
 
     def send_z():
         dst = T.zl[r] if r >= 2 else T.zb[:, 512 * r:512 * r + 512]
         send([(oth[j], T.zs[oth[j]], dst, "az%d" % r, j * NE // 2, NE // 2) for j in range(2)], slot("zs", 0))
         send([(oth[2], T.zs[oth[2]], dst, "az%d" % r, 0, NE)], slot("zs", 1))
 
-    send([(oth[j], T.nxs[oth[j]], T.nxl[r], "an%d" % r, split3[j][0], split3[j][1]) for j in range(3)], slot("nxs", 0))
+    def send_nx():
+        send([(oth[j], T.nxs[oth[j]] if r >= 2 else T.nxd[min(96 * oth[j], 256):min(96 * oth[j], 256) + 128, :],
+               T.nxl[r] if r >= 2 else T.nxb[:, 128 * r:128 * r + 128], "an%d" % r, split3[j][0], split3[j][1]) for j in range(3)], slot("nxs", 0))
+    send_nx()
     if r < 2:
         send_z()
-    iota(A("XM"), [[0, 5], [1, 32]], 0, 0)
-    iota(One, [[0, 128]], 1, 0)
-    if r < 2:
-        send3("HUs", "HUl", 96, "ahu")
-    for cq in range(4):
-        asel(A("Sq", 128 * cq, 128 * cq + 128), One, [[0, 4], [-4, 32]], op.is_equal, -cq, 1)
+    iota(A("XM", 16, 144), [[1, 2], [0, 4], [100, 16]], 0, 0)
+    iota(A("K1"), [[1, 16], [16, 16]], 0, 0)
+    send3("Hs", "Hl", 96, "ah")
+    iota(A("nxw", 0, 2048), [[1, 2048]], 0, 0)
+    iota(A("nxw", 2048, 4096), [[1, 2048]], 2048, 0)
+    for j, c in enumerate((One, Neg)):
+        asel(A("Tri", 128 * j, 128 * j + 128), c, [[1, 128]], op.is_gt, 0, -1)
+    for j in range(2):
+        asel(A("Tri", 128 * j, 128 * j + 128), A("Tri", 128 * j, 128 * j + 128), [[-64, 2], [0, 64]], op.is_ge, 0, 1)
     if r >= 2:
-        send3("HUs", "HUl", 96, "ahu")
         deps("g", whole("zb"), [])
         send_z()
-    iota(A("K0"), [[1, 256]], 0, 0)
-    iota(A("junk"), [[16, 64]], 2048, 0)
+    iota(A("sw", 3072, 5120), [[0, 2048]], 0, 0)
+
+    def Id(j):
+        return A("Id", 128 * j, 128 * j + 128)
+
+    def rep(q, shift=0):
+        return A("Rep", 132 * q + 1 + shift, 132 * q + 129 + shift)
+
+    def half(b, u):
+        return B(b, (2 * u, 2 * u + 2)) if len(T[b].shape) == 3 else A(b, 256 * u, 256 * u + 256)
+
+    def zspread(s, qs, banks=("pW", "pH", "pN", "pY")):
+        def out(cq):
+            o = A("zw0", 2048 * s + 512 * cq, 2048 * s + 512 * cq + 512)
+            if qs[cq] == "a":
+                act(o, A(banks[cq]), fn.Copy)
+            else:
+                cp(o, A(banks[cq]))
+        for cq in range(4):
+            mm(A(banks[cq]), A("Sq", 128 * cq, 128 * cq + 128), A("zb", 512 * s, 512 * s + 512), True, True)
+        return [lambda cq=cq: out(cq) for cq in range(4)]
+    for cq in range(4):
+        mm(half("pF%d" % (cq >> 1), cq & 1), A("Sq", 128 * cq, 128 * cq + 128), A("xs"), True, True, cq & 1 == 1)
+    for h in range(2):
+        act(A("zw0", 4096 + 512 * h, 4608 + 512 * h), A("pF%d" % h), fn.Copy)
+
+    def nxspread(ss, qs):
+        banks = ["pW", "pH", "pN", "pY", "pF0", "pF1", "pC", "pM"]
+        for s in ss:
+            ts(A("nxh", 128 * s, 128 * s + 128), A("nxb", 128 * s, 128 * s + 128), -2047.0, op.add)
+        for n, (s, b) in enumerate([(s, b) for s in ss for b in range(4)]):
+            for j in range(4):
+                c = 128 * (4 * b + j)
+                o = B(banks[n], j) if len(T[banks[n]].shape) == 3 else A(banks[n], 128 * j, 128 * j + 128)
+                mm(o, A("SN", c, c + 128), A("nxh", 128 * s, 128 * s + 128), True, True, j == 3)
+            o = A("XN", 2048 * s + 512 * b, 2048 * s + 512 * b + 512)
+            if qs[n] == "a":
+                act(o, A(banks[n]), fn.Copy)
+            else:
+                cp(o, A(banks[n]))
+    if r < 2:
+        nxspread([r], "aaaa")
+        run(zspread(r, "aaaa"))
+    nxhop()
+    cp(A("Hl", 96 * r, 96 * r + 96), A("Hs", 96 * r, 96 * r + 96))
+    mode["each"] = True
+    ts(A("p16", 16, 20), A("XI", 0, 4), -16.0, op.mult, col("cf", 47), op.add)
+    ts(col("cf", 10), ca, 32.0, op.mult, ce, op.add)
+    ts(col("cf", 12), ca, 2.0, op.mult, ce, op.add)
+    ts(A("MA"), A("XI", 0, 4), ca, op.is_equal)
+    ts(col("cf", 11), ci, 2.0, op.mult, col("cf", 10), op.add)
+    for j, v in enumerate((1.0, 4.0, 64.0, 240.0, 1024.0, 0.25, -16.0)):
+        ts(Id(j), A("XD"), 0.0, op.is_equal, v, op.mult)
+    ts(A("Pm", 0, 128), A("XI", 0, 128), col("cf", 11), op.is_equal)
+    ts(A("Pm", 128, 256), A("XI", 0, 128), col("cf", 11), op.is_equal, 4.0, op.mult)
+    ts(A("GM"), A("XI", 0, 8), col("cf", 12), op.is_equal)
+    cp(A("LA", 0, 16), A("N0t"))
     for q in range(4):
-        asel(A("Rep", 128 * q, 128 * q + 128), One, [[0, 4], [-1, 32]], op.is_equal, -32 * q, 1)
-    o64, n64, t64 = hp("Cb", 128, 256), hp("Cb", 256, 384), hp("tmpb", 0, 128)
-
-    def pl(e, j):
-        return hp("PL", 640 * e + 128 * j, 640 * e + 128 * j + 128)
-    for e in range(2):
-        se = [-128 * (1 - 2 * e), 2]
-        asel(pl(e, 2), o64, [[-16, 4], se, [-1, 16]], op.is_equal, -128 * e, 1)
-        asel(pl(e, 4), n64, [[-16, 4], se, [-1, 16]], op.is_equal, -128 * e, 1)
-        asel(t64, o64, [[-16, 4], se, [-1, 16]], op.is_gt, -128 * e, 1)
-        asel(pl(e, 0), t64, [[16, 4], [0, 32]], op.is_gt, 16, -1)
-        asel(t64, o64, [[16, 4], se, [1, 16]], op.is_gt, -128 * e, -1)
-        asel(pl(e, 1), t64, [[-16, 4], [0, 32]], op.is_ge, 0, 1)
-        asel(pl(e, 3), o64, [[16, 4], se, [0, 16]], op.is_gt, -128 * e, -1)
-    iota(A("sw", 0, 2048), [[0, 2048]], 0, 0)
-    asel(A("E", 0, 1024), A("X0"), [[0, 1024]], op.is_equal, 1, 0, math.exp(-1.0))
-    iota(A("XE"), [[0, 4], [16, 2], [0, 16]], 0, 0)
+        ts(rep(q), A("XR"), col("p16", 16 + q), op.is_equal)
+    ts(col("cf", 13), col("cf", 6), 16.0, op.mult)
+    ts(col("cf", 14), col("cf", 5), 15.0, op.add)
+    ts(col("cf", 15), ca, 256.0, op.mult, 4096.0, op.add)
+    tt(col("cf", 16), col("OH", 13), col("OH", 14), op.add)
+    ts(A("LS"), A("XI", 0, 16), col("cf", 13), op.add)
+    ts(A("Dw"), A("XI", 0, 144), col("cf", 14), op.is_equal)
+    tt(col("cf", 17), col("cf", 15), col("cf", 16), op.mult)
+    tt(col("cf", 18), col("cf", 15), col("OH", 14), op.mult)
+    red(col("cf", 19), A("OH", 0, 12, 4))
+    red(col("cf", 20), A("OH", 1, 12, 4))
+    red(col("cf", 21), A("OH", 6, 16, 4))
     for q in range(4):
-        asel(A("Rep4", 128 * q, 128 * q + 128), Qrt, [[0, 4], [-1, 32]], op.is_equal, -32 * q, 1)
+        ts(A("Wq", 144 * q, 144 * q + 144), A("XM"), ce, op.is_equal, col("MA", q), op.mult)
+    ts(col("cf", 22), col("cf", 19), -2047.0, op.mult)
+    ts(col("cf", 23), col("cf", 21), -4.0, op.mult, col("OH", 3), op.add)
+    ts(col("cf", 27), col("cf", 20), -2047.0, op.mult)
+    tt(col("cf", 24), col("cf", 23), col("cf", 22), op.subtract)
+    ts(col("cf", 25), col("OH", 2), 2.0, op.mult, col("cf", 24), op.add)
+    cGa = col("cf", 22)
+    cEv = [col("cf", 25), col("cf", 26)]
 
-    act(A("zw0", 4096, 5120), A("X0"), fn.Copy)
-    for a in range(4):
-        act(A("xo", 0, 256, 1, 32 * a, 32 * a + 32), A("X0", 256 * a, 256 * a + 256, 1, 32 * a, 32 * a + 32), fn.Copy)
+    act(A("xo"), Ind(A("zw0", 4096, 5120), A("LS")), fn.Copy)
 
-    def nxhop(t, qs, n):
-        for s in [x for x in [r] + frm if x >> 1 == t]:
-            for a in range(4):
-                src = T.nx[6 * r:6 * r + 6, :] if s == r else T.nxl[s]
-                dma(qs[a % len(qs)], T.nxw[32 * a + t:32 * a + 32:6, 2048 * (s & 1):2048 * (s & 1) + 2048], src, "wn%d" % t, n,
-                    whole("nxw"), [] if s == r else slot("nxl", s))
-    nxhop(0, "sa", 8)
+    def fixed():
+        act(A("K", 0, 256), A("K1"), fn.Identity, col("cf", 17), col("cf", 16))
+        for m in range(1, 4):
+            act(A("K", 256 * m, 256 * m + 256), A("K1"), fn.Identity, col("cf", 18), col("OH", 14))
 
-    def zspread(j, cqs):
-        L = []
-        for s in [x for x in frm if x < 2][j:j + 1]:
-            for cq in cqs:
-                b = [["pY", "pA", "pB", "pC"], ["pM", "pY", "pA", "pB"]][j][cq]
-                mm(A(b), A("Sq", 128 * cq, 128 * cq + 128), A("zb", 512 * s, 512 * s + 512), True, True)
-                o = A("zw0", 2048 * s + 512 * cq, 2048 * s + 512 * cq + 512)
-                if (j == 0 and (r >= 2 or cq < 2)) or (j == 1 and cq == 3):
-                    act(o, A(b), fn.Copy)
-                else:
-                    L.append(lambda o=o, b=b: cp(o, A(b)))
+    def sels():
+        c = 28
+        L = [lambda: scan(A("cf", c, c + 4), A("Cb", 128, 132), A("OH", 2, 16, 4), op.mult),
+             lambda: tt(A("cf", c + 4, c + 8), A("cf", c, c + 4), A("OH", 2, 16, 4), op.subtract),
+             lambda: ts(A("cf", c + 4, c + 8), A("cf", c + 4, c + 8), col("MA", 0), op.mult),
+             lambda: tt(A("cf", c, c + 4), A("cf", c + 4, c + 8), A("OH", 2, 16, 4), op.add),
+             lambda: tt(col("cf", c + 8), col("OH", 8), col("OH", 4), op.subtract),
+             lambda: tt(col("cf", c + 9), col("OH", 4), col("OH", 0), op.subtract),
+             lambda: ts(col("cf", c + 10), col("OH", 3), 2048.0, op.mult, col("OH", 0), op.add),
+             lambda: ts(col("cf", c + 11), col("OH", 3), -2048.0, op.mult),
+             lambda: ms(A("SelN"), 0.0), lambda: ms(A("eb"), 1.0), lambda: ms(A("ec"), 1.0), lambda: ms(A("cb"), 0.0),
+             lambda: ms(A("S4"), 1.0), lambda: ms(A("S4", 0, 128, 4), 0.0)]
+        for s in range(4):
+            L.append(lambda s=s: ts(A("SelW", s, 32, 4), A("GM"), col("cf", c + s), op.mult))
+            L.append(lambda s=s: ts(A("SelH", s, 32, 4), A("GM"), col("cf", c + 8 + s), op.mult))
+            if s:
+                L.append(lambda s=s: ts(A("SelN", s, 32, 4), A("GM"), col("OH", 4 * s - 4), op.mult))
         return L
+    run(sels())
+    mode["each"] = False
 
-    ts(A("Id", 0, 128), A("XD", 0, 128), 0.0, op.is_equal)
-    for q in range(4):
-        ts(A("Wq", 136 * q, 136 * q + 136), A("XM", 0, 136), col("cf", 10), op.is_equal, col("MA", q), op.mult)
-    ts(col("cf", 11), ci, 3.0, op.is_lt, 2051.0, op.mult)
-    ts(col("cf", 13), ci, 3.0, op.is_lt, -2047.0, op.mult)
-    ts(A("GM"), A("XI", 0, 8), cg, op.is_equal)
-    ts(col("cf", 15), col("OH16", 6), 2048.0, op.mult)
-    tt(A("cf", 16, 18), A("OH16", 1, 3), A("OH16", 0, 2), op.subtract)
-    cp(A("cf", 21, 24), A("OH16", 3, 6))
-    ts(col("cf", 12), col("cf", 11), -4.0, op.add)
-    tt(col("cf", 14), col("cf", 13), col("OH16", 6), op.add)
-    ts(A("cf", 18, 21), A("OH16", 0, 3), col("cf", 15), op.add)
-    cEv, cGa = col("cf", 12), col("cf", 14)
-    sel = [lambda s=s, e=e: ts(A("SelA" if s < 4 else "SelB", 2 * (s % 4) + e, 32, 8), A("GM", e, 8, 2), col("cf", 16 + s), op.mult)
-           for s in range(8) for e in range(2)]
-    run(sel)
-    ts(col("cf", 24), ca, 256.0, op.mult, 4096.0, op.add)
-    tt(col("cf", 25), col("OH16", 4), col("OH16", 5), op.add)
-    ts(col("cf", 26), col("OH16", 4), -1.0, op.mult, 1.0, op.add)
-    ts(col("cf", 27), c32, 4.0, op.mult, 3.0, op.add)
-    ms(A("Sz"), 0.0)
+    def row_keys(src, off):
+        act(A("hi"), src, fn.Identity, H0 - (30 + off) / 64, 1.0 / 64)
+        act(A("aa"), src, fn.Identity, H0 - (510 + off) / 1024, 1.0 / 1024)
+        act(A("f1"), A("hi"), fn.Identity, 64 * H0 + 0.5 - off, -64.0)
+        return lambda: tt(A("base"), src, A("f1"), op.add)
 
-    def row_keys(src):
-        return [lambda: cp(A("i1"), src),
-                lambda: ts(A("bI"), A("i1"), 2, op.arith_shift_right, 60, op.bitwise_and),
-                lambda: ts(A("baseN"), A("bI"), 0.5, op.add),
-                lambda: ts(A("i2"), A("i1"), 4, op.arith_shift_right, 112, op.bitwise_and),
-                lambda: ts(A("i3"), A("i1"), 15, op.bitwise_and),
-                lambda: tt(A("keyM"), A("i2"), A("i3"), op.add)]
+    def turn(k, terms, first=None):
+        if first:
+            mm(B("pM", k), first[0], first[1], True, False)
+        for e in range(2):
+            for j, (name, c0, st, ident) in enumerate(terms):
+                last = j == len(terms) - 1
+                mm(B("pM", k, 0, 128, 1, 64 * e, 64 * e + 64), A(name, c0 + e * st // 2, T[name].shape[1], st), Id(ident),
+                   j == 0 and not first, last, last and e == 1)
 
-    def hot_m(n):
-        return [lambda v=v: ts(A("Ab", 128 * v, 128 * v + 128), A("keyM"), float(v), op.is_equal) for v in range(n)]
-    steps = [lambda v=v: act(A("Ab", 128 * v, 128 * v + 128), A("keyM"), fn.Sign, 0.5 - v) for v in range(MD, 64)]
+    def track_list(t):
+        turn(2, [("base", 0, 2, 1), ("hi", 0, 2, 0), ("aa", 0, 2, 3)])
+        s, c = (col("cf", 41), col("cf", 42)) if t else (1.0, -KT)
+        return lambda: (ts(A("LT"), B("pM", 2), s, op.mult, c, op.add), ts(A("Tl"), B("pM", 2), s, op.mult, c, op.add))
 
-    def gates(t, early, mid):
+    def hot(v0, v1):
+        return [lambda v=v: ts(A("Ab", 128 * v, 128 * v + 128), A("hi"), H0 + v, op.is_equal) for v in range(v0, v1)]
+
+    def clear(bank, n=512, stop=False):
+        mm(A(bank, 0, n), Zb, A("Wq", 0, n), True, stop, False)
+
+    def tab(lhs, src, last, first=False):
+        for q in range(4):
+            mm(A("pF%d" % (q >> 1), 256 * (q & 1), 256 * (q & 1) + 256), lhs(q), src, first and (q & 1) == 0, last and (q & 1) == 1)
+
+    def gates(t, lst, xo, pause=None, pause2=None):
         zw = A("zw%d" % t, 0, 4096)
 
-        def tab(f, src, m, last):
-            for q in range(4):
-                mm(A("pF%d" % (q >> 1), 256 * (q & 1), 256 * (q & 1) + 256), A("Wq", 136 * q + 8 - f, 136 * q + 136 - f),
-                   A(src, 256 * m, 256 * m + 256), False, last and (q & 1) == 1)
-        for m in range(3):
-            tab(m, "R", m, False)
-        early()
-        for m in range(3):
+        def near(m):
             s = (256 * m, 256 * m + 256)
-            tt(A("d", *s), Ind(zw, A("LN", 16 * m, 16 * m + 16)), A("xo"), op.subtract)
-            act(A("ad", *s), A("d", *s), fn.Abs)
-            if m > 0:
-                ts(A("ind", s[0] - 256, s[0]), A("ad", s[0] - 256, s[0]), 1.0, op.is_le)
-                tab(2 + m, "ind", m - 1, False)
-        gap(3)
-        ts(A("ind", 512, 768), A("ad", 512, 768), 1.0, op.is_le)
-        tab(5, "ind", 2, True)
-        mid()
+            ts(A("ind", *s), A("d", *s), ROUND2, op.add, ROUND2, op.is_equal)
+            f = 6 + 4 * m
+            tab(lambda q: A("Wq", 144 * q + 16 - f, 144 * q + 144 - f), A("ind", *s), m == 2)
+        for m in range(3):
+            tt(A("d", 256 * m, 256 * m + 256), Ind(zw, lst(m)), xo, op.subtract)
+            if m:
+                near(m - 1)
+            elif pause:
+                pause()
+        if pause2:
+            pause2()
+        near(2)
 
-    def clear_tab():
-        for b in range(2):
-            mm(A("pF%d" % b), Zb, A("Wq", 0, 512), True, False, False)
-
-    def fields(pause=None):
-        act(A("F", 0, 512), A("pF0"), fn.Relu, cEv)
-        ts(A("F", 512, 1024), A("pF1"), cEv, op.add, 0.0, op.max)
+    def fields(t, pause=None, pause2=None):
+        act(A("F", 0, 512), A("pF0"), fn.Relu, cEv[t])
+        ts(A("F", 512, 1024), A("pF1"), cEv[t], op.add, 0.0, op.max)
         if pause:
             pause()
-        act(A("G", 0, 1024), Ind(A("F"), A("LT", 0, 64)), fn.Identity, cGa)
-        ts(A("G", 1024, 2048), Ind(A("F"), A("LT", 64, 128)), cGa, op.add)
-        for n, s in (("pB", "SelB"), ("pA", "SelA")):
+        n = FA[t]
+        act(A("G", 0, 16 * n), Ind(A("F"), A("LT", 0, n)), fn.Identity, cGa)
+        ts(A("G", 16 * n, 2048), Ind(A("F"), A("LT", n, 128)), cGa, op.add)
+        if pause2:
+            pause2()
+        for n, s in (("pW", "SelW"), ("pH", "SelH"), ("pN", "SelN")):
             for i in range(16):
-                mm(A(n, i, 512, 16), A("G", i, 2048, 16), A(s), True, True, i == 15)
+                mm(B(n, (0, 4), 8 * i, 8 * i + 8), A("G", i, 2048, 16), A(s), True, True, i == 15)
 
-    def tables(t, banks, later=None):
-        j = 0
+    def exp_table(ad, j, b):
+        m, h = j >> 1, j & 1
+        for u in range(2):
+            mm(half(b, u), rep(2 * h + u), A(ad, 256 * m, 256 * m + 256), True, True, u == 1)
+        o = 1024 * (m + 1) + 512 * h
+        act(A("E", o, o + 512), A(b), fn.Exp, None, -1.0)
+
+    def repeat(src, w, d, dst, c0):
+        for e in range(2):
+            for a in range(4):
+                p = 64 * e + 16 * a
+                dma("s", T[d][16 * e:16 * e + 16, :, a, :], T[src][p:p + 16, 0:w], d + "ab"[e], 4, slot(d, e), whole(src, 0, w))
+        for e in range(2):
+            for k in range(4):
+                p = 64 * e + 16 * k
+                dma("s", T[dst][p:p + 16, c0:c0 + 4 * w], T[d][16 * e:16 * e + 16], d + "1", 8, whole(dst, c0, c0 + 4 * w), slot(d, e))
+
+    def new_x():
         for m in range(3):
-            for h in range(2):
-                b = banks[j % len(banks)]
-                j += 1
-                for u in range(2):
-                    q = 2 * h + u
-                    mm(A(b, 256 * u, 256 * u + 256), A("Rep", 128 * q, 128 * q + 128), A("ad", 256 * m, 256 * m + 256), True, True, u == 1)
-                o = 1024 * (m + 1) + 512 * h
-                if later is None:
-                    act(A("E", o, o + 512), A(b), fn.Exp, None, -1.0)
-                else:
-                    later.append(lambda o=o, b=b: act(A("E", o, o + 512), A(b), fn.Exp, None, -1.0))
+            o = half(["pY", "pF0"][m >> 1], m & 1)
+            mm(o, Id(0), A("xo1"), True, False)
+            mm(o, Id(5), A("d", 256 * m, 256 * m + 256), False, True)
+        if XDMA:
+            act(A("pg", 0, 512), A("pY"), fn.Copy)
+            act(A("pg", 512, 768), half("pF0", 0), fn.Copy)
+            repeat("pg", 768, "Xd", "XN", 1024)
 
-    def new_x(js, banks):
-        for j, b in zip(js, banks):
-            m, h = j >> 1, j & 1
-            for u in range(2):
-                q = 2 * h + u
-                mm(A(b, 256 * u, 256 * u + 256), A("Rep", 128 * q, 128 * q + 128), A("xo"), True, m == 0, m == 0 and u == 1)
-                if m:
-                    mm(A(b, 256 * u, 256 * u + 256), A("Rep4", 128 * q, 128 * q + 128), A("d", 256 * m - 256, 256 * m), False, True, u == 1)
-            act(A("XN", 512 * j, 512 * j + 512), A(b), fn.Copy)
+    def x_table(j, b):
+        m, h = j >> 1, j & 1
+        for u in range(2):
+            q = 2 * h + u
+            mm(half(b, u), rep(q), A("xo1"), True, m == 0, m == 0 and u == 1)
+            if m:
+                mm(half(b, u), A("Rep4", 128 * q, 128 * q + 128), A("d", 256 * m - 256, 256 * m), False, True, u == 1)
+        act(A("XN", 512 * j, 512 * j + 512), A(b), fn.Copy)
 
-    def draws(t):
-        def N(k, f):
-            return A("pA", 128 * k + 64 + 32 * f, 128 * k + 96 + 32 * f) if f < 2 else A("pB", 128 * k, 128 * k + 32)
-
-        def excl(j, k):
-            x = 96 * {(0, 1): 0, (0, 2): 1, (0, 3): 2, (1, 2): 3, (1, 3): 4, (2, 3): 5}[(j, k)]
-            Vk = A("pB", 128 * k + 32, 128 * k + 128)
-            L = [lambda f=f: tt(A("Xq", x + 32 * f, x + 32 * f + 32), N(k, f), A("tk", 32 * j, 32 * j + 32), op.not_equal) for f in (2, 0, 1)]
-            L.append(lambda: tt(Vk, Vk, A("Xq", x, x + 96), op.mult))
-            return L
-        own = []
-
-        def g1():
-            if own:
-                own.pop(0)()
-                gap(NF[t] - 1)
-            else:
-                gap(NF[t])
-        for k in range(4):
-            def V(m):
-                return A("pB", 32 * m, 32 * m + 32) if k == 0 else A("Vs", 32 * m - 32, 32 * m)
-
-            def Pm(m):
-                return A("P", 32 * m, 32 * m + 32)
-
-            def C(s, n=1):
-                return A("c", 96 * k + 32 * s, 96 * k + 32 * (s + n))
-            if t == 0:
-                ts(Pm(1), V(1), 2.0, op.add)
-            else:
-                tt(Pm(1), V(1), A("W0v"), op.add)
-            if k:
-                tt(A("Vs", 96, 128), V(2), V(3), op.add)
-            g1()
-            if k:
-                tt(Pm(3), A("Vs", 96, 128), Pm(1), op.add)
-            tt(Pm(2), V(2), Pm(1), op.add)
-            g1()
-            if k == 0:
-                tt(Pm(3), V(3), Pm(2), op.add)
-                g1()
-            tt(Pm(0), Pm(3), A("uT", 128 * t + 32 * k, 128 * t + 32 * k + 32), op.mult)
-            g1()
-            if t == 0:
-                ts(C(2), Pm(0), 2.0, op.is_ge)
-            else:
-                tt(C(2), Pm(0), A("W0v"), op.is_ge)
-            tt(C(0), Pm(0), Pm(1), op.is_ge)
-            tt(C(1), Pm(0), Pm(2), op.is_ge)
-            kk = [lambda k=k, C=C: tt(A("ka", 0, 32), C(2), A("baseN", 32 * k, 32 * k + 32), op.add),
-                  lambda C=C: tt(A("ka", 32, 64), C(0), C(1), op.add),
-                  lambda k=k: tt(A("key", 32 * k, 32 * k + 32), A("ka", 0, 32), A("ka", 32, 64), op.add)]
-            if k == 3:
-                kk[0]()
-                kk[1]()
-                gap()
-                kk[2]()
-                break
-            kk[0]()
-            tt(A("pr", 0, 96), A("pA", 128 * k, 128 * k + 96), C(0, 3), op.mult)
-            kk[1]()
-            g1()
-            tt(A("pr", 96, 128), A("pr", 0, 32), A("pr", 32, 64), op.add)
-            for f in range(3):
-                tt(A("Xq", 480 + 32 * f, 512 + 32 * f), N(k + 1, f), A("pr", 64, 96), op.subtract)
-            kk[2]()
-            while own:
-                own.pop(0)()
-            for f in range(3):
-                tt(A("Xq", 32 * f, 32 * f + 32), A("Xq", 480 + 32 * f, 512 + 32 * f), A("pr", 96, 128), op.not_equal)
-            if k < 2:
-                tt(A("tk", 32 * k, 32 * k + 32), A("pr", 96, 128), A("pr", 64, 96), op.add)
-            gap(NF[t])
-            tt(A("Vs", 0, 96), A("pB", 128 * k + 160, 128 * k + 256), A("Xq", 0, 96), op.mult)
-            for k2 in range(k + 2, 4):
-                own.extend(excl(k, k2))
-            g1()
-
-    def lists_after(t, Tx, T4):
-        tt(A("mT"), A("key"), A("baseN"), op.subtract)
-        mm(A("pN", 0, 128), A("mT"), A("Id", 128, 256), True, False)
-        mm(A("pN", 0, 128), A("Id", 0, 128), Tx, False, True, False)
-        if t == 0:
-            mm(A("pN", 128, 256), A("mT"), A("Id", 256, 384), True, False)
-            mm(A("pN", 128, 256), A("Id", 0, 128), A("wb"), False, True)
+    def steps(q, c):
+        o = A("Nb", 72 * c, 72 * c + 65)
+        if q == "a":
+            act(o, A("XI", 0, 65), fn.Sign, col("key", c), -1.0)
         else:
-            mm(A("pN", 128, 256), A("mT"), A("Id", 0, 128), True, False)
-            mm(A("pN", 128, 256), A("Id", 384, 512), T4, False, True)
+            ts(o, A("XI", 0, 65), col("key", c), op.is_le, 2.0, op.mult)
 
-    def count_cols(t, between):
-        nd, early = ND[t], EA[t]
-        ca_, cv_ = list(range(128 - nd)), list(range(128 - nd, 128))
-        order = ca_[:early]
-        ra = ca_[early:]
-        j = 0
-        for n, c in enumerate(cv_):
-            order.append(c)
-            while j < len(ra) and j * (len(cv_) - LA[t]) <= (n - LA[t]) * len(ra):
-                order.append(ra[j])
-                j += 1
-        order += ra[j:]
-        first = [[c for c in order if (c >> 4) & 1 == e][0] for e in range(2)]
-        last = [[c for c in order if (c >> 4) & 1 == e][-1] for e in range(2)]
-        for n, c in enumerate(order):
-            o = A("Nb", 72 * c, 72 * c + 65)
-            if c < 128 - nd:
-                act(o, A("XI", 0, 65), fn.Sign, col("key", c), -1.0)
-            else:
-                ts(o, A("XI", 0, 65), col("key", c), op.is_le, 2.0, op.mult)
+    def count(c, last=False):
+        e = c & 1
+        o, a, b = A("pC", 0, 65, 1, 64 * e, 64 * e + 64), A("Ab", c, 8192, 128), A("Nb", 72 * c, 72 * c + 65)
+        issue("p", lambda: g.tensor.matmul(o[0], a[0], b[0], fresh.pop(e, False), last), [o], [a, b], last)
+    fresh = {0: True, 1: True}
+
+    def draws(t, after):
+        def differ(o, j, k):
+            return [lambda f=f: tt(A(o, f, 128, 4), B("pN", k, f, 128, 4), A("tk", 128 * j + 3, 128 * j + 128, 4), op.not_equal) for f in (1, 2, 3)]
+        for k in range(4):
+            def Pm(m):
+                return B("pW", 0, m, 128, 4) if k == 0 else A("P", m, 128, 4)
+            if k:
+                own = []
+                for k2 in range(k + 1, 4):
+                    own.extend(differ("ec", k - 1, k2) + [lambda k2=k2: tt(B("pW", k2), B("pW", k2), A("ec"), op.mult)])
+                run(differ("eb", k - 1, k))
+                key(k - 1)
+                after(k - 1)
+                later(own, True)
+                tt(A("Vs"), B("pW", k), A("eb"), op.mult)
+                scan(A("P"), A("S4"), A("Vs"), op.mult)
+            tt(A("t"), Pm(3), A("uT", 128 * t + 32 * k, 128 * t + 32 * k + 32), op.mult)
+            for m in range(3):
+                tt(A("cb", 128 * k + 3 - m, 128 * k + 128, 4), A("t"), Pm(m), op.is_ge)
+            ck = A("cb", 128 * k, 128 * k + 128)
+            if k < 3:
+                scan(A("tk", 128 * k, 128 * k + 128), ck, B("pH", k), op.mult)
+            scan(A("mb", 128 * k, 128 * k + 128), A("S4"), ck, op.mult)
+        key(3)
+
+    def key(k):
+        tt(A("key", 32 * k, 32 * k + 32), A("mb", 128 * k + 3, 128 * k + 128, 4), A("base", 32 * k, 32 * k + 32), op.add)
+
+    def row_lists(Tx, up):
+        turn(1, [("key", 0, 2, 0), (up, 0, 2, 2)])
+        turn(0, [("mb", 3, 8, 4)], (Id(0), Tx))
+
+    def count_tail(cv_, ca_, between):
+        order = []
+        while cv_ or ca_:
+            for q, L in (("v", cv_), ("a", ca_)):
+                if L:
+                    order.append((q, L.pop(0)))
+        ends = [[c for (q, c) in order if c & 1 == e][-1] for e in range(2)]
+        for n, (q, c) in enumerate(order):
+            steps(q, c)
             if n in between:
                 between[n]()
-            e = (c >> 4) & 1
-            mm(hp(["pC", "pM"][e], 0, 65), A("Ab", c, 8192, 128), o, c == first[e], c == last[e])
+            count(c, c in ends)
 
-    def hot_n(t, between):
-        nd = 64 - NA[t]
-        for v in range(nd, 64):
-            act(A("Nb", 128 * v, 128 * v + 128), A("key"), fn.Sign, 0.5 - v)
-        for v in range(nd):
-            ts(A("Nb", 128 * v, 128 * v + 128), A("key"), float(v), op.is_equal)
-            if v == 10:
-                between()
-
-    def counts(t):
-        nn = 65 if NA[t] else 64
-        nm = 65 - t
-        for e in range(2):
-            cols = [32 * k + 16 * e + i for k in range(4) for i in range(16)]
-            for j, c in enumerate(cols):
-                mm(hp("pC", 65 * e, 65 * e + nn, nm), A("Ab", c, 128 * nm, 128), A("Nb", c, 128 * nn, 128), j == 0, j == 63, j == 63 and e == 1)
-
-    def places(t):
-        for e in range(2):
-            cp(hp("Cs", 64 * e, 64 * e + 64), hp(["pC", "pM"][e], 1, 65))
-        for e in range(2):
-            tt(hp("Mk", 64 * e, 64 * e + 64), hp(["pC", "pM"][e], 0, 64), hp("Cs", 64 * e, 64 * e + 64), op.is_gt)
-        for e in range(2):
-            o, d0, d1 = hp("Sz", 68 * e + 4, 68 * e + 68), hp("Mk", 64 * e, 64 * e + 64), hp("Cb", 0, 64)
-            issue("v", lambda: g.vector.tensor_tensor_scan(o[0], d0[0], d1[0], 0.0, op.add, op.add), [o], [d0, d1])
-        for e in range(2):
-            mm(A("pM", 64, 65), pl(e, 3), hp("Sz", 68 * e + 67, 68 * e + 68), e == 0, e == 1, False)
-        for m in range(4):
-            L = []
-            for e in range(2):
-                L.append((pl(e, 0), hp("Sz", 68 * e + 3, 68 * e + 64, 64, 4)))
-                L.append((pl(e, 1), hp("Sz", 68 * e + 7, 68 * e + 68, 64, 4)))
-                L.append((pl(e, 2), hp("Sz", 68 * e + 3 + m, 68 * e + 64 + m, 64, 4)))
-                if t == 0:
-                    L.append((pl(e, 4), hp("Mk", 64 * e + m, 64 * e + 64, 64, 4)))
-            for j, (a_, b_) in enumerate(L):
-                mm(A("pM", 16 * m, 16 * m + 16), a_, b_, j == 0, j == len(L) - 1, j == len(L) - 1 and m == 3)
+    def marks(t, pause=None):
+        cp(A("Cs"), A("pC", 1, 65))
+        tt(A("Mk"), A("pC", 0, 64), A("Cs"), op.is_gt)
+        if t == 0:
+            tt(A("nM"), A("pC", 0, 64), A("Cs"), op.is_le)
+        scan(A("S"), A("Mk"), A("Cb", 0, 64), op.add)
+        if t == 0:
+            mm(col("pC", 128), A("Tri", 0, 128), col("S", 63), True, True, False)
+            mm(col("pC", 129), A("Tri", 0, 128), col("S", 63), True, False)
+            mm(col("pC", 129), Id(4), col("ch", 1), False, False)
+            mm(col("pC", 129), Id(0), col("ch", 2), False, True)
+        else:
+            mm(col("pC", 129), A("Tri", 128, 256), col("S", 63), True, False)
+            mm(col("pC", 129), Id(0), col("ch", 0), False, True)
+        if pause:
+            pause()
 
     def terms_gather(q):
         act(A("V", 512 * q, 512 * q + 512), Ind(A("E"), A("Lx", 32 * q, 32 * q + 32)), fn.Copy)
 
-    def terms_sum(q, last=False):
+    def terms_sum(q, last=False, first=False, out=None):
         for u in range(4):
-            mm(A("pY", 128 * q, 128 * q + 128), A("Yw32", 3 - u, 131 - u), A("V", 512 * q + 128 * u, 512 * q + 128 * u + 128),
-               False, last and u == 3, u == 3)
+            mm(out or A("pY", 128 * q, 128 * q + 128), A("Yw32", 3 - u, 131 - u), A("V", 512 * q + 128 * u, 512 * q + 128 * u + 128),
+               first and u == 0, last and u == 3, u == 3)
 
     nxw = A("nxw")
-    Tl0 = A("HUl", 0, 384, 3)
-    clear_tab()
-    zev = zspread(0, range(4)) + zspread(1, (0, 1))
-    for m in range(3):
-        ts(A("R", 256 * m, 256 * m + 256), Ind(nxw, A("L0")), -2047.0, op.add, col("M0", m), op.mult)
+    T4 = B("pM", (0, 4), 0, 32)
+    gap(EARLY, True)
+    later([lambda q=q: ts(A("Rep4", 128 * q, 128 * q + 128), A("XR"), col("p16", 16 + q), op.is_equal, 0.25, op.mult) for q in range(4)])
+    later([lambda: ts(col("cf", 40), col("cf", 6), -64.0, op.mult, 4096.0, op.add),
+                 lambda: ts(col("cf", 41), ce, 2.0, op.mult, -1.0, op.add),
+                 lambda: ts(col("cf", 42), ce, -1023 - 2 * KT, op.mult, 1023 + KT, op.add),
+                 lambda: ts(A("J"), A("XI", 0, 64), -1.0, op.mult, col("cf", 40), op.add),
+                 lambda: ms(col("ch", 0), 1025.0), lambda: ms(A("F", 1024, 1032), 1.0),
+                 lambda: ts(col("ch", 1), ce, 8.0, op.mult, -4.0, op.add), lambda: ts(col("ch", 2), ce, -1.0, op.mult),
+                 lambda: cp(A("Sel6", 0, 3), A("OH", 1, 12, 4)),
+                 lambda: cp(col("Sel6", 3), col("OH", 14)), lambda: cp(col("Sel6", 4), col("OH", 13)), lambda: cp(col("Sel6", 5), col("OH", 12)),
+                 lambda: ts(col("cf", 45), ce, 64.0, op.mult, 3.0, op.add),
+                 lambda: ts(A("SelT"), A("GM"), 4.0, op.mult),
+                 lambda: ts(col("cf", 46), ci, 4.0, op.mult, col("cf", 45), op.add),
+                 lambda: ms(A("E", 4096, 4104), 0.0), lambda: ms(A("XN", 4096, 4104), 0.0), lambda: ms(A("OE"), 0.0),
+                 lambda: ts(A("Yw32"), A("XI", 0, 132), col("cf", 46), op.is_equal),
+                 lambda: ts(A("Yw"), A("XI", 0, 132), col("cf", 46), op.is_equal),
+                 lambda: ms(A("OE", 0, 64, 1, 0, 64), 1.0), lambda: ms(A("OE", 64, 128, 1, 64, 128), 1.0)])
+    def misses():
+        act(A("E", 0, 1024), A("zw0", 4096, 5120), fn.Exp, -1.0, 0.0)
+        fixed()
+    if r >= 2:
+        misses()
+    mode["far"] = FAR[0]
+    far = [x for x in frm if x < 2]
+    nxspread(far, "avavavav")
+    names = A("XN", 0, 4096)
+    zs_ = zspread(far[0], "avav", ("pW", "pH", "pN", "pY") if r >= 2 else ("pF0", "pF1", "pM", "pW"))
+    for m in range(2):
+        ts(A("Rm", 256 * m, 256 * m + 256), Ind(names, A("LA", 0, 16)), col("OH", 4 * m), op.mult)
+    act(A("Rm", 512, 768), Ind(names, A("LA", 0, 16)), fn.Copy, None, col("OH", 8))
     for i in range(16):
-        mm(A("pN", 0, 48), A("Dw", 15 - i, 143 - i), A("R", i, 768, 16), i == 0, i == 15)
-    dma("s", T.nxw[4:128:16, :], T.ioi[:], "wn1", 9, whole("nxw"), whole("ioi"))
-    nxhop(1, "s", 9)
-    for s in (2, 3):
-        if s != r:
-            zhop(s, "s")
-    zev += zspread(1, (2, 3))
-    run(zev[:1])
-    ts(A("LN", 0, 48), A("pN", 0, 48), 2047.0, op.add)
-    run(zev[1:])
+        mm(A("pC", 0, 48), A("Dw", 15 - i, 143 - i), A("Rm", i, 768, 16), i == 0, i == 15)
+    zhop()
+    run(zs_[:2])
+    z2 = zspread(far[1], "avav", ("pF0", "pF1", "pM", "pW")) if r >= 2 else []
+    ts(A("LA", 16, 64), A("pC", 0, 48), 2047.0, op.add)
+    run(zs_[2:] + z2)
+    mode["far"] = FAR[1]
+    mm(T4, A("Hl", 0, 384, 3), A("Pm", 128, 256), True, True)
+    act(A("R"), Ind(names, A("LA", 0, 16)), fn.Copy)
+    keys = row_keys(T4, 0.0)
+    if r < 2:
+        misses()
+    tab(rep, A("R"), False, True)
+    ev = []
+    gates(0, lambda m: A("LA", 16 * m + 16, 16 * m + 32), A("xo"),
+          lambda: (keys(), later(hot(0, 64)), ev.append(track_list(0)), turn(1, [("hi", 0, 2, 0), ("aa", 0, 2, 6)])), lambda: run(ev))
+    for t in range(2):
+        mm(A("pC", 128 * t, 128 * t + 128), A("Hl", 1 + t, 384, 3), A("Pm", 0, 128), True, True, t == 1)
+    ts(A("Ly"), B("pM", 1), 15 * H0, op.add)
+    gap(HOT0)
+    mode["far"] = FAR[2]
+    fields(0)
+    act(A("ad0"), A("d"), fn.Abs)
+    ts(A("uT"), A("pC", 0, 256), 1.0 / 64, op.mult)
+    act(A("msk"), Ind(A("OH"), A("Ly")), fn.Copy)
+    gap(HOT1)
+    held = []
 
-    def early0():
-        for kind in range(3):
-            mm(A("pC", 128 * kind, 128 * kind + 128), A("HUl", kind, 384, 3), A("Id", 0, 128), True, True, kind == 2)
+    def after(t):
+        def f(k):
+            n = ACOL[t][k]
+            for c in range(32 * k, 32 * k + n):
+                steps("a", c)
+                held.append(c)
+            if not any(x[0] == "Ab" for e in pool for x in e[2]):
+                while held:
+                    count(held.pop(0))
+            for c in range(32 * k + n, 32 * k + 32):
+                later([lambda: (steps("v", c), count(c))], False, c)
+        return f
 
-    def mid0():
-        cp(A("LT"), Tl0)
-        run(row_keys(A("pC", 0, 128)))
-    gates(0, early0, mid0)
-    fields()
-    tables(0, ["pF0", "pF1", "pY"])
-    ts(A("uT"), A("pC", 128, 384), 1.0 / 64, op.mult)
-    cp(A("i4"), Tl0)
-    for j, v in ((1, 1024.0), (2, 16.0), (3, 4.0)):
-        fill.append(lambda j=j, v=v: ts(A("Id", 128 * j, 128 * j + 128), A("XD", 0, 128), 0.0, op.is_equal, v, op.mult))
-    ts(A("i5"), A("i4"), 15, op.bitwise_and)
-    ts(A("i6"), A("i4"), 2, op.arith_shift_right, 192, op.bitwise_and)
-    fill.extend([lambda: ts(A("i4"), A("i4"), 4, op.arith_shift_right, 15, op.bitwise_and), lambda: ms(A("E", 4096, 4104), 0.0),
-                 lambda: tt(A("wb"), A("i4"), A("i6"), op.add)])
-    fill.extend(hot_m(64))
-    fill.extend([lambda: cp(A("Llo"), A("i5")),
-                 lambda: ts(A("Kb"), A("K0"), col("cf", 24), op.add, col("OH16", 5), op.mult),
-                 lambda: ts(A("K0"), A("K0"), col("cf", 24), op.add, col("cf", 25), op.mult),
-                 lambda: ts(A("junk"), A("junk"), ci, op.add),
-                 lambda: tt(A("Sel5", 0, 3), A("OH32", 1, 14, 6), A("OH32", 19, 32, 6), op.add),
-                 lambda: cp(col("Sel5", 3), col("OH16", 5)), lambda: cp(col("Sel5", 4), col("OH16", 4)),
-                 lambda: ts(A("Yw32"), A("XI", 0, 132), col("cf", 27), op.is_equal),
-                 lambda: ts(A("Yw"), A("XI", 0, 132), col("cf", 27), op.is_equal)])
-    draws(0)
-    gap(100)
-    count_cols(0, {})
-    lists_after(0, Tl0, None)
+    def drain():
+        rest = [e[3] for e in pool if e[3] is not None] + list(range(96, 128))
+        pool[:] = [e for e in pool if e[3] is None]
+        while held:
+            count(held.pop(0))
+        return rest
+    draws(0, after(0))
+    rest = drain()
+    n3 = ACOL[0][3]
+    count_tail(rest[:len(rest) - n3], rest[len(rest) - n3:], {2: lambda: row_lists(A("Tl"), "aa")})
     for k in range(4):
-        mm(A("pA", 0, 32), One, A("c", 96 * k + 64, 96 * k + 96), k == 0, k == 3)
-    act(A("pg"), Ind(nxw, A("L0")), fn.Copy, None, col("cf", 26))
-    act(A("msk"), Ind(A("OH16"), A("Llo")), fn.Copy)
-    places(0)
-
-    def payload(m):
-        tt(A("pay", 256 * m + 256, 256 * m + 512), Ind(nxw, A("LN", 16 * m, 16 * m + 16)), A("Kb"), op.add)
-    cp(A("Lx"), A("pN", 0, 128))
-    payload(0)
-    payload(1)
-    I = A("i1", 0, 64)
-    ts(I, A("pM", 0, 64), col("pM", 64), op.add, 2048.0, op.add)
-    cp(A("Lw"), A("pN", 128, 256))
-    ts(A("i2", 0, 64), I, 4, op.arith_shift_right)
-    ts(A("i3", 0, 64), I, 8, op.arith_shift_right)
-    ts(A("f1", 0, 64), I, 1024.0, op.is_ge, 8192.0, op.mult)
-    ts(A("f2", 0, 64), A("i2", 0, 64), 112.0, op.mult, ce16, op.add)
-    ts(A("f3", 0, 64), A("i3", 0, 64), -2016.0, op.mult)
-    tt(A("f1", 64, 128), A("f1", 0, 64), I, op.add)
-    tt(A("f2", 64, 128), A("f2", 0, 64), A("f3", 0, 64), op.add)
-    ts(A("Pq"), I, 1024.0, op.min)
-    tt(A("f3", 64, 128), A("f1", 64, 128), A("f2", 64, 128), op.add)
+        mm(B("pM", 2, 0, 32), One, A("cb", 128 * k + 3, 128 * k + 128, 4), k == 0, k == 3)
+    act(A("pg"), Ind(nxw, A("LA")), fn.Copy)
+    exp_table("ad0", 0, "pF0")
+    exp_table("ad0", 1, "pF1")
+    mode["far"] = FAR[1]
+    ts(A("Lp"), B("pM", 1), -0.5 - 64 * H0, op.add)
+    cp(A("Lx"), B("pM", 0))
+    later([lambda e=e: red(col("Hc", e), B("pM", 2, e, 32, 2)) for e in range(2)] +
+          [lambda: ts(A("W0b"), A("Hc", 0, 2), -1.0 / 1024, op.mult, 137.0 - 511.5 / 1024, op.add),
+           lambda: ts(A("W0c", 0, 2), A("W0b"), -128.0, op.add)])
+    marks(0)
+    base, thr = col("pC", 128), col("pC", 129)
+    tt(A("J"), A("nM"), A("J"), op.mult)
+    tt(A("nM"), A("S"), A("J"), op.add)
+    ts(A("Pq"), A("S"), base, op.add, 1025.0, op.min)
+    for m in range(4):
+        ts(A("Lsc", 16 * m, 16 * m + 16), A("nM", m, 64, 4), thr, op.add, col("cf", 41), op.mult)
+    send([((r - 1) % 4, T.W0c[:, 0:2], T.w0l[:, 0:2], "aw0", 0, NE)], whole("W0c", 0, 2))
+    tt(Ind(A("sw"), A("Lsc")), A("pg"), A("K"), op.max)
     for q in range(4):
-        mm(A("pC", 64 * q, 64 * q + 64), A("Rep", 128 * q, 128 * q + 128), A("Pq"), True, True, q == 3)
-    act(A("Qw"), A("pC", 0, 256), fn.Copy)
-    for q in range(4):
+        mm(B("pH", q >> 1, 64 * (q & 1), 64 * (q & 1) + 64), rep(q), A("Pq"), True, True, q == 3)
+    act(A("Qw"), B("pH", (0, 2)), fn.Copy)
+    for j in range(2, 6):
+        exp_table("ad0", j, ["pW", "pN", "pF0", "pF1"][j - 2])
+    for q in [r] + oth:
         terms_gather(q)
-    payload(2)
-    tt(A("f1", 0, 64), A("f3", 64, 128), A("junk"), op.min)
-    tt(A("pay", 0, 256), A("pg"), A("K0"), op.add)
-    cp(A("Lsc"), A("f1", 0, 64))
-    cp(Ind(A("sw"), A("Lsc")), A("pay"))
-    mm(A("pY"), Zb, A("Wq", 0, 512), True, False, False)
-    clear_tab()
-    terms_sum(0)
-
-    def miss_weight():
-        for e in range(2):
-            red(col("Hc", e), A("pA", 16 * e, 16 + 16 * e))
-        ts(A("ib", 0, 2), A("Hc", 0, 2), -1.0, op.mult, 8192.0, op.add)
-        ts(A("OE"), A("XE"), ce16, op.is_equal)
-        ts(A("ib", 2, 4), A("ib", 0, 2), 10, op.arith_shift_right)
-        ms(A("XN", 4096, 4104), 0.0)
-        ts(A("W0c", 0, 2), A("ib", 2, 4), 1.0, op.add)
-        send([((r - 1) % 4, T.W0c[:, 0:2], T.w0l[:, 0:2], "aw0", 0, 1)], whole("W0c", 0, 2))
-    fill.append(miss_weight)
     for c in range(16):
-        mm(A("pM", c, 80, 16), A("sw", 128 * c, 128 * c + 128), A("Sel5", 0, 5), True, True, c == 15)
-
-    def place_rows(j):
-        tt(A("G", 512 * j, 512 * j + 512), Ind(A("Qw"), A("Lw", 32 * j, 32 * j + 32)), A("msk", 512 * j, 512 * j + 512), op.mult)
-    for j in range(3):
-        place_rows(j)
-    cp(A("LN"), A("pM", 0, 80))
-
-    def new_rows(h):
-        for i in range(16):
-            mm(A("pN", 64 * h, 64 * h + 64), A("Dw", 15 - i, 143 - i), A("G", 1024 * h + i, 1024 * h + 1024, 16), i == 0, i == 15)
-    new_rows(0)
+        mm(B("pM", 3, c, 96, 16), A("sw", 3072 + c, 5120, 16), A("Sel6", 0, 6), True, True, c == 15)
+    tt(A("G"), Ind(A("Qw"), A("Lp")), A("msk"), op.mult)
+    cp(A("LN"), B("pM", 3, 0, 96))
+    T4 = B("pH", (0, 4), 0, 32)
+    for i in range(16):
+        mm(B("pH", (0, 4), 2 * i, 2 * i + 2), A("G", i, 2048, 16), A("SelT"), True, True, i == 15)
     zx = A("zw0")
     act(A("xa"), Ind(zx, A("LN", 64, 80)), fn.Copy, None, 0.25)
     ts(A("xb"), Ind(zx, A("LN", 48, 64)), 0.75, op.mult)
-    for m in range(3):
-        act(A("R", 256 * m, 256 * m + 256), Ind(nxw, A("LN", 16 * m, 16 * m + 16)), fn.Identity, col("M0", 7), col("M0", 3))
-    tt(A("xo"), A("xa"), A("xb"), op.add)
-    place_rows(3)
+    act(A("R"), Ind(nxw, A("LN", 80, 96)), fn.Identity, col("cf", 27), col("cf", 20))
+    keys = row_keys(T4, 4.0)
+    tt(A("xo1"), A("xa"), A("xb"), op.add)
+    tab(lambda q: rep(q, 1), A("R"), False, True)
+    x_table(0, "pY")
+    x_table(1, "pC")
+    ev = []
+    gates(1, lambda m: A("LN", 16 * m, 16 * m + 16), A("xo1"), lambda: (keys(), ev.append(track_list(1)), later(hot(0, 64))))
+    act(A("ad0"), A("d"), fn.Abs)
+    for e, w in ((0, col("W0c", 1, 0, 64)), (1, col("w0l", 0, 64, 128))):
+        ts(col("cf", 26, 64 * e, 64 * e + 64), col("OH", 2, 64 * e, 64 * e + 64), w, op.mult, col("cf", 24, 64 * e, 64 * e + 64), op.add)
+    ts(A("prf"), A("hi"), H0 + 63.5, op.is_ge, -2.0, op.mult)
+    ts(A("tixf"), B("pM", 2), KT + 1023.5, op.is_ge, 4096.0, op.mult)
+    run(ev)
+    later([lambda: tt(A("uT", 128, 256), A("uT", 128, 256), A("prf"), op.add), lambda: tt(A("Tx"), A("tixf"), A("Tl"), op.max)], True)
+    rot = ["pM", "pC", "pF0", "pF1", "pM", "pC"]
+    gap(HOT0)
+    mode["far"] = FAR[3]
+    fields(1, None, lambda: (new_x() if XDMA else x_table(2, "pY"), exp_table("ad0", 0, rot[0])))
+    gap(HOT1)
+    for j in range(1, 6):
+        exp_table("ad0", j, rot[j])
+    xs_ = [] if XDMA else [lambda j=j: x_table(j, ["pY", "pF0", "pF1"][j % 3]) for j in range(3, 8)]
+    run(xs_[:NX1])
+    fresh.update({0: True, 1: True})
+    draws(1, after(1))
+    rest = drain()
+    row_lists(A("Tx"), "hi")
 
-    def mid1():
-        cp(A("Tl"), A("pN", 0, 128))
-        ts(A("LT"), A("pN", 0, 128), 1023.0, op.min)
-        mm(A("pC", 0, 128), A("Tl"), A("Id", 0, 128), True, True)
-        terms_sum(1)
-        terms_sum(2)
-        ts(A("W0v", 0, 16), A("Cb", 0, 16), col("W0c", 1), op.add)
-        ts(A("f2"), A("Tl"), 1024.0, op.is_ge, 3072.0, op.mult)
-        tt(A("Tx"), A("f2"), A("Tl"), op.add)
-    gates(1, lambda: new_rows(1), mid1)
-    fields()
-    ts(A("f1"), A("pC", 0, 128), 1024.0, op.is_ge, -2.0, op.mult)
-    km = row_keys(A("pC", 0, 128))
-    km[0]()
-    tt(A("uT", 128, 256), A("uT", 128, 256), A("f1"), op.add)
-    ts(A("W0v", 16, 32), A("Cb", 0, 16), col("w0l", 0), op.add)
-    terms_sum(3)
-    tables(1, ["pM", "pN", "pF1", "pF0"])
-    new_x(range(8), ["pC", "pF1", "pF0", "pM", "pC", "pN", "pF1", "pF0"])
-    fill.extend(km[1:] + hot_m(64))
-    draws(1)
-    lists_after(1, A("Tx"), A("Tl"))
-    gap(100)
-    def terms_list():
-        cp(A("Lx"), A("pN", 0, 128))
-        for q in range(4):
-            terms_gather(q)
-    count_cols(1, {EA[1] + 10: terms_list, EA[1] + 36: lambda: terms_sum(0), EA[1] + 56: lambda: terms_sum(1),
-                   EA[1] + 76: lambda: terms_sum(2)})
-    places(1)
-    terms_sum(3, True)
-    act(A("Ye"), A("pY"), fn.Copy)
-    send3("Ye", "yel", 128, "ae%d" % r)
-    cp(A("tixf"), A("pN", 0, 128))
-    cp(A("prf"), A("pN", 128, 256))
-    ts(A("Pq"), A("pM", 0, 64), col("pM", 64), op.add, 1024.0, op.is_lt)
-    mm(A("pC", 0, 64), A("OE"), A("Pq"), True, True)
-    red(col("Hc", 2), A("pC", 0, 64))
-    ts(A("f1"), A("prf"), col("Hc", 2), op.is_ge, 8192.0, op.mult)
-    tt(A("f2"), A("f1"), A("tixf"), op.add)
-    ts(A("Ly"), A("f2"), 4096.0, op.min)
-    bank = dict(zip(oth + [r], ["pA", "pB", "pN", "pM"]))
+    def terms_add(q):
+        v = A("V", 512 * q, 512 * q + 512)
+        tt(v, Ind(A("E"), A("Lx", 32 * q, 32 * q + 32)), v, op.add)
+
+    def terms():
+        cp(A("Lx"), B("pM", 0))
+        terms_add(oth[0])
+    count_tail(rest[:NV1], rest[NV1:], {min(2 * NV1, len(rest) - 1): terms})
+    act(A("tixf"), B("pM", 0), fn.Copy)
+    act(A("prf"), B("pM", 1), fn.Identity, -0.5 - 64 * H0)
+    ybank = dict(zip(oth + [r], ["pY", "pF0", "pF1", "pY"]))
+
+    def ye_sum(q):
+        terms_sum(q, True, True, A(ybank[q], 0, 128))
+
+    def ye_out(q, e):
+        o = A("Ye", 128 * q, 128 * q + 128)
+        if e == "a":
+            act(o, A(ybank[q], 0, 128), fn.Copy)
+        else:
+            cp(o, A(ybank[q], 0, 128))
+        if q != r:
+            send([(q, T.Ye[:, 128 * q:128 * q + 128], T.yel[:, 128 * r:128 * r + 128], "ae%d" % r, 0, NE)], o[1])
+    run(xs_[NX1:])
+    ye_sum(oth[0])
+    marks(1, lambda: terms_add(oth[1]))
+    ye_out(oth[0], "a")
+    ts(A("Lv"), A("S"), thr, op.is_lt)
+    mm(A("pC", 192, 256), A("OE"), A("Lv"), True, True)
+    terms_add(oth[2])
+    ye_sum(oth[1])
+    red(col("Hc", 2), A("pC", 192, 256))
+    ts(A("f1"), A("prf"), col("Hc", 2), op.is_ge, 4096.0, op.mult)
+    tt(A("f1"), A("f1"), A("tixf"), op.max)
+    cp(A("Ly"), A("f1"))
+    bank = dict(zip(oth + [r], ["pW", "pH", "pN", "pM"]))
 
     def last_gather(q, e):
         o, s = A("G", 512 * q, 512 * q + 512), Ind(A("XN"), A("Ly", 32 * q, 32 * q + 32))
@@ -775,31 +891,36 @@ def rank_program(g, core, T, topo):
         else:
             ts(o, s, -4.0, op.add)
         for u in range(4):
-            mm(A(bank[q], 0, 128), A("Yw", 3 - u, 131 - u), A("G", 512 * q + 128 * u, 512 * q + 128 * u + 128), u == 0, u == 3)
+            mm(B(bank[q], 0), A("Yw", 3 - u, 131 - u), A("G", 512 * q + 128 * u, 512 * q + 128 * u + 128), u == 0, u == 3)
 
     def last_out(q, e):
         o = A("Yx", 128 * q, 128 * q + 128)
         if e == "a":
-            act(o, A(bank[q], 0, 128), fn.Identity, 16.0)
+            act(o, B(bank[q], 0), fn.Identity, 16.0)
         else:
-            ts(o, A(bank[q], 0, 128), 16.0, op.add)
+            ts(o, B(bank[q], 0), 16.0, op.add)
     last_gather(oth[0], "v")
     last_gather(oth[1], "a")
+    ye_out(oth[1], "a")
     last_gather(oth[2], "v")
+    ye_sum(oth[2])
     last_out(oth[0], "a")
     last_out(oth[1], "a")
     send([(oth[j], T.Yx[:, 128 * oth[j]:128 * oth[j] + 128], T.yxl[:, 128 * r:128 * r + 128], "ax%d" % r, j * NE // 2, NE // 2)
           for j in range(2)], whole("Yx", 128 * oth[0], 128 * oth[0] + 128) + whole("Yx", 128 * oth[1], 128 * oth[1] + 128))
-    last_gather(r, "a")
     last_out(oth[2], "v")
     send([(oth[2], T.Yx[:, 128 * oth[2]:128 * oth[2] + 128], T.yxl[:, 128 * r:128 * r + 128], "ax%d" % r, 0, NE)],
          whole("Yx", 128 * oth[2], 128 * oth[2] + 128))
-    last_out(r, "v")
-    for out, own, land in (("ye", "Ye", "yel"), ("yx", "Yx", "yxl")):
-        for j, s in enumerate(frm[:2] + [r, frm[2]]):
-            n = own if s == r else land
-            dma("s" if out == "ye" else "sa"[j % 2], T[out][32 * s:32 * s + 32, :], T[n][:, 128 * s:128 * s + 128], "sto", 8, [],
-                whole(n, 128 * s, 128 * s + 128))
+    terms_add(r)
+    last_gather(r, "a")
+    ye_out(oth[2], "v")
+    ye_sum(r)
+    last_out(r, "a")
+    ye_out(r, "v")
+    for q, out, s in (("s", "ye", frm[0]), ("s", "ye", frm[1]), ("a", "yx", r), ("s", "yx", frm[0]), ("a", "yx", frm[1]),
+                      ("s", "ye", r), ("a", "yx", frm[2]), ("s", "ye", frm[2])):
+        n = {"ye": ("Ye", "yel"), "yx": ("Yx", "yxl")}[out][s != r]
+        dma(q, T[out][32 * s:32 * s + 32, :], T[n][:, 128 * s:128 * s + 128], "sto", 8, [], whole(n, 128 * s, 128 * s + 128))
     for q in cnt:
         total["c" + q] = cnt[q]
     for sem, val in total.items():

@@ -12,12 +12,12 @@ for _n, _w, _d in [
     ("Hl", 384, F16), ("XS", 128, BF), ("XR", 128, BF),
     ("N0t", 16, I32), ("X0", 256, F32), ("xs", 256, BF), ("xo", 256, F16), ("xo1", 256, F16), ("xa", 256, F32), ("xb", 256, F32),
     ("ib", 10, I32), ("cf", 48, F32), ("XI", 176, BF), ("XD", 128, BF), ("XM", 144, BF),
-    ("MA", 4, F32), ("MQ", 4, F32), ("OH", 16, F32), ("GM", 8, F32), ("Wd", 704, BF), ("Dw", 144, BF), ("Wq", 576, BF),
+    ("MA", 4, F32), ("MQ", 4, F32), ("OH", 16, F32), ("GM", 8, F32), ("Wd", 704, BF), ("XJ", 128, BF), ("Wq", 576, BF),
     ("Rep", 528, BF), ("Rep4", 512, BF), ("Sq", 512, BF), ("SelW", 32, BF), ("SelH", 32, BF), ("SelN", 32, BF), ("SelT", 8, BF),
-    ("Sel6", 8, F32), ("Id", 896, BF), ("Qw", 256, F32), ("msk", 2048, BF), ("Pm", 256, BF), ("Tri", 256, BF), ("OE", 128, BF), ("Yw", 132, BF), ("Yw32", 132, F32),
-    ("Cb", 512, BF), ("ch", 4, F16), ("nxb", 256, I32), ("nxh", 256, F16), ("XQ", 128, BF),
-    ("SN", 2048, BF), ("p16", 20, F32), ("K1", 256, F32), ("K", 1024, F32), ("J", 64, F32), ("LS", 16, U16),
-    ("LA", 64, U16), ("LN", 96, U16), ("R", 256, F16), ("Rm", 768, F16), ("d", 768, F16), ("ad0", 768, F16),
+    ("Sel6", 8, F32), ("Id", 1024, BF), ("Qw", 256, F32), ("msk", 2048, BF), ("Pm", 256, BF), ("Tri", 256, BF), ("OE", 128, BF), ("Yw", 132, BF), ("Yw32", 132, F32),
+    ("Cb", 512, BF), ("ch", 4, F16), ("nxb", 256, I32), ("ni", 48, I32), ("nf", 32, F16), ("XQ", 128, BF),
+    ("SN", 648, BF), ("p16", 20, F32), ("K1", 256, F32), ("K", 1024, F32), ("J", 64, F32), ("LS", 16, U16),
+    ("LA", 64, U16), ("LN", 96, U16), ("R", 256, F16), ("d", 768, F16), ("ad0", 768, F16),
     ("ind", 768, BF), ("F", 1032, F32), ("G", 2048, F16), ("E", 4104, F32), ("XN", 4104, F32), ("V", 2048, F32),
     ("pg", 1024, F32), ("sw", 8192, F32), ("Ab", 8192, BF), ("Nb", 9216, BF),
     ("LT", 128, U16), ("Lp", 128, U16), ("Lx", 128, U16), ("Ly", 128, U16), ("Lsc", 64, U16),
@@ -29,8 +29,10 @@ for _n, _w, _d in [
     ("tixf", 128, F32), ("prf", 128, F32), ("Ye", 512, F32), ("Yx", 512, F32), ("yel", 512, F32), ("yxl", 512, F32),
 ]:
     SCRATCH[_n] = ("sbuf", [128, _w], _d)
-for _n in ["pY", "pF0", "pF1", "pC"]:
+for _n in ["pY", "pC"]:
     SCRATCH[_n] = ("psum", [128, 512], F32)
+for _n in ["pF0", "pF1"]:
+    SCRATCH[_n] = ("psum", [128, 2, 256], F32)
 for _n in ["pW", "pH", "pN", "pM"]:
     SCRATCH[_n] = ("psum", [128, 4, 128], F32)
 
@@ -41,11 +43,13 @@ H0 = 160.0
 KT = 2 + 241 * H0
 NF = 4
 FAR = (0, 4, 4, 4)
-EARLY = 80
+EARLY = (48, 8, 30)
 ACOL = ((20, 20, 20, 14), (20, 20, 20, 0))
 FA = (64, 64)
-NV1 = 12
+NV1 = 17
 HOT0, HOT1 = 8, 12
+ZQ, ZG = ("avav", "avav"), 0
+TURN = 2
 XDMA = True
 NX1 = 5
 
@@ -73,10 +77,11 @@ def rank_program(g, core, T, topo):
 
     def B(name, k, c0=0, c1=128, st=1, p0=0, p1=128):
         t = T[name]
+        w = t.shape[2]
         if isinstance(k, tuple):
-            return (t[p0:p1, k[0]:k[1], c0:c1], [(name, p0, p1, 128 * k[0] + c0, 128 * (k[1] - 1) + c1, 1)])
+            return (t[p0:p1, k[0]:k[1], c0:c1], [(name, p0, p1, w * k[0] + c0, w * (k[1] - 1) + c1, 1)])
         ap = t[p0:p1, k, c0:c1] if st == 1 else t[p0:p1, k, c0:c1:st]
-        return (ap, [(name, p0, p1, 128 * k + c0, 128 * k + c1, st)])
+        return (ap, [(name, p0, p1, w * k + c0, w * k + c1, st)])
 
     def col(name, c, p0=0, p1=128):
         return A(name, c, c + 1, 1, p0, p1)
@@ -340,8 +345,12 @@ def rank_program(g, core, T, topo):
     Zb, One, Neg, Qrt = [A("Cb", 128 * j, 128 * j + 128) for j in range(4)]
     iota(col("ib", 8), [[0, 1]], 0, 1)
     iota(A("XI"), [[1, 176]], 0, 0)
+    row0 = 6 * r - min(6 * r, 16)
     for e in range(2):
-        iota(A("XQ", 64 * e, 64 * e + 64), [[0, 4], [16, 4], [1000, 4]], 48 * e + 96 * r - min(96 * r, 256), 0)
+        c0, c1 = ((0, row0 + 3), (row0 + 3, 8))[e]
+        iota(A("XJ", 16 * c0, 16 * c1), [[0, c1 - c0], [1, 16]], 64 * e, 0)
+    for e in range(2):
+        iota(A("XQ", 64 * e, 64 * e + 64), [[0, 4], [16, 4], [1000, 4]], 48 * e + 16 * row0, 0)
     iota(A("XS"), [[64, 2], [0, 4], [4, 16]], 0, 0)
     iota(A("XD"), [[1, 128]], 0, -1)
     iota(A("XR"), [[64, 2], [0, 4], [1, 16]], 0, 0)
@@ -370,20 +379,25 @@ def rank_program(g, core, T, topo):
     ts(A("p16", 0, 16), A("XI", 0, 16), -1.0, op.mult, col("cf", 47), op.add)
     ms(A("Rep"), 0.0)
     ms(A("XM", 0, 16), 99.0)
-    for j in range(16):
-        ts(A("SN", 128 * j, 128 * j + 128), A("XQ"), col("p16", j), op.is_equal)
+    ts(A("p16", 16, 20), A("XI", 0, 4), -16.0, op.mult, col("cf", 47), op.add)
+    ts(col("cf", 14), col("cf", 5), 1.0 / 16, op.mult, float(-row0), op.add)
+    for a in range(4):
+        ts(A("SN", 128 * a, 128 * a + 128), A("XJ"), col("p16", 16 + a), op.is_equal)
+    ts(A("SN", 512, 640), A("XQ"), col("cf", 5), op.is_equal)
+    ts(A("SN", 640, 646), A("XI", 0, 6), col("cf", 14), op.is_equal)
 
     for cq in range(4):
         ts(A("Sq", 128 * cq, 128 * cq + 128), A("XS"), col("p16", cq), op.is_equal)
-    mode["each"] = False
-    gap(100, True)
-    for kind in range(3):
-        cp(A("Hh", kind, 384, 3), A("HU", 128 * kind, 128 * kind + 128))
-    for q in oth + [r]:
-        for k in range(4):
-            mm(A("pY", 96 * q, 96 * q + 96), A("Wd", 176 * q + 48 - 16 * k, 176 * q + 176 - 16 * k), A("Hh", 96 * k, 96 * k + 96), k == 0, k == 3)
-    cp(A("xs"), A("X0"))
-    cp(A("Hs"), A("pY", 0, 384))
+
+    def lists_out():
+        for kind in range(3):
+            cp(A("Hh", kind, 384, 3), A("HU", 128 * kind, 128 * kind + 128))
+        for q in oth + [r]:
+            for k in range(4):
+                mm(A("pY", 96 * q, 96 * q + 96), A("Wd", 176 * q + 48 - 16 * k, 176 * q + 176 - 16 * k), A("Hh", 96 * k, 96 * k + 96),
+                   k == 0, k == 3)
+        cp(A("xs"), A("X0"))
+        cp(A("Hs"), A("pY", 0, 384))
 
     def send_z():
         dst = T.zl[r] if r >= 2 else T.zb[:, 512 * r:512 * r + 512]
@@ -393,22 +407,24 @@ def rank_program(g, core, T, topo):
     def send_nx():
         send([(oth[j], T.nxs[oth[j]] if r >= 2 else T.nxd[min(96 * oth[j], 256):min(96 * oth[j], 256) + 128, :],
                T.nxl[r] if r >= 2 else T.nxb[:, 128 * r:128 * r + 128], "an%d" % r, split3[j][0], split3[j][1]) for j in range(3)], slot("nxs", 0))
-    send_nx()
-    if r < 2:
-        send_z()
-    iota(A("XM", 16, 144), [[1, 2], [0, 4], [100, 16]], 0, 0)
-    iota(A("K1"), [[1, 16], [16, 16]], 0, 0)
-    send3("Hs", "Hl", 96, "ah")
-    iota(A("nxw", 0, 2048), [[1, 2048]], 0, 0)
-    iota(A("nxw", 2048, 4096), [[1, 2048]], 2048, 0)
-    for j, c in enumerate((One, Neg)):
-        asel(A("Tri", 128 * j, 128 * j + 128), c, [[1, 128]], op.is_gt, 0, -1)
-    for j in range(2):
-        asel(A("Tri", 128 * j, 128 * j + 128), A("Tri", 128 * j, 128 * j + 128), [[-64, 2], [0, 64]], op.is_ge, 0, 1)
-    if r >= 2:
-        deps("g", whole("zb"), [])
-        send_z()
-    iota(A("sw", 3072, 5120), [[0, 2048]], 0, 0)
+
+    def writes_out():
+        send_nx()
+        if r < 2:
+            send_z()
+        iota(A("XM", 16, 144), [[1, 2], [0, 4], [100, 16]], 0, 0)
+        iota(A("K1"), [[1, 16], [16, 16]], 0, 0)
+        send3("Hs", "Hl", 96, "ah")
+        iota(A("nxw", 0, 2048), [[1, 2048]], 0, 0)
+        iota(A("nxw", 2048, 4096), [[1, 2048]], 2048, 0)
+        for j, c in enumerate((One, Neg)):
+            asel(A("Tri", 128 * j, 128 * j + 128), c, [[1, 128]], op.is_gt, 0, -1)
+        for j in range(2):
+            asel(A("Tri", 128 * j, 128 * j + 128), A("Tri", 128 * j, 128 * j + 128), [[-64, 2], [0, 64]], op.is_ge, 0, 1)
+        if r >= 2:
+            deps("g", whole("zb"), [])
+            send_z()
+        iota(A("sw", 3072, 5120), [[0, 2048]], 0, 0)
 
     def Id(j):
         return A("Id", 128 * j, 128 * j + 128)
@@ -417,7 +433,9 @@ def rank_program(g, core, T, topo):
         return A("Rep", 132 * q + 1 + shift, 132 * q + 129 + shift)
 
     def half(b, u):
-        return B(b, (2 * u, 2 * u + 2)) if len(T[b].shape) == 3 else A(b, 256 * u, 256 * u + 256)
+        if len(T[b].shape) == 2:
+            return A(b, 256 * u, 256 * u + 256)
+        return B(b, (2 * u, 2 * u + 2)) if T[b].shape[2] == 128 else B(b, u, 0, 256)
 
     def zspread(s, qs, banks=("pW", "pH", "pN", "pY")):
         def out(cq):
@@ -429,57 +447,48 @@ def rank_program(g, core, T, topo):
         for cq in range(4):
             mm(A(banks[cq]), A("Sq", 128 * cq, 128 * cq + 128), A("zb", 512 * s, 512 * s + 512), True, True)
         return [lambda cq=cq: out(cq) for cq in range(4)]
-    for cq in range(4):
-        mm(half("pF%d" % (cq >> 1), cq & 1), A("Sq", 128 * cq, 128 * cq + 128), A("xs"), True, True, cq & 1 == 1)
-    for h in range(2):
-        act(A("zw0", 4096 + 512 * h, 4608 + 512 * h), A("pF%d" % h), fn.Copy)
 
-    def nxspread(ss, qs):
-        banks = ["pW", "pH", "pN", "pY", "pF0", "pF1", "pC", "pM"]
-        for s in ss:
-            ts(A("nxh", 128 * s, 128 * s + 128), A("nxb", 128 * s, 128 * s + 128), -2047.0, op.add)
-        for n, (s, b) in enumerate([(s, b) for s in ss for b in range(4)]):
-            for j in range(4):
-                c = 128 * (4 * b + j)
-                o = B(banks[n], j) if len(T[banks[n]].shape) == 3 else A(banks[n], 128 * j, 128 * j + 128)
-                mm(o, A("SN", c, c + 128), A("nxh", 128 * s, 128 * s + 128), True, True, j == 3)
-            o = A("XN", 2048 * s + 512 * b, 2048 * s + 512 * b + 512)
-            if qs[n] == "a":
-                act(o, A(banks[n]), fn.Copy)
-            else:
-                cp(o, A(banks[n]))
-    if r < 2:
-        nxspread([r], "aaaa")
-        run(zspread(r, "aaaa"))
-    nxhop()
-    cp(A("Hl", 96 * r, 96 * r + 96), A("Hs", 96 * r, 96 * r + 96))
-    mode["each"] = True
-    ts(A("p16", 16, 20), A("XI", 0, 4), -16.0, op.mult, col("cf", 47), op.add)
+    def prepare():
+        for cq in range(4):
+            mm(half("pF%d" % (cq >> 1), cq & 1), A("Sq", 128 * cq, 128 * cq + 128), A("xs"), True, True, cq & 1 == 1)
+        for h in range(2):
+            act(A("zw0", 4096 + 512 * h, 4608 + 512 * h), A("pF%d" % h), fn.Copy)
+        ts(A("ni", 0, 16), A("N0t"), 4, op.arith_shift_right, 128, op.bitwise_and)
+        ts(A("ni", 16, 32), A("N0t"), 127, op.bitwise_and)
+        ts(A("ni", 32, 48), A("N0t"), 7, op.arith_shift_right, 15, op.bitwise_and)
+        cp(A("LA", 0, 16), A("N0t"))
+        cp(A("Hl", 96 * r, 96 * r + 96), A("Hs", 96 * r, 96 * r + 96))
+        tt(A("nf", 0, 16), A("ni", 0, 16), A("ni", 16, 32), op.add)
+        cp(A("nf", 16, 32), A("ni", 32, 48))
+        for a in range(4):
+            mm(A("pC", a, 128, 4), A("SN", 128 * a, 128 * a + 128), A("nf"), True, True, a == 3)
+        cp(A("Lp"), A("pC", 0, 128))
+        act(A("msk", 0, 1024), Ind(A("OH"), A("Lp", 64, 128)), fn.Copy)
+        if r < 2:
+            ts(A("xa", 128 * r, 128 * r + 128), A("nxb", 128 * r, 128 * r + 128), -2047.0, op.add)
+            run(zspread(r, "aaaa"))
+        nxhop()
+        act(A("xo"), Ind(A("zw0", 4096, 5120), A("LS")), fn.Copy)
     ts(col("cf", 10), ca, 32.0, op.mult, ce, op.add)
     ts(col("cf", 12), ca, 2.0, op.mult, ce, op.add)
     ts(A("MA"), A("XI", 0, 4), ca, op.is_equal)
     ts(col("cf", 11), ci, 2.0, op.mult, col("cf", 10), op.add)
-    for j, v in enumerate((1.0, 4.0, 64.0, 240.0, 1024.0, 0.25, -16.0)):
+    for j, v in enumerate((1.0, 4.0, 64.0, 240.0, 1024.0, 0.25, -16.0, -1024.0)):
         ts(Id(j), A("XD"), 0.0, op.is_equal, v, op.mult)
     ts(A("Pm", 0, 128), A("XI", 0, 128), col("cf", 11), op.is_equal)
     ts(A("Pm", 128, 256), A("XI", 0, 128), col("cf", 11), op.is_equal, 4.0, op.mult)
     ts(A("GM"), A("XI", 0, 8), col("cf", 12), op.is_equal)
-    cp(A("LA", 0, 16), A("N0t"))
     for q in range(4):
         ts(rep(q), A("XR"), col("p16", 16 + q), op.is_equal)
     ts(col("cf", 13), col("cf", 6), 16.0, op.mult)
-    ts(col("cf", 14), col("cf", 5), 15.0, op.add)
     ts(col("cf", 15), ca, 256.0, op.mult, 4096.0, op.add)
     tt(col("cf", 16), col("OH", 13), col("OH", 14), op.add)
     ts(A("LS"), A("XI", 0, 16), col("cf", 13), op.add)
-    ts(A("Dw"), A("XI", 0, 144), col("cf", 14), op.is_equal)
     tt(col("cf", 17), col("cf", 15), col("cf", 16), op.mult)
     tt(col("cf", 18), col("cf", 15), col("OH", 14), op.mult)
     red(col("cf", 19), A("OH", 0, 12, 4))
     red(col("cf", 20), A("OH", 1, 12, 4))
     red(col("cf", 21), A("OH", 6, 16, 4))
-    for q in range(4):
-        ts(A("Wq", 144 * q, 144 * q + 144), A("XM"), ce, op.is_equal, col("MA", q), op.mult)
     ts(col("cf", 22), col("cf", 19), -2047.0, op.mult)
     ts(col("cf", 23), col("cf", 21), -4.0, op.mult, col("OH", 3), op.add)
     ts(col("cf", 27), col("cf", 20), -2047.0, op.mult)
@@ -487,8 +496,6 @@ def rank_program(g, core, T, topo):
     ts(col("cf", 25), col("OH", 2), 2.0, op.mult, col("cf", 24), op.add)
     cGa = col("cf", 22)
     cEv = [col("cf", 25), col("cf", 26)]
-
-    act(A("xo"), Ind(A("zw0", 4096, 5120), A("LS")), fn.Copy)
 
     def fixed():
         act(A("K", 0, 256), A("K1"), fn.Identity, col("cf", 17), col("cf", 16))
@@ -544,7 +551,7 @@ def rank_program(g, core, T, topo):
 
     def tab(lhs, src, last, first=False):
         for q in range(4):
-            mm(A("pF%d" % (q >> 1), 256 * (q & 1), 256 * (q & 1) + 256), lhs(q), src, first and (q & 1) == 0, last and (q & 1) == 1)
+            mm(half("pF%d" % (q >> 1), q & 1), lhs(q), src, first and (q & 1) == 0, last and (q & 1) == 1)
 
     def gates(t, lst, xo, pause=None, pause2=None):
         zw = A("zw%d" % t, 0, 4096)
@@ -616,10 +623,11 @@ def rank_program(g, core, T, topo):
 
     def steps(q, c):
         o = A("Nb", 72 * c, 72 * c + 65)
+        kc = col("key", c) if c < 96 else col("mb", 4 * c + 3)
         if q == "a":
-            act(o, A("XI", 0, 65), fn.Sign, col("key", c), -1.0)
+            act(o, A("XI", 0, 65), fn.Sign, kc, -1.0)
         else:
-            ts(o, A("XI", 0, 65), col("key", c), op.is_le, 2.0, op.mult)
+            ts(o, A("XI", 0, 65), kc, op.is_le, 2.0, op.mult)
 
     def count(c, last=False):
         e = c & 1
@@ -630,6 +638,7 @@ def rank_program(g, core, T, topo):
     def draws(t, after):
         def differ(o, j, k):
             return [lambda f=f: tt(A(o, f, 128, 4), B("pN", k, f, 128, 4), A("tk", 128 * j + 3, 128 * j + 128, 4), op.not_equal) for f in (1, 2, 3)]
+        later([lambda: cp(A("cb", 384, 512, 4), A("base", 96, 128))], True)
         for k in range(4):
             def Pm(m):
                 return B("pW", 0, m, 128, 4) if k == 0 else A("P", m, 128, 4)
@@ -650,14 +659,14 @@ def rank_program(g, core, T, topo):
             if k < 3:
                 scan(A("tk", 128 * k, 128 * k + 128), ck, B("pH", k), op.mult)
             scan(A("mb", 128 * k, 128 * k + 128), A("S4"), ck, op.mult)
-        key(3)
+        later([lambda: cp(A("key", 96, 128), A("mb", 387, 512, 4))], True)
 
     def key(k):
         tt(A("key", 32 * k, 32 * k + 32), A("mb", 128 * k + 3, 128 * k + 128, 4), A("base", 32 * k, 32 * k + 32), op.add)
 
     def row_lists(Tx, up):
+        turn(0, [("key", 0, 2, 4), ("base", 0, 2, 7)], (Id(0), Tx))
         turn(1, [("key", 0, 2, 0), (up, 0, 2, 2)])
-        turn(0, [("mb", 3, 8, 4)], (Id(0), Tx))
 
     def count_tail(cv_, ca_, between):
         order = []
@@ -672,11 +681,13 @@ def rank_program(g, core, T, topo):
                 between[n]()
             count(c, c in ends)
 
-    def marks(t, pause=None):
+    def marks(t, pause=None, early=None):
         cp(A("Cs"), A("pC", 1, 65))
         tt(A("Mk"), A("pC", 0, 64), A("Cs"), op.is_gt)
         if t == 0:
             tt(A("nM"), A("pC", 0, 64), A("Cs"), op.is_le)
+        if early:
+            early()
         scan(A("S"), A("Mk"), A("Cb", 0, 64), op.add)
         if t == 0:
             mm(col("pC", 128), A("Tri", 0, 128), col("S", 63), True, True, False)
@@ -699,8 +710,8 @@ def rank_program(g, core, T, topo):
 
     nxw = A("nxw")
     T4 = B("pM", (0, 4), 0, 32)
-    gap(EARLY, True)
-    later([lambda q=q: ts(A("Rep4", 128 * q, 128 * q + 128), A("XR"), col("p16", 16 + q), op.is_equal, 0.25, op.mult) for q in range(4)])
+    if not XDMA:
+        later([lambda q=q: ts(A("Rep4", 128 * q, 128 * q + 128), A("XR"), col("p16", 16 + q), op.is_equal, 0.25, op.mult) for q in range(4)])
     later([lambda: ts(col("cf", 40), col("cf", 6), -64.0, op.mult, 4096.0, op.add),
                  lambda: ts(col("cf", 41), ce, 2.0, op.mult, -1.0, op.add),
                  lambda: ts(col("cf", 42), ce, -1023 - 2 * KT, op.mult, 1023 + KT, op.add),
@@ -716,33 +727,45 @@ def rank_program(g, core, T, topo):
                  lambda: ts(A("Yw32"), A("XI", 0, 132), col("cf", 46), op.is_equal),
                  lambda: ts(A("Yw"), A("XI", 0, 132), col("cf", 46), op.is_equal),
                  lambda: ms(A("OE", 0, 64, 1, 0, 64), 1.0), lambda: ms(A("OE", 64, 128, 1, 64, 128), 1.0)])
+    gap(EARLY[0], True)
+    mode["far"] = EARLY[1]
+    lists_out()
+    writes_out()
+    prepare()
+    later([lambda q=q: ts(A("Wq", 144 * q, 144 * q + 144), A("XM"), ce, op.is_equal, col("MA", q), op.mult) for q in range(4)])
+    gap(EARLY[2], True)
+
     def misses():
         act(A("E", 0, 1024), A("zw0", 4096, 5120), fn.Exp, -1.0, 0.0)
-        fixed()
     if r >= 2:
         misses()
     mode["far"] = FAR[0]
     far = [x for x in frm if x < 2]
-    nxspread(far, "avavavav")
-    names = A("XN", 0, 4096)
-    zs_ = zspread(far[0], "avav", ("pW", "pH", "pN", "pY") if r >= 2 else ("pF0", "pF1", "pM", "pW"))
-    for m in range(2):
-        ts(A("Rm", 256 * m, 256 * m + 256), Ind(names, A("LA", 0, 16)), col("OH", 4 * m), op.mult)
-    act(A("Rm", 512, 768), Ind(names, A("LA", 0, 16)), fn.Copy, None, col("OH", 8))
-    for i in range(16):
-        mm(A("pC", 0, 48), A("Dw", 15 - i, 143 - i), A("Rm", i, 768, 16), i == 0, i == 15)
+    for s in far:
+        ts(A("xa", 128 * s, 128 * s + 128), A("nxb", 128 * s, 128 * s + 128), -2047.0, op.add)
+    for h in range(2):
+        tt(A("G", 512 * h, 512 * h + 512), Ind(A("xa"), A("Lp", 32 * h, 32 * h + 32)), A("msk", 512 * h, 512 * h + 512), op.mult)
+        for c in range(8 * h, 8 * h + 8):
+            for e in range(2):
+                mm(A("pC", c, 48, 16, 64 * e, 64 * e + 64), A("G", 64 * c, 64 * c + 64), A("SN", 640 + 3 * e, 643 + 3 * e), True, True,
+                   c == 15 and e == 1)
     zhop()
-    run(zs_[:2])
-    z2 = zspread(far[1], "avav", ("pF0", "pF1", "pM", "pW")) if r >= 2 else []
+    zs_ = zspread(far[0], ZQ[0] if r >= 2 else "avav")
     ts(A("LA", 16, 64), A("pC", 0, 48), 2047.0, op.add)
-    run(zs_[2:] + z2)
+    gap(ZG)
+    run(zs_)
+    if r >= 2:
+        run(zspread(far[1], ZQ[1], ("pM", "pF0", "pF1", "pW")))
     mode["far"] = FAR[1]
     mm(T4, A("Hl", 0, 384, 3), A("Pm", 128, 256), True, True)
-    act(A("R"), Ind(names, A("LA", 0, 16)), fn.Copy)
     keys = row_keys(T4, 0.0)
     if r < 2:
         misses()
-    tab(rep, A("R"), False, True)
+    else:
+        fixed()
+    for h in range(2):
+        for c in range(16):
+            mm(B("pF%d" % h, (0, 2), 16 * c, 16 * c + 16), A("SN", 512, 640), A("G", 64 * c + 32 * h, 64 * c + 32 * h + 32), c == 0, False)
     ev = []
     gates(0, lambda m: A("LA", 16 * m + 16, 16 * m + 32), A("xo"),
           lambda: (keys(), later(hot(0, 64)), ev.append(track_list(0)), turn(1, [("hi", 0, 2, 0), ("aa", 0, 2, 6)])), lambda: run(ev))
@@ -755,6 +778,8 @@ def rank_program(g, core, T, topo):
     act(A("ad0"), A("d"), fn.Abs)
     ts(A("uT"), A("pC", 0, 256), 1.0 / 64, op.mult)
     act(A("msk"), Ind(A("OH"), A("Ly")), fn.Copy)
+    if r < 2:
+        fixed()
     gap(HOT1)
     held = []
 
@@ -780,33 +805,36 @@ def rank_program(g, core, T, topo):
     draws(0, after(0))
     rest = drain()
     n3 = ACOL[0][3]
-    count_tail(rest[:len(rest) - n3], rest[len(rest) - n3:], {2: lambda: row_lists(A("Tl"), "aa")})
+    count_tail(rest[:len(rest) - n3], rest[len(rest) - n3:], {})
     for k in range(4):
         mm(B("pM", 2, 0, 32), One, A("cb", 128 * k + 3, 128 * k + 128, 4), k == 0, k == 3)
+    row_lists(A("Tl"), "aa")
     act(A("pg"), Ind(nxw, A("LA")), fn.Copy)
+    mode["far"] = FAR[1]
+
+    def lists0():
+        ts(A("Lp"), B("pM", 1), -0.5 - 64 * H0, op.add)
+        cp(A("Lx"), B("pM", 0))
+        later([lambda e=e: red(col("Hc", e), B("pM", 2, e, 32, 2)) for e in range(2)] +
+              [lambda: ts(A("W0b"), A("Hc", 0, 2), -1.0 / 1024, op.mult, 137.0 - 511.5 / 1024, op.add),
+               lambda: ts(A("W0c", 0, 2), A("W0b"), -128.0, op.add)])
+    marks(0, None, lists0)
     exp_table("ad0", 0, "pF0")
     exp_table("ad0", 1, "pF1")
-    mode["far"] = FAR[1]
-    ts(A("Lp"), B("pM", 1), -0.5 - 64 * H0, op.add)
-    cp(A("Lx"), B("pM", 0))
-    later([lambda e=e: red(col("Hc", e), B("pM", 2, e, 32, 2)) for e in range(2)] +
-          [lambda: ts(A("W0b"), A("Hc", 0, 2), -1.0 / 1024, op.mult, 137.0 - 511.5 / 1024, op.add),
-           lambda: ts(A("W0c", 0, 2), A("W0b"), -128.0, op.add)])
-    marks(0)
     base, thr = col("pC", 128), col("pC", 129)
     tt(A("J"), A("nM"), A("J"), op.mult)
     tt(A("nM"), A("S"), A("J"), op.add)
     ts(A("Pq"), A("S"), base, op.add, 1025.0, op.min)
     for m in range(4):
         ts(A("Lsc", 16 * m, 16 * m + 16), A("nM", m, 64, 4), thr, op.add, col("cf", 41), op.mult)
-    send([((r - 1) % 4, T.W0c[:, 0:2], T.w0l[:, 0:2], "aw0", 0, NE)], whole("W0c", 0, 2))
     tt(Ind(A("sw"), A("Lsc")), A("pg"), A("K"), op.max)
+    send([((r - 1) % 4, T.W0c[:, 0:2], T.w0l[:, 0:2], "aw0", 0, NE)], whole("W0c", 0, 2))
     for q in range(4):
         mm(B("pH", q >> 1, 64 * (q & 1), 64 * (q & 1) + 64), rep(q), A("Pq"), True, True, q == 3)
     act(A("Qw"), B("pH", (0, 2)), fn.Copy)
     for j in range(2, 6):
         exp_table("ad0", j, ["pW", "pN", "pF0", "pF1"][j - 2])
-    for q in [r] + oth:
+    for q in range(3):
         terms_gather(q)
     for c in range(16):
         mm(B("pM", 3, c, 96, 16), A("sw", 3072 + c, 5120, 16), A("Sel6", 0, 6), True, True, c == 15)
@@ -822,6 +850,7 @@ def rank_program(g, core, T, topo):
     keys = row_keys(T4, 4.0)
     tt(A("xo1"), A("xa"), A("xb"), op.add)
     tab(lambda q: rep(q, 1), A("R"), False, True)
+    terms_gather(3)
     x_table(0, "pY")
     x_table(1, "pC")
     ev = []
@@ -834,7 +863,6 @@ def rank_program(g, core, T, topo):
     run(ev)
     later([lambda: tt(A("uT", 128, 256), A("uT", 128, 256), A("prf"), op.add), lambda: tt(A("Tx"), A("tixf"), A("Tl"), op.max)], True)
     rot = ["pM", "pC", "pF0", "pF1", "pM", "pC"]
-    gap(HOT0)
     mode["far"] = FAR[3]
     fields(1, None, lambda: (new_x() if XDMA else x_table(2, "pY"), exp_table("ad0", 0, rot[0])))
     gap(HOT1)
@@ -845,7 +873,6 @@ def rank_program(g, core, T, topo):
     fresh.update({0: True, 1: True})
     draws(1, after(1))
     rest = drain()
-    row_lists(A("Tx"), "hi")
 
     def terms_add(q):
         v = A("V", 512 * q, 512 * q + 512)
@@ -854,20 +881,20 @@ def rank_program(g, core, T, topo):
     def terms():
         cp(A("Lx"), B("pM", 0))
         terms_add(oth[0])
-    count_tail(rest[:NV1], rest[NV1:], {min(2 * NV1, len(rest) - 1): terms})
+    count_tail(rest[:NV1], rest[NV1:], {TURN: lambda: row_lists(A("Tx"), "hi"), 2 * NV1: terms})
     act(A("tixf"), B("pM", 0), fn.Copy)
     act(A("prf"), B("pM", 1), fn.Identity, -0.5 - 64 * H0)
-    ybank = dict(zip(oth + [r], ["pY", "pF0", "pF1", "pY"]))
+    ybank = dict(zip(oth + [r], [A("pY", 0, 128), B("pF0", 0), B("pF1", 0), A("pY", 0, 128)]))
 
     def ye_sum(q):
-        terms_sum(q, True, True, A(ybank[q], 0, 128))
+        terms_sum(q, True, True, ybank[q])
 
     def ye_out(q, e):
         o = A("Ye", 128 * q, 128 * q + 128)
         if e == "a":
-            act(o, A(ybank[q], 0, 128), fn.Copy)
+            act(o, ybank[q], fn.Copy)
         else:
-            cp(o, A(ybank[q], 0, 128))
+            cp(o, ybank[q])
         if q != r:
             send([(q, T.Ye[:, 128 * q:128 * q + 128], T.yel[:, 128 * r:128 * r + 128], "ae%d" % r, 0, NE)], o[1])
     run(xs_[NX1:])
@@ -878,18 +905,18 @@ def rank_program(g, core, T, topo):
     mm(A("pC", 192, 256), A("OE"), A("Lv"), True, True)
     terms_add(oth[2])
     ye_sum(oth[1])
+    ye_sum(oth[2])
+    ye_out(oth[1], "a")
     red(col("Hc", 2), A("pC", 192, 256))
+    terms_add(r)
     ts(A("f1"), A("prf"), col("Hc", 2), op.is_ge, 4096.0, op.mult)
     tt(A("f1"), A("f1"), A("tixf"), op.max)
     cp(A("Ly"), A("f1"))
     bank = dict(zip(oth + [r], ["pW", "pH", "pN", "pM"]))
 
-    def last_gather(q, e):
-        o, s = A("G", 512 * q, 512 * q + 512), Ind(A("XN"), A("Ly", 32 * q, 32 * q + 32))
-        if e == "a":
-            act(o, s, fn.Identity, -4.0)
-        else:
-            ts(o, s, -4.0, op.add)
+    def last_gather(q):
+        ts(A("G", 512 * q, 512 * q + 256), Ind(A("XN"), A("Ly", 32 * q, 32 * q + 16)), -4.0, op.add)
+        act(A("G", 512 * q + 256, 512 * q + 512), Ind(A("XN"), A("Ly", 32 * q + 16, 32 * q + 32)), fn.Identity, -4.0)
         for u in range(4):
             mm(B(bank[q], 0), A("Yw", 3 - u, 131 - u), A("G", 512 * q + 128 * u, 512 * q + 128 * u + 128), u == 0, u == 3)
 
@@ -899,26 +926,21 @@ def rank_program(g, core, T, topo):
             act(o, B(bank[q], 0), fn.Identity, 16.0)
         else:
             ts(o, B(bank[q], 0), 16.0, op.add)
-    last_gather(oth[0], "v")
-    last_gather(oth[1], "a")
-    ye_out(oth[1], "a")
-    last_gather(oth[2], "v")
-    ye_sum(oth[2])
-    last_out(oth[0], "a")
+    ye_out(oth[2], "a")
+    for q in oth + [r]:
+        last_gather(q)
+    ye_sum(r)
+    last_out(oth[0], "v")
     last_out(oth[1], "a")
     send([(oth[j], T.Yx[:, 128 * oth[j]:128 * oth[j] + 128], T.yxl[:, 128 * r:128 * r + 128], "ax%d" % r, j * NE // 2, NE // 2)
           for j in range(2)], whole("Yx", 128 * oth[0], 128 * oth[0] + 128) + whole("Yx", 128 * oth[1], 128 * oth[1] + 128))
     last_out(oth[2], "v")
     send([(oth[2], T.Yx[:, 128 * oth[2]:128 * oth[2] + 128], T.yxl[:, 128 * r:128 * r + 128], "ax%d" % r, 0, NE)],
          whole("Yx", 128 * oth[2], 128 * oth[2] + 128))
-    terms_add(r)
-    last_gather(r, "a")
-    ye_out(oth[2], "v")
-    ye_sum(r)
     last_out(r, "a")
     ye_out(r, "v")
-    for q, out, s in (("s", "ye", frm[0]), ("s", "ye", frm[1]), ("a", "yx", r), ("s", "yx", frm[0]), ("a", "yx", frm[1]),
-                      ("s", "ye", r), ("a", "yx", frm[2]), ("s", "ye", frm[2])):
+    for q, out, s in (("s", "ye", frm[0]), ("s", "ye", frm[1]), ("a", "yx", r), ("s", "ye", r), ("s", "ye", frm[2]),
+                      ("a", "yx", frm[0]), ("s", "yx", frm[1]), ("a", "yx", frm[2])):
         n = {"ye": ("Ye", "yel"), "yx": ("Yx", "yxl")}[out][s != r]
         dma(q, T[out][32 * s:32 * s + 32, :], T[n][:, 128 * s:128 * s + 128], "sto", 8, [], whole(n, 128 * s, 128 * s + 128))
     for q in cnt:

from concourse.bass import DstId, RemoteDMATransfer
from concourse.mybir import AluOpType, AxisListType, ActivationFunctionType

F32, BF, F16, I32, U16 = "float32", "bfloat16", "float16", "int32", "uint16"
SCRATCH = {
    "zs": ("dram", [4, 128, 512], BF), "zl": ("dram", [4, 128, 512], BF),
    "nxs": ("dram", [4, 128, 96], I32), "nxl": ("dram", [4, 128, 96], I32), "nxd": ("dram", [384, 128], I32),
    "Xd": ("dram", [32, 3, 4, 256], F32),
}
for _n, _w, _d in [
    ("zw0", 5120, BF), ("zw1", 4096, BF), ("nxw", 4096, I32), ("HU", 384, I32), ("Hh", 384, F16), ("Hs", 384, F16),
    ("Hl", 384, F16), ("XS", 128, BF), ("XR", 128, BF),
    ("N0t", 16, I32), ("X0", 256, F32), ("xs", 256, BF), ("xo", 256, F16), ("xo1", 256, F16), ("xa", 256, F32), ("xb", 256, F32),
    ("ib", 10, I32), ("cf", 48, F32), ("XI", 176, BF), ("XD", 128, BF), ("XM", 144, BF),
    ("MA", 4, F32), ("MQ", 4, F32), ("OH", 16, F32), ("GM", 8, F32), ("Wd", 704, BF), ("XJ", 128, BF), ("Wq", 576, BF),
    ("Rep", 528, BF), ("Rep4", 512, BF), ("Sq", 512, BF), ("SelW", 32, BF), ("SelH", 32, BF), ("SelN", 32, BF), ("SelT", 8, BF),
    ("Sel6", 8, F32), ("Id", 1024, BF), ("Qw", 256, F32), ("msk", 2048, BF), ("Pm", 256, BF), ("Tri", 256, BF), ("OE", 128, BF), ("Yw", 132, BF), ("Yw32", 132, F32),
    ("Cb", 512, BF), ("ch", 4, F16), ("nxb", 256, I32), ("ni", 48, I32), ("nf", 32, F16), ("XQ", 128, BF),
    ("SN", 648, BF), ("p16", 20, F32), ("K1", 256, F32), ("K", 1024, F32), ("J", 64, F32), ("LS", 16, U16),
    ("LA", 64, U16), ("LN", 96, U16), ("R", 256, F16), ("d", 768, F16), ("ad0", 768, F16),
    ("ind", 768, BF), ("F", 1032, F32), ("G", 2048, F16), ("E", 4104, F32), ("XN", 4104, F32), ("V", 2048, F32),
    ("pg", 1024, F32), ("sw", 8192, F32), ("Ab", 8192, BF), ("Nb", 9216, BF),
    ("LT", 128, U16), ("Lp", 128, U16), ("Lx", 128, U16), ("Ly", 128, U16), ("Lsc", 64, U16),
    ("hi", 128, BF), ("aa", 128, BF), ("base", 128, BF), ("key", 128, BF), ("uT", 256, F32), ("f1", 128, F32),
    ("Tl", 128, F16), ("Tx", 128, F16), ("S4", 128, F16), ("eb", 128, F16), ("ec", 128, F16), ("Vs", 128, F16),
    ("P", 128, F16), ("t", 32, F32), ("cb", 512, BF), ("mb", 512, BF), ("tk", 384, F32),
    ("Cs", 64, F32), ("Mk", 64, BF), ("nM", 64, F32), ("S", 64, BF),
    ("Pq", 64, F16), ("Lv", 64, BF), ("zb", 1024, BF), ("Hc", 4, F32), ("W0b", 2, BF), ("W0c", 4, F32), ("w0l", 4, F32),
    ("tixf", 128, F32), ("prf", 128, F32), ("Ye", 512, F32), ("Yx", 512, F32), ("yel", 512, F32), ("yxl", 512, F32),
]:
    SCRATCH[_n] = ("sbuf", [128, _w], _d)
for _n in ["pY", "pC"]:
    SCRATCH[_n] = ("psum", [128, 512], F32)
for _n in ["pF0", "pF1"]:
    SCRATCH[_n] = ("psum", [128, 2, 256], F32)
for _n in ["pW", "pH", "pN", "pM"]:
    SCRATCH[_n] = ("psum", [128, 4, 128], F32)

SEMAPHORES = (["cv", "ca", "cp", "cg", "lsem", "dz", "dz2", "dn", "dh", "d0", "dx", "du", "wn0", "wn1", "wn1a", "wn1b", "wz1a", "wz1b", "Xda", "Xdb", "Xd1", "wz0", "wz1", "ah", "aw0", "sto"]
              + ["%s%d" % (a, b) for a in ("an", "az", "ae", "ax") for b in range(4)])
ROUND2 = 3.0 * 2 ** 23
H0 = 160.0
KT = 2 + 241 * H0
NF = 4
FAR = (0, 4, 4, 4)
EARLY = (48, 8, 30)
ACOL = ((20, 20, 20, 14), (20, 20, 20, 0))
FA = (64, 64)
NV1 = 17
HOT0, HOT1 = 8, 12
ZQ, ZG = ("avav", "avav"), 0
TURN = 2
XDMA = True
NX1 = 5


def rank_program(g, core, T, topo):
    r = T.rank_of(core)
    if r is None:
        return
    op = AluOpType
    fn = ActivationFunctionType
    Q = {"v": g.vector, "a": g.scalar, "p": g.tensor, "g": g, "s": g.sync}
    cnt = {"v": 0, "a": 0, "p": 0, "g": 0}
    seen = {q: {} for q in Q}
    hist = {}
    total = {}

    def A(name, c0=0, c1=None, st=1, p0=0, p1=128):
        t = T[name]
        if len(t.shape) == 3:
            return (t[p0:p1], [(name, p0, p1, 0, 512, 1)])
        if c1 is None:
            c1 = t.shape[1]
        ap = t[p0:p1, c0:c1] if st == 1 else t[p0:p1, c0:c1:st]
        return (ap, [(name, p0, p1, c0, c1, st)])

    def B(name, k, c0=0, c1=128, st=1, p0=0, p1=128):
        t = T[name]
        w = t.shape[2]
        if isinstance(k, tuple):
            return (t[p0:p1, k[0]:k[1], c0:c1], [(name, p0, p1, w * k[0] + c0, w * (k[1] - 1) + c1, 1)])
        ap = t[p0:p1, k, c0:c1] if st == 1 else t[p0:p1, k, c0:c1:st]
        return (ap, [(name, p0, p1, w * k + c0, w * k + c1, st)])

    def col(name, c, p0=0, p1=128):
        return A(name, c, c + 1, 1, p0, p1)

    def Ind(win, off):
        return (win[0].indirect(off[0]), win[1] + off[1], win[1], off[1])

    def wait(q, sem, val):
        if seen[q].get(sem, 0) < val:
            Q[q].wait_ge(T.sem[sem], val)
            seen[q][sem] = val

    pool = []
    mode = {"hold": None, "each": False, "far": 0}

    def meet(ra, rb):
        for (n, p0, p1, c0, c1, st) in ra:
            for (m, a0, a1, b0, b1, bs) in rb:
                if n == m and a0 < p1 and p0 < a1 and b0 < c1 and c0 < b1 and not (bs == st and (c0 - b0) % st != 0):
                    return True
        return False

    def clash(a, reads, writes):
        return meet(a[2], reads) or meet(a[2], writes) or meet(a[1], writes)

    def later(fs, front=False, tag=None):
        for j, f in enumerate(fs):
            mode["hold"] = []
            f()
            calls, mode["hold"] = mode["hold"], None
            e = (calls, [x for c in calls for x in c[2]], [x for c in calls for x in c[3] if tag is None or x[0] != "pC"], tag)
            pool.insert(j if front else len(pool), e)

    def emit(j):
        for c in pool.pop(j)[0]:
            put(*c)

    def force(reads, writes):
        j = 0
        while j < len(pool):
            if clash(pool[j], reads, writes):
                e = pool[j]
                first = [i for i in range(j) if clash(pool[i], e[1], e[2])]
                emit(first[0] if first else j)
                j = 0
            else:
                j += 1

    def gap(n=1, wait_ok=False):
        while n > 0 and pool:
            for j, e in enumerate(pool[:24]):
                c = e[0][0]
                need = needs("v", c[2], c[3])
                free = all(seen["v"].get(s, 0) >= v or (s == "cv" and v <= cnt["v"] - NF) for s, v in need.items())
                if free and not any(clash(pool[i], e[1], e[2]) for i in range(j)):
                    break
            else:
                if not wait_ok:
                    return
                j = 0
            emit(j)
            n -= 1

    def deps(q, reads, writes, skip=None):
        for sem, val in needs(q, reads, writes, skip).items():
            wait(q, sem, val)

    def needs(q, reads, writes, skip=None):
        need = {}
        for regs, w in ((reads, False), (writes, True)):
            for (n, p0, p1, c0, c1, st) in regs:
                ps = SCRATCH[n][0] == "psum"
                for key, (sem, val) in hist.get(n, {}).items():
                    rq, rw, a0, a1, b0, b1, bs = key
                    if (rq == "p" and q == "p") or sem == skip:
                        continue
                    apart = bs == st and (c0 - b0) % st != 0
                    if (ps and rq != q) or ((w or rw) and a0 < p1 and p0 < a1 and b0 < c1 and c0 < b1 and not apart):
                        need[sem] = max(need.get(sem, 0), val)
        return need

    def note(q, reads, writes, sem, val):
        for regs, w in ((reads, False), (writes, True)):
            for (n, p0, p1, c0, c1, st) in regs:
                hist.setdefault(n, {})[(q, w, p0, p1, c0, c1, st)] = (sem, val)

    def issue(q, call, outs, ins, inc=True):
        reads, writes = [], []
        for x in ins:
            if isinstance(x, tuple):
                reads += x[1]
        for x in outs:
            if len(x) == 4:
                writes += x[2]
                reads += x[3]
            else:
                writes += x[1]
        if mode["hold"] is not None:
            mode["hold"].append((q, call, reads, writes, inc))
            return
        if q == "v" and mode["each"]:
            pool.append(([(q, call, reads, writes, inc)], reads, writes, None))
            return
        force(reads, writes)
        if q == "v":
            need = {s: v for s, v in needs(q, reads, writes).items() if seen[q].get(s, 0) < v}
            gap(max([NF - (cnt[q] - need["cv"]) if "cv" in need else 0] + [mode["far"] for s in need if s != "cv"]))
        put(q, call, reads, writes, inc)

    def put(q, call, reads, writes, inc):
        deps(q, reads, writes)
        ins_ = call()
        note(q, reads, writes, "c" + q, cnt[q] + 1)
        if inc:
            ins_.then_inc(T.sem["c" + q], 1)
            cnt[q] += 1

    def raw(x):
        return x[0] if isinstance(x, tuple) else x

    def ts(out, in0, s1, o0, s2=None, o1=None):
        if o1 is None:
            issue("v", lambda: g.vector.tensor_scalar(out[0], in0[0], raw(s1), None, o0), [out], [in0, s1])
        else:
            issue("v", lambda: g.vector.tensor_scalar(out[0], in0[0], raw(s1), raw(s2), o0, o1), [out], [in0, s1, s2])

    def tt(out, a, b, o):
        issue("v", lambda: g.vector.tensor_tensor(out[0], a[0], b[0], o), [out], [a, b])

    def cp(out, a):
        issue("v", lambda: g.vector.tensor_copy(out[0], a[0]), [out], [a])

    def ms(out, val):
        issue("v", lambda: g.vector.memset(out[0], val), [out], [])

    def red(out, a):
        issue("v", lambda: g.vector.tensor_reduce(out[0], a[0], AxisListType.X, op.add), [out], [a])

    def scan(out, d0, d1, o0):
        issue("v", lambda: g.vector.tensor_tensor_scan(out[0], d0[0], d1[0], 0.0, o0, op.add), [out], [d0, d1])

    def act(out, a, f, bias=None, scale=None):
        kw = {}
        if bias is not None:
            kw["bias"] = raw(bias)
        if scale is not None:
            kw["scale"] = raw(scale)
        issue("a", lambda: g.scalar.activation(out[0], a[0], f, **kw), [out], [a, bias, scale])

    def mm(out, l, rhs, start, stop, inc=None):
        issue("p", lambda: g.tensor.matmul(out[0], l[0], rhs[0], start, stop), [out], [l, rhs], stop if inc is None else inc)

    def iota(out, pat, base, cm):
        if SCRATCH[out[1][0][0]][2] == I32:
            issue("g", lambda: g.iota(out[0], pat, base, cm), [out], [])
        else:
            issue("g", lambda: g.iota(out[0], pat, base, cm, allow_small_or_imprecise_dtypes=True), [out], [])

    def asel(out, a, pat, o, base, cm, fl=0.0):
        issue("g", lambda: g.affine_select(out[0], a[0], pat, o, fl, base, cm), [out], [a])

    def dma(q, out, in_, sem, n, wr=(), rd=()):
        force(list(rd), list(wr))
        deps(q, list(rd), list(wr), sem)
        Q[q].dma_start(out, in_).then_inc(T.sem[sem], 16)
        total[sem] = 16 * n
        note("d" + sem, list(rd), list(wr), sem, 16 * n)

    def landed(regs, sem, val):
        total[sem] = val
        note("x" + sem, [], regs, sem, val)

    def whole(n, c0=0, c1=None):
        return [(n, 0, 128, c0, T[n].shape[-1] if c1 is None else c1, 1)]

    def slot(n, s):
        return [(n, 128 * s, 128 * s + 128, 0, 1, 1)]

    def send(items, rd):
        force(rd, [])
        deps("g", rd, [])
        tr = []
        for (q, src, dst, sem, e0, ne) in items:
            eng = topo.engines(core, T.cores[q])
            m = 0
            for e in eng[e0:e0 + ne]:
                m |= 1 << e
            rid, pid, se = topo.addr(T.cores[q])
            tr.append((rid, pid, m, src, dst, sem))
            total["lsem"] = total.get("lsem", 0) + ne
        if len(tr) == 1:
            rid, pid, m, src, dst, sem = tr[0]
            g.remote_dma(dst, src, T.sem[sem], T.sem.lsem, pid, rid, m)
        else:
            g.remote_dma_fused([RemoteDMATransfer(dst_ids=[DstId(rid=rid, pnc=pid)], dma_engine_mask=m, remote_sem=T.sem[sem],
                                                  src=src, dst=dst) for (rid, pid, m, src, dst, sem) in tr], local_sem=T.sem.lsem)

    NE = len(topo.engines(core, T.cores[(r + 1) % 4]))
    oth = [(r + 1) % 4, (r + 2) % 4, (r + 3) % 4]
    frm = [(r - 1) % 4, (r - 2) % 4, (r - 3) % 4]
    split3 = [(0, NE // 2), (NE // 2, NE // 4), (3 * NE // 4, NE // 4)]
    eng3 = [NE // 2, NE // 4, NE // 4]
    engz = [NE // 2, NE // 2, NE]
    EA = [(e, a) for a in range(4) for e in range(2)]

    def send3(src, dst, w, sem):
        send([(oth[j], T[src][:, w * oth[j]:w * oth[j] + w], T[dst][:, w * r:w * r + w], sem, split3[j][0], split3[j][1])
              for j in range(3)], whole(src))

    def run(L):
        for f in L:
            f()

    if r < 2:
        dma("s", T.nxd[:], T.nx[:], "dn", 1, slot("nxs", 0))
    dma("a", T.HU[:, 0:128], T.hyp[:], "dh", 1, whole("HU", 0, 128))
    if r < 2:
        dma("s", T.zs[oth[0]:oth[0] + 2], T.z[32 * oth[0]:32 * oth[0] + 64, :], "dz", 1, slot("zs", 0))
        dma("a", T.zs[oth[2]], T.z[32 * oth[2]:32 * oth[2] + 32, :], "dz2", 1, slot("zs", 1))
    else:
        dma("s", T.nxs[:], T.nx[:], "dn", 1, slot("nxs", 0))
    dma("s", T.X0[:], T.x0[32 * r:32 * r + 32, :], "dx", 1, whole("X0"))
    dma("a", T.HU[:, 128:384], T.uu[:], "du", 1, whole("HU", 128, 384))
    dma("s", T.N0t[:], T.n0[2 * r:2 * r + 2, :], "d0", 1, whole("N0t"))
    if r < 2:
        dma("a", T.nxb[:, 128 * r:128 * r + 128], T.nx[6 * r:6 * r + 8, :], "wn0", 1, whole("nxb", 128 * r, 128 * r + 128))
        dma("s", T.zb[:, 512 * r:512 * r + 512], T.z[32 * r:32 * r + 32, :], "wz0", 1, whole("zb", 512 * r, 512 * r + 512))
    else:
        dma("a", T.zs[:], T.z[:], "dz", 1, slot("zs", 0) + slot("zs", 1))

    def double(w, p0, st, sem):
        for j, n in enumerate((16, 32)):
            for e in range(2):
                p = 64 * e + p0
                dma("s", T[w][p + n:64 * e + 2 * n:st, :], T[w][p:64 * e + n:st, :], sem + "ab"[j], 2, whole(w), whole(w))

    def zhop():
        for s in [x for x in [r] + frm if x >= 2]:
            for e in range(2):
                src = T.z[32 * r + 16 * e:32 * r + 16 * e + 16, :] if s == r else T.zl[s, 64 * e:64 * e + 64]
                dma("s", T.zw1[64 * e:64 * e + 16, 2048 * (s & 1):2048 * (s & 1) + 2048], src, "wz1", 4, whole("zw1"),
                    [] if s == r else slot("zl", s))
        double("zw1", 0, 1, "wz1")

    def nxhop():
        for s in [x for x in [r] + frm if x >= 2]:
            for e in range(2):
                src = T.nx[6 * r + 3 * e:6 * r + 3 * e + 3, :] if s == r else T.nxl[s, 64 * e:64 * e + 64]
                dma("s", T.nxw[64 * e + 1:64 * e + 13:4, 2048 * (s & 1):2048 * (s & 1) + 2048], src, "wn1", 4,
                    whole("nxw"), [] if s == r else slot("nxl", s))
        double("nxw", 1, 4, "wn1")

    for j, s in enumerate(frm):
        landed(slot("nxl", s) if s >= 2 else whole("nxb", 128 * s, 128 * s + 128), "an%d" % s, eng3[j])
        landed(slot("zl", s) if s >= 2 else whole("zb", 512 * s, 512 * s + 512), "az%d" % s, engz[j])
        landed(whole("yel", 128 * s, 128 * s + 128), "ae%d" % s, NE)
        landed(whole("yxl", 128 * s, 128 * s + 128), "ax%d" % s, engz[j])
        landed(whole("Hl", 96 * s, 96 * s + 96), "ah", NE)
    landed(whole("w0l"), "aw0", NE)

    Zb, One, Neg, Qrt = [A("Cb", 128 * j, 128 * j + 128) for j in range(4)]
    iota(col("ib", 8), [[0, 1]], 0, 1)
    iota(A("XI"), [[1, 176]], 0, 0)
    row0 = 6 * r - min(6 * r, 16)
    for e in range(2):
        c0, c1 = ((0, row0 + 3), (row0 + 3, 8))[e]
        iota(A("XJ", 16 * c0, 16 * c1), [[0, c1 - c0], [1, 16]], 64 * e, 0)
    for e in range(2):
        iota(A("XQ", 64 * e, 64 * e + 64), [[0, 4], [16, 4], [1000, 4]], 48 * e + 16 * row0, 0)
    iota(A("XS"), [[64, 2], [0, 4], [4, 16]], 0, 0)
    iota(A("XD"), [[1, 128]], 0, -1)
    iota(A("XR"), [[64, 2], [0, 4], [1, 16]], 0, 0)
    mode["each"] = True
    ms(One, 1.0)
    ms(Zb, 0.0)
    ms(Neg, -1.0)
    P0 = col("ib", 8)
    ts(col("ib", 0), P0, 15, op.bitwise_and)
    ts(col("ib", 1), P0, 5, op.arith_shift_right)
    ts(col("ib", 2), P0, 16, op.bitwise_and)
    ts(col("ib", 3), P0, 6, op.arith_shift_right)
    ts(col("ib", 4), P0, 4, op.arith_shift_right, 3, op.bitwise_and)
    ts(col("ib", 5), P0, 112, op.bitwise_and)
    ts(col("ib", 6), P0, 63, op.bitwise_and)
    ts(col("ib", 7), P0, 3, op.arith_shift_right, 4, op.bitwise_and)
    cp(A("cf", 0, 8), A("ib", 0, 8))
    ci, ce, ca = col("cf", 0), col("cf", 3), col("cf", 4)
    cp(col("cf", 47), P0)
    ts(col("cf", 8), col("cf", 2), 4.0, op.mult, ci, op.add)
    ts(A("MQ"), A("XI", 0, 4), col("cf", 1), op.is_equal)
    ts(col("cf", 9), col("cf", 8), 48.0, op.add)
    ts(A("OH"), A("XI", 0, 16), ci, op.is_equal)
    for q in oth + [r]:
        ts(A("Wd", 176 * q, 176 * q + 176), A("XI"), col("cf", 9), op.is_equal, col("MQ", q), op.mult)
    ts(A("p16", 0, 16), A("XI", 0, 16), -1.0, op.mult, col("cf", 47), op.add)
    ms(A("Rep"), 0.0)
    ms(A("XM", 0, 16), 99.0)
    ts(A("p16", 16, 20), A("XI", 0, 4), -16.0, op.mult, col("cf", 47), op.add)
    ts(col("cf", 14), col("cf", 5), 1.0 / 16, op.mult, float(-row0), op.add)
    for a in range(4):
        ts(A("SN", 128 * a, 128 * a + 128), A("XJ"), col("p16", 16 + a), op.is_equal)
    ts(A("SN", 512, 640), A("XQ"), col("cf", 5), op.is_equal)
    ts(A("SN", 640, 646), A("XI", 0, 6), col("cf", 14), op.is_equal)

    for cq in range(4):
        ts(A("Sq", 128 * cq, 128 * cq + 128), A("XS"), col("p16", cq), op.is_equal)

    def lists_out():
        for kind in range(3):
            cp(A("Hh", kind, 384, 3), A("HU", 128 * kind, 128 * kind + 128))
        for q in oth + [r]:
            for k in range(4):
                mm(A("pY", 96 * q, 96 * q + 96), A("Wd", 176 * q + 48 - 16 * k, 176 * q + 176 - 16 * k), A("Hh", 96 * k, 96 * k + 96),
                   k == 0, k == 3)
        cp(A("xs"), A("X0"))
        cp(A("Hs"), A("pY", 0, 384))

    def send_z():
        dst = T.zl[r] if r >= 2 else T.zb[:, 512 * r:512 * r + 512]
        send([(oth[j], T.zs[oth[j]], dst, "az%d" % r, j * NE // 2, NE // 2) for j in range(2)], slot("zs", 0))
        send([(oth[2], T.zs[oth[2]], dst, "az%d" % r, 0, NE)], slot("zs", 1))

    def send_nx():
        send([(oth[j], T.nxs[oth[j]] if r >= 2 else T.nxd[min(96 * oth[j], 256):min(96 * oth[j], 256) + 128, :],
               T.nxl[r] if r >= 2 else T.nxb[:, 128 * r:128 * r + 128], "an%d" % r, split3[j][0], split3[j][1]) for j in range(3)], slot("nxs", 0))

    def writes_out():
        send_nx()
        if r < 2:
            send_z()
        iota(A("XM", 16, 144), [[1, 2], [0, 4], [100, 16]], 0, 0)
        iota(A("K1"), [[1, 16], [16, 16]], 0, 0)
        send3("Hs", "Hl", 96, "ah")
        iota(A("nxw", 0, 2048), [[1, 2048]], 0, 0)
        iota(A("nxw", 2048, 4096), [[1, 2048]], 2048, 0)
        for j, c in enumerate((One, Neg)):
            asel(A("Tri", 128 * j, 128 * j + 128), c, [[1, 128]], op.is_gt, 0, -1)
        for j in range(2):
            asel(A("Tri", 128 * j, 128 * j + 128), A("Tri", 128 * j, 128 * j + 128), [[-64, 2], [0, 64]], op.is_ge, 0, 1)
        if r >= 2:
            deps("g", whole("zb"), [])
            send_z()
        iota(A("sw", 3072, 5120), [[0, 2048]], 0, 0)

    def Id(j):
        return A("Id", 128 * j, 128 * j + 128)

    def rep(q, shift=0):
        return A("Rep", 132 * q + 1 + shift, 132 * q + 129 + shift)

    def half(b, u):
        if len(T[b].shape) == 2:
            return A(b, 256 * u, 256 * u + 256)
        return B(b, (2 * u, 2 * u + 2)) if T[b].shape[2] == 128 else B(b, u, 0, 256)

    def zspread(s, qs, banks=("pW", "pH", "pN", "pY")):
        def out(cq):
            o = A("zw0", 2048 * s + 512 * cq, 2048 * s + 512 * cq + 512)
            if qs[cq] == "a":
                act(o, A(banks[cq]), fn.Copy)
            else:
                cp(o, A(banks[cq]))
        for cq in range(4):
            mm(A(banks[cq]), A("Sq", 128 * cq, 128 * cq + 128), A("zb", 512 * s, 512 * s + 512), True, True)
        return [lambda cq=cq: out(cq) for cq in range(4)]

    def prepare():
        for cq in range(4):
            mm(half("pF%d" % (cq >> 1), cq & 1), A("Sq", 128 * cq, 128 * cq + 128), A("xs"), True, True, cq & 1 == 1)
        for h in range(2):
            act(A("zw0", 4096 + 512 * h, 4608 + 512 * h), A("pF%d" % h), fn.Copy)
        ts(A("ni", 0, 16), A("N0t"), 4, op.arith_shift_right, 128, op.bitwise_and)
        ts(A("ni", 16, 32), A("N0t"), 127, op.bitwise_and)
        ts(A("ni", 32, 48), A("N0t"), 7, op.arith_shift_right, 15, op.bitwise_and)
        cp(A("LA", 0, 16), A("N0t"))
        cp(A("Hl", 96 * r, 96 * r + 96), A("Hs", 96 * r, 96 * r + 96))
        tt(A("nf", 0, 16), A("ni", 0, 16), A("ni", 16, 32), op.add)
        cp(A("nf", 16, 32), A("ni", 32, 48))
        for a in range(4):
            mm(A("pC", a, 128, 4), A("SN", 128 * a, 128 * a + 128), A("nf"), True, True, a == 3)
        cp(A("Lp"), A("pC", 0, 128))
        act(A("msk", 0, 1024), Ind(A("OH"), A("Lp", 64, 128)), fn.Copy)
        if r < 2:
            ts(A("xa", 128 * r, 128 * r + 128), A("nxb", 128 * r, 128 * r + 128), -2047.0, op.add)
            run(zspread(r, "aaaa"))
        nxhop()
        act(A("xo"), Ind(A("zw0", 4096, 5120), A("LS")), fn.Copy)
    ts(col("cf", 10), ca, 32.0, op.mult, ce, op.add)
    ts(col("cf", 12), ca, 2.0, op.mult, ce, op.add)
    ts(A("MA"), A("XI", 0, 4), ca, op.is_equal)
    ts(col("cf", 11), ci, 2.0, op.mult, col("cf", 10), op.add)
    for j, v in enumerate((1.0, 4.0, 64.0, 240.0, 1024.0, 0.25, -16.0, -1024.0)):
        ts(Id(j), A("XD"), 0.0, op.is_equal, v, op.mult)
    ts(A("Pm", 0, 128), A("XI", 0, 128), col("cf", 11), op.is_equal)
    ts(A("Pm", 128, 256), A("XI", 0, 128), col("cf", 11), op.is_equal, 4.0, op.mult)
    ts(A("GM"), A("XI", 0, 8), col("cf", 12), op.is_equal)
    for q in range(4):
        ts(rep(q), A("XR"), col("p16", 16 + q), op.is_equal)
    ts(col("cf", 13), col("cf", 6), 16.0, op.mult)
    ts(col("cf", 15), ca, 256.0, op.mult, 4096.0, op.add)
    tt(col("cf", 16), col("OH", 13), col("OH", 14), op.add)
    ts(A("LS"), A("XI", 0, 16), col("cf", 13), op.add)
    tt(col("cf", 17), col("cf", 15), col("cf", 16), op.mult)
    tt(col("cf", 18), col("cf", 15), col("OH", 14), op.mult)
    red(col("cf", 19), A("OH", 0, 12, 4))
    red(col("cf", 20), A("OH", 1, 12, 4))
    red(col("cf", 21), A("OH", 6, 16, 4))
    ts(col("cf", 22), col("cf", 19), -2047.0, op.mult)
    ts(col("cf", 23), col("cf", 21), -4.0, op.mult, col("OH", 3), op.add)
    ts(col("cf", 27), col("cf", 20), -2047.0, op.mult)
    tt(col("cf", 24), col("cf", 23), col("cf", 22), op.subtract)
    ts(col("cf", 25), col("OH", 2), 2.0, op.mult, col("cf", 24), op.add)
    cGa = col("cf", 22)
    cEv = [col("cf", 25), col("cf", 26)]

    def fixed():
        act(A("K", 0, 256), A("K1"), fn.Identity, col("cf", 17), col("cf", 16))
        for m in range(1, 4):
            act(A("K", 256 * m, 256 * m + 256), A("K1"), fn.Identity, col("cf", 18), col("OH", 14))

    def sels():
        c = 28
        L = [lambda: scan(A("cf", c, c + 4), A("Cb", 128, 132), A("OH", 2, 16, 4), op.mult),
             lambda: tt(A("cf", c + 4, c + 8), A("cf", c, c + 4), A("OH", 2, 16, 4), op.subtract),
             lambda: ts(A("cf", c + 4, c + 8), A("cf", c + 4, c + 8), col("MA", 0), op.mult),
             lambda: tt(A("cf", c, c + 4), A("cf", c + 4, c + 8), A("OH", 2, 16, 4), op.add),
             lambda: tt(col("cf", c + 8), col("OH", 8), col("OH", 4), op.subtract),
             lambda: tt(col("cf", c + 9), col("OH", 4), col("OH", 0), op.subtract),
             lambda: ts(col("cf", c + 10), col("OH", 3), 2048.0, op.mult, col("OH", 0), op.add),
             lambda: ts(col("cf", c + 11), col("OH", 3), -2048.0, op.mult),
             lambda: ms(A("SelN"), 0.0), lambda: ms(A("eb"), 1.0), lambda: ms(A("ec"), 1.0), lambda: ms(A("cb"), 0.0),
             lambda: ms(A("S4"), 1.0), lambda: ms(A("S4", 0, 128, 4), 0.0)]
        for s in range(4):
            L.append(lambda s=s: ts(A("SelW", s, 32, 4), A("GM"), col("cf", c + s), op.mult))
            L.append(lambda s=s: ts(A("SelH", s, 32, 4), A("GM"), col("cf", c + 8 + s), op.mult))
            if s:
                L.append(lambda s=s: ts(A("SelN", s, 32, 4), A("GM"), col("OH", 4 * s - 4), op.mult))
        return L
    run(sels())
    mode["each"] = False

    def row_keys(src, off):
        act(A("hi"), src, fn.Identity, H0 - (30 + off) / 64, 1.0 / 64)
        act(A("aa"), src, fn.Identity, H0 - (510 + off) / 1024, 1.0 / 1024)
        act(A("f1"), A("hi"), fn.Identity, 64 * H0 + 0.5 - off, -64.0)
        return lambda: tt(A("base"), src, A("f1"), op.add)

    def turn(k, terms, first=None):
        if first:
            mm(B("pM", k), first[0], first[1], True, False)
        for e in range(2):
            for j, (name, c0, st, ident) in enumerate(terms):
                last = j == len(terms) - 1
                mm(B("pM", k, 0, 128, 1, 64 * e, 64 * e + 64), A(name, c0 + e * st // 2, T[name].shape[1], st), Id(ident),
                   j == 0 and not first, last, last and e == 1)

    def track_list(t):
        turn(2, [("base", 0, 2, 1), ("hi", 0, 2, 0), ("aa", 0, 2, 3)])
        s, c = (col("cf", 41), col("cf", 42)) if t else (1.0, -KT)
        return lambda: (ts(A("LT"), B("pM", 2), s, op.mult, c, op.add), ts(A("Tl"), B("pM", 2), s, op.mult, c, op.add))

    def hot(v0, v1):
        return [lambda v=v: ts(A("Ab", 128 * v, 128 * v + 128), A("hi"), H0 + v, op.is_equal) for v in range(v0, v1)]

    def clear(bank, n=512, stop=False):
        mm(A(bank, 0, n), Zb, A("Wq", 0, n), True, stop, False)

    def tab(lhs, src, last, first=False):
        for q in range(4):
            mm(half("pF%d" % (q >> 1), q & 1), lhs(q), src, first and (q & 1) == 0, last and (q & 1) == 1)

    def gates(t, lst, xo, pause=None, pause2=None):
        zw = A("zw%d" % t, 0, 4096)

        def near(m):
            s = (256 * m, 256 * m + 256)
            ts(A("ind", *s), A("d", *s), ROUND2, op.add, ROUND2, op.is_equal)
            f = 6 + 4 * m
            tab(lambda q: A("Wq", 144 * q + 16 - f, 144 * q + 144 - f), A("ind", *s), m == 2)
        for m in range(3):
            tt(A("d", 256 * m, 256 * m + 256), Ind(zw, lst(m)), xo, op.subtract)
            if m:
                near(m - 1)
            elif pause:
                pause()
        if pause2:
            pause2()
        near(2)

    def fields(t, pause=None, pause2=None):
        act(A("F", 0, 512), A("pF0"), fn.Relu, cEv[t])
        ts(A("F", 512, 1024), A("pF1"), cEv[t], op.add, 0.0, op.max)
        if pause:
            pause()
        n = FA[t]
        act(A("G", 0, 16 * n), Ind(A("F"), A("LT", 0, n)), fn.Identity, cGa)
        ts(A("G", 16 * n, 2048), Ind(A("F"), A("LT", n, 128)), cGa, op.add)
        if pause2:
            pause2()
        for n, s in (("pW", "SelW"), ("pH", "SelH"), ("pN", "SelN")):
            for i in range(16):
                mm(B(n, (0, 4), 8 * i, 8 * i + 8), A("G", i, 2048, 16), A(s), True, True, i == 15)

    def exp_table(ad, j, b):
        m, h = j >> 1, j & 1
        for u in range(2):
            mm(half(b, u), rep(2 * h + u), A(ad, 256 * m, 256 * m + 256), True, True, u == 1)
        o = 1024 * (m + 1) + 512 * h
        act(A("E", o, o + 512), A(b), fn.Exp, None, -1.0)

    def repeat(src, w, d, dst, c0):
        for e in range(2):
            for a in range(4):
                p = 64 * e + 16 * a
                dma("s", T[d][16 * e:16 * e + 16, :, a, :], T[src][p:p + 16, 0:w], d + "ab"[e], 4, slot(d, e), whole(src, 0, w))
        for e in range(2):
            for k in range(4):
                p = 64 * e + 16 * k
                dma("s", T[dst][p:p + 16, c0:c0 + 4 * w], T[d][16 * e:16 * e + 16], d + "1", 8, whole(dst, c0, c0 + 4 * w), slot(d, e))

    def new_x():
        for m in range(3):
            o = half(["pY", "pF0"][m >> 1], m & 1)
            mm(o, Id(0), A("xo1"), True, False)
            mm(o, Id(5), A("d", 256 * m, 256 * m + 256), False, True)
        if XDMA:
            act(A("pg", 0, 512), A("pY"), fn.Copy)
            act(A("pg", 512, 768), half("pF0", 0), fn.Copy)
            repeat("pg", 768, "Xd", "XN", 1024)

    def x_table(j, b):
        m, h = j >> 1, j & 1
        for u in range(2):
            q = 2 * h + u
            mm(half(b, u), rep(q), A("xo1"), True, m == 0, m == 0 and u == 1)
            if m:
                mm(half(b, u), A("Rep4", 128 * q, 128 * q + 128), A("d", 256 * m - 256, 256 * m), False, True, u == 1)
        act(A("XN", 512 * j, 512 * j + 512), A(b), fn.Copy)

    def steps(q, c):
        o = A("Nb", 72 * c, 72 * c + 65)
        kc = col("key", c) if c < 96 else col("mb", 4 * c + 3)
        if q == "a":
            act(o, A("XI", 0, 65), fn.Sign, kc, -1.0)
        else:
            ts(o, A("XI", 0, 65), kc, op.is_le, 2.0, op.mult)

    def count(c, last=False):
        e = c & 1
        o, a, b = A("pC", 0, 65, 1, 64 * e, 64 * e + 64), A("Ab", c, 8192, 128), A("Nb", 72 * c, 72 * c + 65)
        issue("p", lambda: g.tensor.matmul(o[0], a[0], b[0], fresh.pop(e, False), last), [o], [a, b], last)
    fresh = {0: True, 1: True}

    def draws(t, after):
        def differ(o, j, k):
            return [lambda f=f: tt(A(o, f, 128, 4), B("pN", k, f, 128, 4), A("tk", 128 * j + 3, 128 * j + 128, 4), op.not_equal) for f in (1, 2, 3)]
        later([lambda: cp(A("cb", 384, 512, 4), A("base", 96, 128))], True)
        for k in range(4):
            def Pm(m):
                return B("pW", 0, m, 128, 4) if k == 0 else A("P", m, 128, 4)
            if k:
                own = []
                for k2 in range(k + 1, 4):
                    own.extend(differ("ec", k - 1, k2) + [lambda k2=k2: tt(B("pW", k2), B("pW", k2), A("ec"), op.mult)])
                run(differ("eb", k - 1, k))
                key(k - 1)
                after(k - 1)
                later(own, True)
                tt(A("Vs"), B("pW", k), A("eb"), op.mult)
                scan(A("P"), A("S4"), A("Vs"), op.mult)
            tt(A("t"), Pm(3), A("uT", 128 * t + 32 * k, 128 * t + 32 * k + 32), op.mult)
            for m in range(3):
                tt(A("cb", 128 * k + 3 - m, 128 * k + 128, 4), A("t"), Pm(m), op.is_ge)
            ck = A("cb", 128 * k, 128 * k + 128)
            if k < 3:
                scan(A("tk", 128 * k, 128 * k + 128), ck, B("pH", k), op.mult)
            scan(A("mb", 128 * k, 128 * k + 128), A("S4"), ck, op.mult)
        later([lambda: cp(A("key", 96, 128), A("mb", 387, 512, 4))], True)

    def key(k):
        tt(A("key", 32 * k, 32 * k + 32), A("mb", 128 * k + 3, 128 * k + 128, 4), A("base", 32 * k, 32 * k + 32), op.add)

    def row_lists(Tx, up):
        turn(0, [("key", 0, 2, 4), ("base", 0, 2, 7)], (Id(0), Tx))
        turn(1, [("key", 0, 2, 0), (up, 0, 2, 2)])

    def count_tail(cv_, ca_, between):
        order = []
        while cv_ or ca_:
            for q, L in (("v", cv_), ("a", ca_)):
                if L:
                    order.append((q, L.pop(0)))
        ends = [[c for (q, c) in order if c & 1 == e][-1] for e in range(2)]
        for n, (q, c) in enumerate(order):
            steps(q, c)
            if n in between:
                between[n]()
            count(c, c in ends)

    def marks(t, pause=None, early=None):
        cp(A("Cs"), A("pC", 1, 65))
        tt(A("Mk"), A("pC", 0, 64), A("Cs"), op.is_gt)
        if t == 0:
            tt(A("nM"), A("pC", 0, 64), A("Cs"), op.is_le)
        if early:
            early()
        scan(A("S"), A("Mk"), A("Cb", 0, 64), op.add)
        if t == 0:
            mm(col("pC", 128), A("Tri", 0, 128), col("S", 63), True, True, False)
            mm(col("pC", 129), A("Tri", 0, 128), col("S", 63), True, False)
            mm(col("pC", 129), Id(4), col("ch", 1), False, False)
            mm(col("pC", 129), Id(0), col("ch", 2), False, True)
        else:
            mm(col("pC", 129), A("Tri", 128, 256), col("S", 63), True, False)
            mm(col("pC", 129), Id(0), col("ch", 0), False, True)
        if pause:
            pause()

    def terms_gather(q):
        act(A("V", 512 * q, 512 * q + 512), Ind(A("E"), A("Lx", 32 * q, 32 * q + 32)), fn.Copy)

    def terms_sum(q, last=False, first=False, out=None):
        for u in range(4):
            mm(out or A("pY", 128 * q, 128 * q + 128), A("Yw32", 3 - u, 131 - u), A("V", 512 * q + 128 * u, 512 * q + 128 * u + 128),
               first and u == 0, last and u == 3, u == 3)

    nxw = A("nxw")
    T4 = B("pM", (0, 4), 0, 32)
    if not XDMA:
        later([lambda q=q: ts(A("Rep4", 128 * q, 128 * q + 128), A("XR"), col("p16", 16 + q), op.is_equal, 0.25, op.mult) for q in range(4)])
    later([lambda: ts(col("cf", 40), col("cf", 6), -64.0, op.mult, 4096.0, op.add),
                 lambda: ts(col("cf", 41), ce, 2.0, op.mult, -1.0, op.add),
                 lambda: ts(col("cf", 42), ce, -1023 - 2 * KT, op.mult, 1023 + KT, op.add),
                 lambda: ts(A("J"), A("XI", 0, 64), -1.0, op.mult, col("cf", 40), op.add),
                 lambda: ms(col("ch", 0), 1025.0), lambda: ms(A("F", 1024, 1032), 1.0),
                 lambda: ts(col("ch", 1), ce, 8.0, op.mult, -4.0, op.add), lambda: ts(col("ch", 2), ce, -1.0, op.mult),
                 lambda: cp(A("Sel6", 0, 3), A("OH", 1, 12, 4)),
                 lambda: cp(col("Sel6", 3), col("OH", 14)), lambda: cp(col("Sel6", 4), col("OH", 13)), lambda: cp(col("Sel6", 5), col("OH", 12)),
                 lambda: ts(col("cf", 45), ce, 64.0, op.mult, 3.0, op.add),
                 lambda: ts(A("SelT"), A("GM"), 4.0, op.mult),
                 lambda: ts(col("cf", 46), ci, 4.0, op.mult, col("cf", 45), op.add),
                 lambda: ms(A("E", 4096, 4104), 0.0), lambda: ms(A("XN", 4096, 4104), 0.0), lambda: ms(A("OE"), 0.0),
                 lambda: ts(A("Yw32"), A("XI", 0, 132), col("cf", 46), op.is_equal),
                 lambda: ts(A("Yw"), A("XI", 0, 132), col("cf", 46), op.is_equal),
                 lambda: ms(A("OE", 0, 64, 1, 0, 64), 1.0), lambda: ms(A("OE", 64, 128, 1, 64, 128), 1.0)])
    gap(EARLY[0], True)
    mode["far"] = EARLY[1]
    lists_out()
    writes_out()
    prepare()
    later([lambda q=q: ts(A("Wq", 144 * q, 144 * q + 144), A("XM"), ce, op.is_equal, col("MA", q), op.mult) for q in range(4)])
    gap(EARLY[2], True)

    def misses():
        act(A("E", 0, 1024), A("zw0", 4096, 5120), fn.Exp, -1.0, 0.0)
    if r >= 2:
        misses()
    mode["far"] = FAR[0]
    far = [x for x in frm if x < 2]
    for s in far:
        ts(A("xa", 128 * s, 128 * s + 128), A("nxb", 128 * s, 128 * s + 128), -2047.0, op.add)
    for h in range(2):
        tt(A("G", 512 * h, 512 * h + 512), Ind(A("xa"), A("Lp", 32 * h, 32 * h + 32)), A("msk", 512 * h, 512 * h + 512), op.mult)
        for c in range(8 * h, 8 * h + 8):
            for e in range(2):
                mm(A("pC", c, 48, 16, 64 * e, 64 * e + 64), A("G", 64 * c, 64 * c + 64), A("SN", 640 + 3 * e, 643 + 3 * e), True, True,
                   c == 15 and e == 1)
    zhop()
    zs_ = zspread(far[0], ZQ[0] if r >= 2 else "avav")
    ts(A("LA", 16, 64), A("pC", 0, 48), 2047.0, op.add)
    gap(ZG)
    run(zs_)
    if r >= 2:
        run(zspread(far[1], ZQ[1], ("pM", "pF0", "pF1", "pW")))
    mode["far"] = FAR[1]
    mm(T4, A("Hl", 0, 384, 3), A("Pm", 128, 256), True, True)
    keys = row_keys(T4, 0.0)
    if r < 2:
        misses()
    else:
        fixed()
    for h in range(2):
        for c in range(16):
            mm(B("pF%d" % h, (0, 2), 16 * c, 16 * c + 16), A("SN", 512, 640), A("G", 64 * c + 32 * h, 64 * c + 32 * h + 32), c == 0, False)
    ev = []
    gates(0, lambda m: A("LA", 16 * m + 16, 16 * m + 32), A("xo"),
          lambda: (keys(), later(hot(0, 64)), ev.append(track_list(0)), turn(1, [("hi", 0, 2, 0), ("aa", 0, 2, 6)])), lambda: run(ev))
    for t in range(2):
        mm(A("pC", 128 * t, 128 * t + 128), A("Hl", 1 + t, 384, 3), A("Pm", 0, 128), True, True, t == 1)
    ts(A("Ly"), B("pM", 1), 15 * H0, op.add)
    gap(HOT0)
    mode["far"] = FAR[2]
    fields(0)
    act(A("ad0"), A("d"), fn.Abs)
    ts(A("uT"), A("pC", 0, 256), 1.0 / 64, op.mult)
    act(A("msk"), Ind(A("OH"), A("Ly")), fn.Copy)
    if r < 2:
        fixed()
    gap(HOT1)
    held = []

    def after(t):
        def f(k):
            n = ACOL[t][k]
            for c in range(32 * k, 32 * k + n):
                steps("a", c)
                held.append(c)
            if not any(x[0] == "Ab" for e in pool for x in e[2]):
                while held:
                    count(held.pop(0))
            for c in range(32 * k + n, 32 * k + 32):
                later([lambda: (steps("v", c), count(c))], False, c)
        return f

    def drain():
        rest = [e[3] for e in pool if e[3] is not None] + list(range(96, 128))
        pool[:] = [e for e in pool if e[3] is None]
        while held:
            count(held.pop(0))
        return rest
    draws(0, after(0))
    rest = drain()
    n3 = ACOL[0][3]
    count_tail(rest[:len(rest) - n3], rest[len(rest) - n3:], {})
    for k in range(4):
        mm(B("pM", 2, 0, 32), One, A("cb", 128 * k + 3, 128 * k + 128, 4), k == 0, k == 3)
    row_lists(A("Tl"), "aa")
    act(A("pg"), Ind(nxw, A("LA")), fn.Copy)
    mode["far"] = FAR[1]

    def lists0():
        ts(A("Lp"), B("pM", 1), -0.5 - 64 * H0, op.add)
        cp(A("Lx"), B("pM", 0))
        later([lambda e=e: red(col("Hc", e), B("pM", 2, e, 32, 2)) for e in range(2)] +
              [lambda: ts(A("W0b"), A("Hc", 0, 2), -1.0 / 1024, op.mult, 137.0 - 511.5 / 1024, op.add),
               lambda: ts(A("W0c", 0, 2), A("W0b"), -128.0, op.add)])
    marks(0, None, lists0)
    exp_table("ad0", 0, "pF0")
    exp_table("ad0", 1, "pF1")
    base, thr = col("pC", 128), col("pC", 129)
    tt(A("J"), A("nM"), A("J"), op.mult)
    tt(A("nM"), A("S"), A("J"), op.add)
    ts(A("Pq"), A("S"), base, op.add, 1025.0, op.min)
    for m in range(4):
        ts(A("Lsc", 16 * m, 16 * m + 16), A("nM", m, 64, 4), thr, op.add, col("cf", 41), op.mult)
    tt(Ind(A("sw"), A("Lsc")), A("pg"), A("K"), op.max)
    send([((r - 1) % 4, T.W0c[:, 0:2], T.w0l[:, 0:2], "aw0", 0, NE)], whole("W0c", 0, 2))
    for q in range(4):
        mm(B("pH", q >> 1, 64 * (q & 1), 64 * (q & 1) + 64), rep(q), A("Pq"), True, True, q == 3)
    act(A("Qw"), B("pH", (0, 2)), fn.Copy)
    for j in range(2, 6):
        exp_table("ad0", j, ["pW", "pN", "pF0", "pF1"][j - 2])
    for q in range(3):
        terms_gather(q)
    for c in range(16):
        mm(B("pM", 3, c, 96, 16), A("sw", 3072 + c, 5120, 16), A("Sel6", 0, 6), True, True, c == 15)
    tt(A("G"), Ind(A("Qw"), A("Lp")), A("msk"), op.mult)
    cp(A("LN"), B("pM", 3, 0, 96))
    T4 = B("pH", (0, 4), 0, 32)
    for i in range(16):
        mm(B("pH", (0, 4), 2 * i, 2 * i + 2), A("G", i, 2048, 16), A("SelT"), True, True, i == 15)
    zx = A("zw0")
    act(A("xa"), Ind(zx, A("LN", 64, 80)), fn.Copy, None, 0.25)
    ts(A("xb"), Ind(zx, A("LN", 48, 64)), 0.75, op.mult)
    act(A("R"), Ind(nxw, A("LN", 80, 96)), fn.Identity, col("cf", 27), col("cf", 20))
    keys = row_keys(T4, 4.0)
    tt(A("xo1"), A("xa"), A("xb"), op.add)
    tab(lambda q: rep(q, 1), A("R"), False, True)
    terms_gather(3)
    x_table(0, "pY")
    x_table(1, "pC")
    ev = []
    gates(1, lambda m: A("LN", 16 * m, 16 * m + 16), A("xo1"), lambda: (keys(), ev.append(track_list(1)), later(hot(0, 64))))
    act(A("ad0"), A("d"), fn.Abs)
    for e, w in ((0, col("W0c", 1, 0, 64)), (1, col("w0l", 0, 64, 128))):
        ts(col("cf", 26, 64 * e, 64 * e + 64), col("OH", 2, 64 * e, 64 * e + 64), w, op.mult, col("cf", 24, 64 * e, 64 * e + 64), op.add)
    ts(A("prf"), A("hi"), H0 + 63.5, op.is_ge, -2.0, op.mult)
    ts(A("tixf"), B("pM", 2), KT + 1023.5, op.is_ge, 4096.0, op.mult)
    run(ev)
    later([lambda: tt(A("uT", 128, 256), A("uT", 128, 256), A("prf"), op.add), lambda: tt(A("Tx"), A("tixf"), A("Tl"), op.max)], True)
    rot = ["pM", "pC", "pF0", "pF1", "pM", "pC"]
    mode["far"] = FAR[3]
    fields(1, None, lambda: (new_x() if XDMA else x_table(2, "pY"), exp_table("ad0", 0, rot[0])))
    gap(HOT1)
    for j in range(1, 6):
        exp_table("ad0", j, rot[j])
    xs_ = [] if XDMA else [lambda j=j: x_table(j, ["pY", "pF0", "pF1"][j % 3]) for j in range(3, 8)]
    run(xs_[:NX1])
    fresh.update({0: True, 1: True})
    draws(1, after(1))
    rest = drain()

    def terms_add(q):
        v = A("V", 512 * q, 512 * q + 512)
        tt(v, Ind(A("E"), A("Lx", 32 * q, 32 * q + 32)), v, op.add)

    def terms():
        cp(A("Lx"), B("pM", 0))
        terms_add(oth[0])
    count_tail(rest[:NV1], rest[NV1:], {TURN: lambda: row_lists(A("Tx"), "hi"), 2 * NV1: terms})
    act(A("tixf"), B("pM", 0), fn.Copy)
    act(A("prf"), B("pM", 1), fn.Identity, -0.5 - 64 * H0)
    ybank = dict(zip(oth + [r], [A("pY", 0, 128), B("pF0", 0), B("pF1", 0), A("pY", 0, 128)]))

    def ye_sum(q):
        terms_sum(q, True, True, ybank[q])

    def ye_out(q, e):
        o = A("Ye", 128 * q, 128 * q + 128)
        if e == "a":
            act(o, ybank[q], fn.Copy)
        else:
            cp(o, ybank[q])
        if q != r:
            send([(q, T.Ye[:, 128 * q:128 * q + 128], T.yel[:, 128 * r:128 * r + 128], "ae%d" % r, 0, NE)], o[1])
    run(xs_[NX1:])
    ye_sum(oth[0])
    marks(1, lambda: terms_add(oth[1]))
    ye_out(oth[0], "a")
    ts(A("Lv"), A("S"), thr, op.is_lt)
    mm(A("pC", 192, 256), A("OE"), A("Lv"), True, True)
    terms_add(oth[2])
    ye_sum(oth[1])
    ye_sum(oth[2])
    ye_out(oth[1], "a")
    red(col("Hc", 2), A("pC", 192, 256))
    terms_add(r)
    ts(A("f1"), A("prf"), col("Hc", 2), op.is_ge, 4096.0, op.mult)
    tt(A("f1"), A("f1"), A("tixf"), op.max)
    cp(A("Ly"), A("f1"))
    bank = dict(zip(oth + [r], ["pW", "pH", "pN", "pM"]))

    def last_gather(q):
        ts(A("G", 512 * q, 512 * q + 256), Ind(A("XN"), A("Ly", 32 * q, 32 * q + 16)), -4.0, op.add)
        act(A("G", 512 * q + 256, 512 * q + 512), Ind(A("XN"), A("Ly", 32 * q + 16, 32 * q + 32)), fn.Identity, -4.0)
        for u in range(4):
            mm(B(bank[q], 0), A("Yw", 3 - u, 131 - u), A("G", 512 * q + 128 * u, 512 * q + 128 * u + 128), u == 0, u == 3)

    def last_out(q, e):
        o = A("Yx", 128 * q, 128 * q + 128)
        if e == "a":
            act(o, B(bank[q], 0), fn.Identity, 16.0)
        else:
            ts(o, B(bank[q], 0), 16.0, op.add)
    ye_out(oth[2], "a")
    for q in oth + [r]:
        last_gather(q)
    ye_sum(r)
    last_out(oth[0], "v")
    last_out(oth[1], "a")
    send([(oth[j], T.Yx[:, 128 * oth[j]:128 * oth[j] + 128], T.yxl[:, 128 * r:128 * r + 128], "ax%d" % r, j * NE // 2, NE // 2)
          for j in range(2)], whole("Yx", 128 * oth[0], 128 * oth[0] + 128) + whole("Yx", 128 * oth[1], 128 * oth[1] + 128))
    last_out(oth[2], "v")
    send([(oth[2], T.Yx[:, 128 * oth[2]:128 * oth[2] + 128], T.yxl[:, 128 * r:128 * r + 128], "ax%d" % r, 0, NE)],
         whole("Yx", 128 * oth[2], 128 * oth[2] + 128))
    last_out(r, "a")
    ye_out(r, "v")
    for q, out, s in (("s", "ye", frm[0]), ("s", "ye", frm[1]), ("a", "yx", r), ("s", "ye", r), ("s", "ye", frm[2]),
                      ("a", "yx", frm[0]), ("s", "yx", frm[1]), ("a", "yx", frm[2])):
        n = {"ye": ("Ye", "yel"), "yx": ("Yx", "yxl")}[out][s != r]
        dma(q, T[out][32 * s:32 * s + 32, :], T[n][:, 128 * s:128 * s + 128], "sto", 8, [], whole(n, 128 * s, 128 * s + 128))
    for q in cnt:
        total["c" + q] = cnt[q]
    for sem, val in total.items():
        if val:
            wait("g", sem, val)
